import numpy as np, ml_dtypes
CORES = [6,15,38,47]
N = 4
BF = ml_dtypes.bfloat16
D, L, H, S1, S2, VI = 3456, 256, 256, 1, 1, 4
def effects(rng):
    cap = rng.integers(1, 256, (N, 8, 1, D))
    return np.minimum((rng.random((N, 8, 16, D)) * (cap + 1)).astype(np.int64), cap)
def near(rng, n, share, few=64):
    pop = rng.integers(0, D, (N, 8, few)); v = rng.integers(0, D, (N, 8, 16, n))
    c = np.take_along_axis(pop, rng.integers(0, few, (N, 8, 16 * n)), 2).reshape(N, 8, 16, n)
    return np.where(rng.random(v.shape) < share, c, v)
def rows(rng, n):
    return np.argsort(np.argsort(rng.random((N, 8, 16, L)), axis=2), axis=2) < n
def forest(rng, filled, own, deep):
    o = np.argsort(np.where(filled, rng.random(filled.shape), 2.0), axis=2); r = np.arange(16)[:, None]
    u = rng.random(filled.shape); b = np.minimum((rng.random(filled.shape) * (r + 1)).astype(np.int64), r)
    b = np.where(u < own, r, np.where(u > 1 - deep, np.maximum(r - 1, 0), b))
    w = np.zeros(filled.shape, np.int64); np.put_along_axis(w, o, np.take_along_axis(o, b, 2), 2)
    return np.where(filled, w, 0)
def pack(eff, rem, lim, drugs, why, filled):
    return {"eff": np.ascontiguousarray(eff.reshape(N, 128, D)).astype(np.float32).astype(BF), "rem": np.ascontiguousarray(rem.reshape(N, 128, D)).astype(np.int32),
            "lim": np.repeat(lim, 16, axis=1)[:, :, None].astype(np.int32), "drugs": np.ascontiguousarray(np.where(filled, drugs, D).reshape(N, 128, L)).astype(np.int32),
            "why": np.ascontiguousarray(np.where(filled, why, 0).reshape(N, 128, L)).astype(np.int32)}
def setup_inputs(rng):
    n = np.maximum(rng.integers(0, 17, (N, 8, 1, L)), rng.integers(0, 17, (N, 8, 1, L)))
    filled = rows(rng, n); why = forest(rng, filled, 0.3, 0.3)
    return pack(effects(rng), near(rng, D, 0.3), rng.integers(6000, 20000, (N, 8)), near(rng, L, 0.3), why, filled)
def setup_inputs_ties(rng):
    v = rng.integers(0, 256, (N, 8, 16)); v[:, :, 0] = 255
    sh = rng.integers(0, 16, (N, 8, 1, D)); sh[:, ::2, :, 1::2] = sh[:, ::2, :, ::2] + 8
    ix = (np.arange(16)[:, None] + sh) % 16
    eff = np.take_along_axis(v, ix.reshape(N, 8, 16 * D), 2).reshape(N, 8, 16, D)
    lim = np.minimum(rng.integers(3, 12, (N, 8)) * np.add.reduce(v, axis=2), 65280)
    filled = rows(rng, rng.integers(1, 17, (N, 8, 1, L))); drugs = near(rng, L, 0.9, 6)
    pair = rng.random((N, 8, 1, L)) < 0.5; pair[:, 1::2] = False
    twin = np.repeat(drugs[:, :, ::2], 2, axis=2); twin[:, :, 1::2] = twin[:, :, 1::2] ^ 1
    drugs = np.where(pair, twin, drugs); filled = np.where(pair, np.repeat(filled[:, :, ::2], 2, axis=2), filled)
    why = forest(rng, filled, 0.4, 0.2)
    return pack(eff, near(rng, D, 0.7, 6), lim, drugs, why, filled)
def setup_inputs_corners(rng):
    eff = effects(rng); eff[..., 0] = 0; eff[..., D - 1] = 255
    lim = rng.choice(np.array([1, 12000, 65280]), (N, 8)); lim[:, 1] = 1; lim[:, 2] = 65280
    kind = rng.integers(0, 10, (N, 8, 1, L)); m = np.arange(16)[:, None]; hv = rng.random((N, 8, 1, L)) < 0.5
    filled = rows(rng, np.where(kind == 6, 15, rng.integers(0, 17, (N, 8, 1, L))))
    filled = filled | (kind == 1) | (kind == 2) | (kind == 5) | (kind == 8) | (kind == 9)
    filled = np.where(kind == 0, False, np.where(kind == 3, m == 15, np.where(kind == 4, m == 0, filled)))
    why = forest(rng, filled, 0.2, 0.2)
    for k, w in ((1, np.maximum(m - 1, 0)), (2, m), (5, 0 * m), (8, np.minimum(m + 1, 15)), (9, 0 * m + 15)):
        why = np.where(kind == k, w, why)
    drugs = near(rng, L, 0.3)
    low = (kind == 1) | (kind == 5); high = (kind == 8) | (kind == 9)
    top = (low & (m == np.where(hv, 0, 15))) | (high & (m == np.where(hv, 15, 0)))
    drugs = np.where(top | (kind == 3), D - 1, np.where(kind == 4, 0, drugs))
    return pack(eff, near(rng, D, 0.3), lim, drugs, why, filled)
def setup_inputs_great(rng):
    low = np.array([11, 0, 1, 0, 11, 0, 0, 11]).reshape(8, 1, 1); lane = np.arange(L)
    eff = effects(rng); rem = near(rng, D, 0.3); drugs = near(rng, L, 0.3); lim = rng.integers(6000, 20000, (N, 8))
    filled = rows(rng, rng.integers(low, 16, (N, 8, 1, L)))
    for g in (1, 6):
        eff[:, g] = rng.integers(0, 16, (N, 16, D)) < np.array([0, 1, 2, 4, 6, 8, 12, 16])[np.arange(D) % 8]
        lim[:, g] = 1
        h = np.maximum(rng.integers(-4, 8, (N, 1, L)), 0); pure = rng.random((N, 1, L)) < 0.6
        drugs[:, g] = np.where(pure, drugs[:, g] // 8 * 8 + h, drugs[:, g])
        filled[:, g] = filled[:, g] | (pure & (h == 0))
        faint = rng.random((N, 1, D)) < 0.3
        rem[:, g] = np.where(faint, rem[:, g] // 8 * 8 + rng.integers(0, 2, (N, 16, D)), rem[:, g])
    eff[:, 2] = rng.integers(0, 101, (N, 16, D)); lim[:, 2] = 1
    for q in range(N):
        o = rng.permutation(D); i = rng.integers(0, 16, L)
        eff[q, 2][:, o[:L]] = rng.integers(128, 256, (16, L))
        v = rng.choice(o[L:], (16, L)); v[i, lane] = o[:L]; drugs[q, 2] = v
        filled[q, 2][i, lane] = True
    for g in (0, 4, 7):
        eff[:, g] = rng.integers(0, 32, (N, 16, D)) + rng.integers(192, 225, (N, 1, 1))
        if g == 7:
            eff[:, g, :, 7::8] = 255
            drugs[:, g, :, L - 1] = drugs[:, g, :, L - 1] // 8 * 8 + 7
            filled[:, g, :, L - 1] = np.arange(16)[None, :] != rng.integers(0, 16, (N, 1))
        e = np.add.reduce(eff[:, g], axis=1)
        b = np.add.reduce(np.where(filled[:, g], np.take_along_axis(e, drugs[:, g].reshape(N, 16 * L), 1).reshape(N, 16, L), 0), axis=1)
        i = np.argmax(rng.random((N, L)) * (b % 128 > 0), axis=1); v = b[np.arange(N), i]
        lim[:, g] = v + (v % 256 > 128)
    lim[N - 1, 7] = 61200
    filled[0] = True; filled[2] = True
    o = rng.permutation(8 * L)[:int(rng.integers(100, 201))]
    for j in o: filled[2, j // L, :, j % L] = False
    return pack(eff, rem, lim, drugs, forest(rng, filled, 0.3, 0.3), filled)
def setup_inputs_spread(rng):
    cap = np.exp2(8 * rng.random((N, 8, 1, D))).astype(np.int64); cap = np.minimum(cap, 255)
    eff = np.minimum((rng.random((N, 8, 16, D)) * (cap + 1)).astype(np.int64), cap)
    e = rng.choice(np.array([1.0, 3.0, 8.0]), (N, 8, 1, 1))
    rem = np.minimum((D * rng.random((N, 8, 16, D)) ** 3).astype(np.int64), D - 1); drugs = np.minimum((D * rng.random((N, 8, 16, L)) ** e).astype(np.int64), D - 1)
    lim = np.minimum(np.maximum(np.exp2(16 * rng.random((N, 8))).astype(np.int64), 1), 65280); lim[:, 5] = rng.integers(3000, 9000, N)
    filled = rows(rng, rng.integers(0, 17, (N, 8, 1, L))); why = forest(rng, filled, rng.random((N, 8, 1, L)), 0.3)
    return pack(eff, rem, lim, drugs, why, filled)
def setup_inputs_ends(rng):
    eff = 255 * (rng.random((N, 8, 16, D)) < rng.choice(np.array([0.0, 0.5, 1.0]), (N, 8, 1, D))).astype(np.int64)
    case = rng.integers(0, 4, (N, 8)); case[0, 0] = 1; case[N - 1, 7] = 0; case[:, 4] = 2
    a = np.where((case == 0) | (case == 3), 255, np.where(case == 1, 0, -1))[:, :, None]; b = np.where(case == 0, 255, np.where((case == 1) | (case == 3), 0, -1))[:, :, None]
    eff[..., 0] = np.where(a >= 0, a, eff[..., 0]); eff[..., D - 1] = np.where(b >= 0, b, eff[..., D - 1])
    rem = (D - 1) * rng.integers(0, 2, (N, 8, 16, D))
    lim = np.where(rng.random((N, 8)) < 0.5, 1, 65280); lim[:, 0] = 1; lim[:, 7] = 65280
    filled = rng.random((N, 8, 16, L)) < 0.65; filled[:, :, 0] = True; filled[:, :, 15] = True
    none = rng.random((N, 8, 1, L)) < 0.05; full = rng.random((N, 8, 1, L)) < 0.1; full[..., 1] = True; full[..., L - 1] = True
    filled = full | (filled & ~none)
    drugs = np.where(rng.random((N, 8, 16, L)) < 0.7, 0, D - 1); drugs[..., 1] = 0; drugs[..., L - 1] = D - 1
    why = 15 * rng.integers(0, 2, (N, 8, 16, L)); z = rng.integers(0, 2, (N, 8, L))
    why[:, :, 0] = 15 * z; why[:, :, 15] = np.where(z == 1, 15, why[:, :, 15])
    return pack(eff, rem, lim, drugs, why, filled)
def check_inputs(d):
    bad = []
    for k, lo, hi in (("eff", 0, 255), ("rem", 0, D - 1), ("lim", 1, 65280), ("drugs", 0, D), ("why", 0, 15)):
        v = np.asarray(d[k]).astype(np.float64)
        if not (np.min(v) >= lo and np.max(v) <= hi): bad.append("range of " + k)
        elif k == "eff" and np.any(v != np.floor(v)): bad.append("whole numbers in eff")
    v = np.asarray(d["lim"]).reshape(N, 8, 16)
    if np.any(v != v[:, :, :1]): bad.append("lim alike in a group")
    if "range of drugs" in bad or "range of why" in bad: return bad
    filled = np.asarray(d["drugs"]).reshape(N, 8, 16, L) < D; w = np.asarray(d["why"]).astype(np.int64).reshape(N, 8, 16, L)
    if np.any(~filled & (w != 0)): bad.append("why is 0 in empty rows")
    if np.any(filled & ~np.take_along_axis(filled, w, 2)): bad.append("reasons are filled rows")
    c = w
    for _ in range(4): c = np.take_along_axis(c, c, 2)
    if np.any(filled & (np.take_along_axis(w, c, 2) != c)): bad.append("reasons end in a row that is its own reason")
    return bad
def stand(A, a, t):
    return np.concatenate([A[(a - S1 * t) % N][..., :H], A[(a - S2 * t) % N][..., H:]], axis=2)
def reference(eff, rem, lim, drugs, why):
    X = eff.astype(np.float32).astype(np.int32).reshape(N, 8, 16, D)
    X = np.concatenate([X, np.zeros((N, 8, 16, 1), np.int32)], axis=3)
    R = rem.astype(np.int64).reshape(N, 8, 16, D); B = lim.astype(np.int64).reshape(N, 8, 16)[:, :, :1]
    P = drugs.astype(np.int64).reshape(N, 8, 16, L); Q = why.astype(np.int64).reshape(N, 8, 16, L)
    m16 = np.arange(16)[None, :, None]; c = np.zeros(N, np.int64)
    for t in range(VI):
        NP = np.zeros_like(P); NQ = np.zeros_like(Q); stops = np.zeros(N, np.int64)
        for a in range(N):
            p = stand(P, a, t); w = stand(Q, a, t); filled = p < D
            x = np.take_along_axis(X[a], p.reshape(8, 1, 16 * L), 2).reshape(8, 16, 16, L)
            T = np.add.reduce(x, axis=2); burden = np.add.reduce(T, axis=1)
            stop = np.any(filled, axis=1) & ((burden >= B[a] + c[a]) | np.all(filled, axis=1))
            s = np.argmax(np.where(filled, np.add.reduce(x, axis=1), -1), axis=1)[:, None, :]
            cur = np.broadcast_to(m16, p.shape); reach = np.zeros(p.shape, bool)
            for _ in range(16):
                reach = reach | (cur == s); cur = np.take_along_axis(w, cur, 1)
            gone = reach & filled & stop[:, None, :]
            d = np.take_along_axis(p, s, 1)[:, 0]; xs = np.take_along_axis(x, s[:, None], 2)[:, :, 0]; xn = (xs + (T >> 4)) >> 1
            p = np.where(gone, D, p); w = np.where(gone, 0, w); filled = p < D; some = np.any(filled, axis=1)
            U = np.add.reduce(np.where(filled[:, None], x, 0), axis=2)
            f = np.argmax(U, axis=1)
            k = np.argmax(np.where(filled, np.take_along_axis(x, f[:, None, None, :], 1)[:, 0], -1), axis=1)
            dk = np.minimum(np.take_along_axis(p, k[:, None, :], 1), D - 1)
            cand = np.take_along_axis(R[a], dk, 2)
            xc = np.take_along_axis(X[a], cand.reshape(8, 1, 16 * L), 2).reshape(8, 16, 16, L)
            score = np.add.reduce(np.abs(255 - xc - (U >> 4)[:, :, None, :]), axis=1)
            new = np.take_along_axis(cand, np.argmin(score, axis=1)[:, None, :], 1)
            put = (m16 == np.argmin(filled, axis=1)[:, None, :]) & some[:, None, :]
            p = np.where(put, new, p); w = np.where(put, k[:, None, :], w)
            for A, v in ((NP, p), (NQ, w)):
                A[(a - S1 * t) % N, :, :, :H] = v[..., :H]; A[(a - S2 * t) % N, :, :, H:] = v[..., H:]
            for g in range(8):
                lanes = np.flatnonzero(stop[g]); u, i = np.unique(d[g, lanes], return_index=True)
                X[a, g][:, u] = xn[g][:, lanes[i]]
            stops[a] = np.count_nonzero(stop)
        P, Q, c = NP, NQ, stops & 255
    yp = np.stack([stand(P, a, VI - 1) for a in range(N)]); yq = np.stack([stand(Q, a, VI - 1) for a in range(N)])
    return {"yp": yp.reshape(N, 128, L).astype(np.float32), "yq": yq.reshape(N, 128, L).astype(np.float32),
            "yx": np.ascontiguousarray(X[..., :D]).reshape(N, 128, D).astype(np.float32).astype(BF)}

@@ -1,0 +1,647 @@
+import math
+from concourse.mybir import dt, AluOpType, AxisListType, ActivationFunctionType
+
+A = AluOpType
+AF = ActivationFunctionType
+N, D, NV, CH = 4, 3456, 4, 128
+PAD = 4112
+XW = PAD + 256
+MAGIC = 12582912.0
+BIG = 131072.0
+KK = 4194304.0
+NP = 4
+PW = D // NP
+HALF = (("S", 0, 64), ("V", 64, 128))
+SHARE = {"f0": (("S", 0, 32), ("V", 32, 64), ("S", 64, 96), ("V", 96, 128)), "f1": (("S", 0, 32), ("V", 32, 64), ("S", 64, 96), ("V", 96, 128)),
+         "a0": HALF, "a1": HALF, "x2": HALF, "xc": HALF}
+PRI = {}
+BONUS = [-4, -2, -2, 13, 18, 1, 0, 2, 0, 6]
+
+POOLS = {"float32": ("pf", 4), "bfloat16": ("pb", 2), "int32": ("pi", 4), "uint16": ("pu", 2)}
+TILES, SIZE = {}, {"float32": 0, "bfloat16": 0, "int32": 0, "uint16": 0}
+
+
+def tile(name, dtype, cols):
+    per = 32 // POOLS[dtype][1]
+    TILES[name] = (POOLS[dtype][0], SIZE[dtype], cols)
+    SIZE[dtype] += -(-cols // per) * per
+
+
+for _n, _c in (("ONES", 128), ("IDENT", 128), ("BO", 128), ("E16", 8), ("E16N", 8), ("E32N", 8), ("CONSTL", 128), ("KC", 128), ("KS", 128),
+               ("KM", 128), ("K8", 128), ("LT", 128), ("P15", 128), ("P2", 128), ("M64", 128), ("NBO", 128), ("BO4K", 128),
+               ("I8N", 128), ("IBIG", 128), ("NID", 128), ("ONE16", 128), ("K63", 8), ("K155", 128), ("PNUM", 128), ("ZC", 128), ("BO01", 128), ("INEG", 128), ("I8P", 128), ("SELP", 1024),
+               ("SELN", 1024), ("DQ", 128), ("ZA", 128), ("ZB", 128)):
+    tile(_n, "bfloat16", _c)
+for _n, _c in (("BOF", 128), ("MASK", 128), ("IDF", 128), ("DQF", 128), ("SELC", 8), ("DUM", 16), ("MCOL", 1), ("M64C", 1),
+               ("THR", 1), ("THR2", 1), ("B135", 1), ("PC15", 1), ("PC2", 1), ("LIMF", 1), ("THETA", 1), ("CNT", 2), ("RJ", 2048),
+               ("QROW", 128), ("MB1", 1), ("PB1", 1), ("R01", 1), ("WN", 1), ("WP", 1), ("M3", 1), ("M3B", 1), ("JB", 16), ("DC", 16), ("WM", 16), ("LL", 16), ("TT", 16), ("OFF", 16)):
+    tile(_n, "float32", _c)
+for _n, _c in (("MI", 1), ("MI2", 1), ("PCI", 1), ("PCI2", 1), ("LIMI", 1), ("CI", 1), ("CI2", 1), ("DI", 256), ("WI", 256), ("XN", 256)):
+    tile(_n, "int32", _c)
+tile("XS", "bfloat16", 256)
+tile("GL", "uint16", 16)
+tile("SL", "uint16", 16)
+for _h in range(2):
+    for _n in ("F1", "DHI", "DLO", "FULL", "ST", "OHS", "F2", "OHE", "NOE", "OHK", "OHD", "MBH", "MBL", "VMW", "VB", "SG", "TFB", "Z"):
+        tile(_n + str(_h), "bfloat16", CH)
+    for _n in ("SC", "SCA", "D1", "D2", "T32", "U32", "Y", "W2", "MBK", "VM", "MBA", "CF", "MB2", "D3", "VMD", "TM", "AA", "F0",
+               "FN", "VI", "VV", "T1", "T2", "YP", "YQ", "YR"):
+        tile(_n + str(_h), "float32", CH)
+    for _n in ("TI", "GI", "A2"):
+        tile(_n + str(_h), "int32", CH)
+    tile("RED" + str(_h), "float32", 8)
+    for _n in ("L2", "CU"):
+        tile(_n + str(_h), "uint16", CH)
+    tile("LC" + str(_h), "uint16", 16)
+    for _t in range(NV):
+        tile("LU%d%d" % (_h, _t), "uint16", CH)
+        tile("W%d%d" % (_h, _t), "float32", CH)
+    for _t in range(1, NV):
+        tile("SLU%d%d" % (_h, _t), "uint16", CH)
+        tile("SW%d%d" % (_h, _t), "float32", CH)
+
+SCRATCH = {"X": ("sbuf", [128, XW], "bfloat16"), "Y": ("sbuf", [128, XW], "bfloat16"), "R": ("sbuf", [128, D], "int32")}
+for _d in POOLS:
+    SCRATCH[POOLS[_d][0]] = ("sbuf", [128, SIZE[_d]], _d)
+for _h in range(2):
+    for _n in ("x1", "x2", "z", "xc"):
+        SCRATCH[_n + str(_h)] = ("sbuf", [128, 16 * CH], "bfloat16")
+    SCRATCH["ax" + str(_h)] = ("sbuf", [128, 16, CH], "bfloat16")
+    SCRATCH["P0_" + str(_h)] = ("psum", [128, 512], "float32")
+    for _b in (1, 2, 3):
+        SCRATCH["P%d_%d" % (_b, _h)] = ("psum", [128, 4, CH], "float32")
+
+SEMAPHORES = ["cV", "cS", "cT", "cG"] + ["d%d" % k for k in range(40)] + \
+    ["r%d" % k for k in range(12)] + ["l%d" % k for k in range(12)]
+
+
+def rank_program(g, core, T, topo):
+    rank = T.rank_of(core)
+    if rank is None:
+        return
+    nxt, prv = T.cores[(rank + 1) % N], T.cores[(rank - 1) % N]
+    QUEUE = {"V": g.vector, "S": g.scalar, "T": g.tensor, "G": g, "Y": g.sync, "SD": g.scalar}
+
+    def t(name, a=0, b=None, s=None):
+        pool, off, cols = TILES[name]
+        b = cols if b is None else b
+        return T[pool][:, off + a:off + b:s] if s else T[pool][:, off + a:off + b]
+
+    ops = []
+    last_w, readers, banks = {}, {}, {}
+    dcount, now = [0], [0.0]
+
+    def add(eng, fn, rd, wr, cost, sem=None, need=1, extra=(), comp=True, acc=False):
+        k = len(ops)
+        deps = {}
+        phys = {"SD": "S"}.get(eng, eng)
+
+        def dep(o, kind):
+            if o == k:
+                return
+            if (kind == "war" or kind == "waw" and acc) and comp and ops[o]["phys"] == phys and ops[o]["comp"]:
+                deps.setdefault(o, "order")
+            else:
+                deps[o] = "wait"
+        for x in rd:
+            if x in last_w:
+                dep(last_w[x], "raw")
+        for x in wr:
+            if x in last_w:
+                dep(last_w[x], "waw")
+            for o in readers.get(x, ()):
+                dep(o, "war")
+        for x in sorted(set(rd) | set(wr)):
+            if x[0] == "P" and x[2:3] == "_":
+                ep = banks.setdefault(x[:4], [phys, [], []])
+                if ep[0] != phys:
+                    ep[0], ep[1], ep[2] = phys, [], ep[1]
+                for o in ep[2]:
+                    dep(o, "bank")
+                if k not in ep[1]:
+                    ep[1].append(k)
+        for o in extra:
+            deps.setdefault(o, "order")
+        ops.append(dict(eng=eng, phys=phys, comp=comp, fn=fn, deps=deps, cost=cost, sem=sem, need=need, name=(wr or rd)[0], base=now[0], bonus=now[0] + PRI.get((wr or rd)[0], 0)))
+        for x in rd:
+            readers.setdefault(x, []).append(k)
+        for x in wr:
+            last_w[x] = k
+            readers[x] = []
+        return k
+
+    def V(fn, rd, wr, n, c=0.83):
+        return add("V", lambda: fn(g.vector), rd, wr, 0.04 + max(n, 64) * c / 1000)
+
+    def S(fn, rd, wr, n):
+        return add("S", lambda: fn(g.scalar), rd, wr, 0.06 + max(n, 64) * 0.83 / 1000)
+
+    def P(fn, rd, wr, n, acc=False, extra=()):
+        return add("T", lambda: fn(g.tensor), rd, wr, 0.05 + n * 0.45 / 1000, acc=acc, extra=extra)
+
+    def G(fn, rd, wr, n):
+        return add("G", lambda: fn(g), rd, wr, 0.17 + n * 1.66 / 1000)
+
+    def dma(eng, out, in_, rd, wr, lat):
+        s = "d%d" % dcount[0]
+        dcount[0] += 1
+        return add(eng, lambda: QUEUE[eng].dma_start(out, in_), rd, wr, lat, sem=s, need=16, comp=False)
+
+    def ts(out, i0, s1, op0, s2=None, op1=None):
+        if s2 is None:
+            return lambda v: v.tensor_scalar(out, i0, s1, None, op0)
+        return lambda v: v.tensor_scalar(out, i0, s1, s2, op0, op1)
+
+    def tt(out, a, b, op):
+        return lambda v: v.tensor_tensor(out, a, b, op)
+
+    def cp(out, a):
+        return lambda v: v.tensor_copy(out, a)
+
+    def act(out, a, func=AF.Identity, bias=0.0, scale=1.0):
+        return lambda s: s.activation(out, a, func, bias=bias, scale=scale)
+
+    def mms(lst, start=True, stop=True):
+        def f(pe):
+            r = None
+            for k, (o, l, x) in enumerate(lst):
+                r = pe.matmul(o, l, x, start and k == 0, stop and k == len(lst) - 1)
+            return r
+        return f
+
+    dma("Y", t("WI"), T.why[:], [], ["WI"], 2.5)
+    dma("SD", t("DI"), T.drugs[:], [], ["DI"], 2.5)
+    for k in range(NP):
+        dma("Y" if k % 2 == 0 else "SD", T.X[:, k * PW:(k + 1) * PW], T.eff[:, k * PW:(k + 1) * PW], [], ["Xr%d" % k], 4.0 + 1.2 * k)
+    dma("Y", t("LIMI"), T.lim[:], [], ["LIMI"], 3)
+    dma("Y", T.R[:, :D // 2], T.rem[:, :D // 2], [], ["Ra"], 11.0)
+    dma("Y", T.R[:, D // 2:], T.rem[:, D // 2:], [], ["Rb"], 11.0)
+
+    LN2 = math.log(2.0)
+    V(lambda v: v.memset(t("ONES"), 1.0), [], ["ONES"], 64)
+    V(lambda v: v.memset(t("SELP"), 1.0), [], ["SELP"], 512)
+    V(lambda v: v.memset(T.X[:, D:], 0.0), [], ["Xz"], 456)
+    G(lambda q: q.iota(t("MI"), [[0, 1]], 0, 1), [], ["MI"], 1)
+    V(ts(t("MI2"), t("MI"), 15, A.bitwise_and), ["MI"], ["MI2"], 64)
+    V(cp(t("MCOL"), t("MI2")), ["MI2"], ["MCOL"], 64)
+    G(lambda q: q.affine_select(t("IDENT"), t("ONES"), [[-1, 128]], A.is_equal, 0.0, 0, 1), ["ONES"], ["IDENT"], 128)
+    G(lambda q: q.affine_select(t("BO"), t("ONES"), [[-16, 8], [0, 16]], A.is_ge, 0.0, 0, 1), ["ONES"], ["BO"], 128)
+    G(lambda q: q.affine_select(t("BO"), t("BO"), [[16, 8], [0, 16]], A.is_ge, 0.0, 15, -1), ["BO"], ["BO"], 128)
+    G(lambda q: q.iota(t("QROW"), [[0, 8], [1, 16]], 0, 0, allow_small_or_imprecise_dtypes=True), [], ["QROW"], 128)
+    V(ts(t("DQ"), t("QROW"), t("MCOL"), A.is_equal), ["QROW", "MCOL"], ["DQ"], 128)
+    G(lambda q: q.affine_select(t("CONSTL"), t("ONES"), [[0, 128]], A.is_ge, 0.0, 1, -1), ["ONES"], ["CONSTL"], 128)
+    S(act(t("PC2"), t("MCOL"), AF.Exp, 0.0, LN2), ["MCOL"], ["PC2"], 1500)
+    V(cp(t("PCI2"), t("PC2")), ["PC2"], ["PCI2"], 64)
+    V(cp(t("PC2"), t("PCI2")), ["PCI2"], ["PC2"], 64)
+    S(act(t("PC15"), t("MCOL"), AF.Exp, 0.0, -LN2), ["MCOL"], ["PC15"], 64)
+    V(ts(t("PCI"), t("PC15"), 32768.0, A.mult), ["PC15"], ["PCI"], 64)
+    V(cp(t("PC15"), t("PCI")), ["PCI"], ["PC15"], 64)
+    S(act(t("DQF"), t("DQ"), AF.Copy), ["DQ"], ["DQF"], 128)
+    S(act(t("BOF"), t("BO"), AF.Copy), ["BO"], ["BOF"], 128)
+    V(ts(t("MB1"), t("MCOL"), -BIG, A.mult, -BIG, A.add), ["MCOL"], ["MB1"], 64)
+    V(ts(t("PB1"), t("MCOL"), BIG, A.mult, BIG, A.add), ["MCOL"], ["PB1"], 64)
+    G(lambda q: q.iota(t("JB"), [[int(BIG) // 8, 16]], 0, 0, allow_small_or_imprecise_dtypes=True), [], ["JB"], 16)
+    V(ts(t("JB"), t("JB"), 8.0, A.mult, t("PB1"), A.subtract), ["JB", "PB1"], ["JB"], 64)
+    V(ts(t("JB"), t("JB"), BIG - 0.5, A.add, KK, A.mult), ["JB"], ["JB"], 64)
+
+    for h in range(2):
+        H = str(h)
+        now[0] = BONUS[9] * (1 - h)
+        DI = t("DI", h * CH, h * CH + CH)
+        WI = t("WI", h * CH, h * CH + CH)
+        V(ts(t("FN" + H), WI, t("MCOL"), A.not_equal), ["WI", "MCOL"], ["FN" + H], 128)
+        V(ts(t("VI" + H), WI, 1.0, A.add, BIG, A.mult), ["WI"], ["VI" + H], 128)
+        V(tt(t("VI" + H), t("VI" + H), t("FN" + H), A.mult), ["VI" + H, "FN" + H], ["VI" + H], 256)
+        V(ts(t("VV" + H), t("VI" + H), t("MB1"), A.add, t("PC2"), A.add), ["VI" + H, "MB1", "PC2"], ["VV" + H], 128)
+        V(cp(t("LU%d0" % h), DI), ["DI"], ["LU%d0" % h], 128)
+        V(ts(t("T2" + H), WI, 1 / 64, A.mult), ["WI"], ["T2" + H], 128)
+    now[0] = 0.0
+    for j in range(15, -1, -1):
+        RJ = "RJ%d" % j
+        rj = t("RJ", j * 128, j * 128 + 128)
+        S(act(rj, t("BOF"), AF.Copy, 0.0, t("DQF", j, j + 1)), ["BOF", "DQF"], [RJ], 128)
+        G((lambda rj: lambda q: q.affine_select(rj, rj, [[1, 128]], A.not_equal, 1.0, 0, -1))(rj), [RJ], [RJ], 128)
+        for h in range(2):
+            H = str(h)
+            now[0] = BONUS[9] * (1 - h)
+            o, key = T["P1_" + H][:, 0, :], "P1_%s0" % H
+            S(act(t("SG" + H), t("VV" + H), AF.Relu, t("JB", j, j + 1), -KK), ["VV" + H, "JB"], ["SG" + H], 128)
+            P(mms([(o, rj, t("VV" + H))], True, False), [RJ, "VV" + H], [key], 512)
+            P(mms([(o, t("IDENT"), t("SG" + H))], False, True), ["IDENT", "SG" + H], [key], 128, True)
+            V(tt(t("VV" + H), t("VV" + H), o, A.min), ["VV" + H, key], ["VV" + H], 128)
+    for h in range(2):
+        H = str(h)
+        now[0] = BONUS[9] * (1 - h)
+        S(act(t("T1" + H), t("VV" + H), AF.Identity, t("PB1"), 1.0), ["VV" + H, "PB1"], ["T1" + H], 128)
+        V(tt(t("W%d0" % h), t("T1" + H), t("T2" + H), A.add), ["T1" + H, "T2" + H], ["W%d0" % h], 256)
+
+    now[0] = 0.0
+
+    V(ts(t("E16"), t("BO", 0, 128, 16), 16.0, A.mult), ["BO"], ["E16"], 64)
+    V(ts(t("E16N"), t("BO", 0, 128, 16), -16.0, A.mult), ["BO"], ["E16N"], 64)
+    V(ts(t("E32N"), t("BO", 0, 128, 16), -32.0, A.mult), ["BO"], ["E32N"], 64)
+    V(cp(t("SELC"), t("BO", 0, 128, 16)), ["BO"], ["SELC"], 64)
+    G(lambda q: q.iota(t("KC"), [[0, 8], [-1, 16]], 15, 0, allow_small_or_imprecise_dtypes=True), [], ["KC"], 128)
+    G(lambda q: q.affine_select(t("KS"), t("KC"), [[0, 128]], A.is_ge, 131072.0, 0, -1), ["KC"], ["KS"], 128)
+    G(lambda q: q.affine_select(t("KC"), t("KC"), [[0, 128]], A.is_ge, 0.0, 0, -1), ["KC"], ["KC"], 128)
+    EPS = 2.0 ** -8
+    G(lambda q: q.affine_select(t("LT"), t("BO"), [[1, 128]], A.is_gt, EPS, 0, -1), ["BO"], ["LT"], 128)
+    G(lambda q: q.affine_select(t("LT"), t("LT"), [[1, 128]], A.not_equal, -32.0, 0, -1), ["LT"], ["LT"], 128)
+    V(tt(t("LT"), t("LT"), t("BO"), A.mult), ["LT", "BO"], ["LT"], 256)
+    V(ts(t("THR"), t("MCOL"), 0.5, A.subtract, EPS / 2, A.max), ["MCOL"], ["THR"], 64)
+    V(ts(t("THR"), t("THR"), 2.0, A.mult), ["THR"], ["THR"], 64)
+    V(ts(t("THR2"), t("MCOL"), EPS - 1, A.mult, 32 - 15 * EPS, A.add), ["MCOL"], ["THR2"], 64)
+    V(tt(t("THR"), t("THR"), t("THR2"), A.add), ["THR", "THR2"], ["THR"], 64)
+    V(ts(t("M64C"), t("MCOL"), 1 / 64, A.mult), ["MCOL"], ["M64C"], 64)
+    for nm, src, sc in (("P15", "BO", "PC15"), ("P2", "BO", "PC2"), ("M64", "BO", "M64C"), ("NBO", "BO", -0.5), ("BO4K", "BO", 4096.0),
+                        ("I8P", "IDENT", 8192.0), ("INEG", "IDENT", -BIG), ("IBIG", "IDENT", BIG), ("NID", "IDENT", -1.0), ("IDF", "IDENT", 1.0)):
+        S(act(t(nm), t(src), AF.Copy, 0.0, t(sc) if sc in TILES else sc), [src] + ([sc] if sc in TILES else []), [nm], 128)
+    for k, nm in enumerate(("ZA", "ZB")):
+        G((lambda k, nm: lambda q: q.affine_select(t(nm), t("BO"), [[0, 8], [1, 16]], A.is_equal, 0.0, -k, 0))(k, nm), ["BO"], [nm], 128)
+    V(lambda v: v.memset(t("ONE16"), 1 / 16), [], ["ONE16"], 64)
+    V(ts(t("B135"), t("MCOL"), -1.0, A.mult, 135.0, A.add), ["MCOL"], ["B135"], 64)
+    V(lambda v: v.memset(t("MASK"), 1.0), [], ["MASK"], 128)
+    V(lambda v: v.memset(t("MASK", 0, 128, 16), 0.0), [], ["MASK"], 64)
+    V(lambda v: v.memset(t("K63"), -31.5), [], ["K63"], 64)
+    V(lambda v: v.memset(t("K155"), -7.75), [], ["K155"], 64)
+    G(lambda q: q.iota(t("PNUM"), [[1, 128]], 0, 0, allow_small_or_imprecise_dtypes=True), [], ["PNUM"], 128)
+    G(lambda q: q.affine_select(t("PNUM"), t("PNUM"), [[0, 128]], A.is_ge, 1.0, 0, -1), ["PNUM"], ["PNUM"], 128)
+    V(lambda v: v.memset(t("ZC"), 0.0), [], ["ZC"], 64)
+    for r, m in ((0, 2), (1, 3)):
+        G((lambda r, m: lambda q: q.affine_select(t("ZC"), t("ZC"), [[0, 8], [1, 16]], A.not_equal, 1.0, 64 * r - m, -64))(r, m), ["ZC"], ["ZC"], 128)
+    V(ts(t("R01"), t("MCOL"), 1.5, A.is_lt), ["MCOL"], ["R01"], 64)
+    V(ts(t("BO01"), t("BO"), t("R01"), A.mult), ["BO", "R01"], ["BO01"], 64)
+    V(ts(t("WN"), t("R01"), -255.0, A.mult, -1.0, A.add), ["R01"], ["WN"], 64)
+    V(ts(t("M3"), t("MCOL"), 2.5, A.is_lt), ["MCOL"], ["M3"], 64)
+    V(tt(t("WN"), t("WN"), t("M3"), A.mult), ["WN", "M3"], ["WN"], 64)
+    V(ts(t("M3B"), t("MCOL"), 3.0, A.is_equal, 64.0, A.mult), ["MCOL"], ["M3B"], 64)
+    V(tt(t("WP"), t("M3B"), t("WN"), A.subtract), ["M3B", "WN"], ["WP"], 64)
+    G(lambda q: q.affine_select(t("SELP"), t("SELP"), [[-16, 8], [0, 128]], A.is_ge, 0.0, 0, 1), ["SELP"], ["SELP"], 1024)
+    G(lambda q: q.affine_select(t("SELP"), t("SELP"), [[16, 8], [0, 128]], A.is_ge, 0.0, 15, -1), ["SELP"], ["SELP"], 1024)
+    S(act(t("SELN"), t("SELP"), AF.Copy, 0.0, t("WN")), ["SELP", "WN"], ["SELN"], 1024)
+    S(act(t("SELP"), t("SELP"), AF.Copy, 0.0, t("WP")), ["SELP", "WP"], ["SELP"], 1024)
+    G(lambda q: q.iota(t("DUM"), [[16, 16]], PAD + 1, 0, allow_small_or_imprecise_dtypes=True), [], ["DUM"], 16)
+    V(ts(t("DUM"), t("DUM"), t("MCOL"), A.add), ["DUM", "MCOL"], ["DUM"], 64)
+    for k in range(NP):
+        sl = T.X[:, k * PW:(k + 1) * PW]
+        V(ts(sl, sl, 1.0, A.add), ["Xr%d" % k], ["Xr%d" % k], PW / 2)
+    V(cp(t("LIMF"), t("LIMI")), ["LIMI"], ["LIMF"], 64)
+    V(ts(t("THETA"), t("LIMF"), 120.0, A.subtract), ["LIMF"], ["THETA"], 64)
+    XK = ["Xr%d" % k for k in range(NP)] + ["Xz"]
+    XALL = T.X[:]
+
+    def gather(dst, lst, h, plan):
+        w = []
+        for (e, a, b) in plan:
+            if a < b:
+                key = "%s%d:%d" % (dst, h, a)
+                o, s = T[dst + str(h)][:, 16 * a:16 * b], XALL.indirect(t(lst, a, b))
+                if e == "S":
+                    S(act(o, s, AF.Copy), XK + [lst], [key], 16 * (b - a) * 1.5)
+                else:
+                    V(cp(o, s), XK + [lst], [key], 16 * (b - a) * 1.5)
+                w.append(key)
+        return w
+
+    def sums(h, slot, x, f, plan, kx):
+        H = str(h)
+        for (e, a, b), key in zip(plan, kx):
+            o = T["P3_" + H][:, slot, a:b]
+            P(mms([(o, t("IDENT"), x[:, 16 * a + m:16 * b:16]) for m in range(16)] + [(o, t("NBO"), t(f, a, b)), (o, t("CONSTL"), t("K155", a, b))]),
+              ["IDENT", "NBO", "CONSTL", "K155", f, key], ["P3_%s%d" % (H, slot)] if a == 0 else ["P3_%s%d+%d" % (H, slot, a)], 18 * max(64, b - a))
+        return ["P3_%s%d" % (H, slot)] + ["P3_%s%d+%d" % (H, slot, a) for e, a, b in plan if a]
+
+    def argmax(h):
+        H = str(h)
+        src, p0 = "P0_" + H, T["P0_" + H]
+        V(lambda v: v.tensor_tensor_scan(t("SCA" + H), t("MASK"), p0[:, 0:128], 0.0, A.mult, A.max), [src, "MASK"], ["SCA" + H], 128)
+        V(lambda v: v.tensor_tensor_scan(t("SC" + H)[:, ::-1], t("MASK"), t("SCA" + H)[:, ::-1], 0.0, A.mult, A.max), ["SCA" + H, "MASK"], ["SC" + H], 128)
+        V(tt(t("OHD" + H), p0[:, 0:128], t("SC" + H), A.is_equal), [src, "SC" + H], ["OHD" + H], 128)
+
+    def phase1(vt, h):
+        H = str(h)
+        LU, W = "LU%d%d" % (h, vt), "W%d%d" % (h, vt)
+        p0, p1, p3 = T["P0_" + H], T["P1_" + H], T["P3_" + H]
+        x = T["x1" + H]
+        kx = gather("x1", LU, h, SHARE[("a" if vt else "f") + H])
+        V(ts(t("D1" + H), t(LU), 1.0, A.add), [LU], ["D1" + H], 128)
+        S(act(t("F1" + H), t("D1" + H), AF.Sign, 3456.5, -1.0), ["D1" + H], ["F1" + H], 128)
+        S(act(t("DHI" + H), t("D1" + H), AF.Copy), ["D1" + H], ["DHI" + H], 128)
+        V(tt(t("DLO" + H), t("D1" + H), t("DHI" + H), A.subtract), ["D1" + H, "DHI" + H], ["DLO" + H], 256)
+        P(mms([(p1[:, 3, :], t("BO"), t("F1" + H))]), ["BO", "F1" + H], ["P1_%s3" % H], 128)
+        S(act(t("FULL" + H), p1[:, 3, :], AF.Relu, -15.0), ["P1_%s3" % H], ["FULL" + H], 128)
+        P(mms([(p0[:, 0:128], t("CONSTL"), t("KC"))] + [(p0[:, m:128:16], x[:, m::16], t("E16")) for m in range(16)]),
+          ["CONSTL", "KC", "E16"] + kx, ["P0_" + H], 128 + 16 * 64)
+        argmax(h)
+        kt = sums(h, 0, x, "F1" + H, SHARE[("a" if vt else "f") + H], kx)
+        S(act(t("T32" + H), p3[:, 0, :], AF.Copy), kt, ["T32" + H], 128)
+        P(mms([(p3[:, 1, :], t("BOF"), t("T32" + H)), (p3[:, 1, :], t("BO4K"), t("FULL" + H))]),
+          ["BOF", "T32" + H, "BO4K", "FULL" + H], ["P3_%s1" % H], 640)
+        V(ts(t("ST" + H), p3[:, 1, :], t("THETA"), A.is_ge), ["P3_%s1" % H, "THETA"], ["ST" + H], 128)
+        P(mms([(p1[:, 0, :], t("OHD" + H), t("IDENT"))]), ["OHD" + H, "IDENT"], ["P1_%s0" % H], 128)
+        V(tt(t("OHS" + H), p1[:, 0, :], t("ST" + H), A.mult), ["P1_%s0" % H, "ST" + H], ["OHS" + H], 128)
+        P(mms([(p1[:, 1, :], t("P15"), t("OHS" + H))]), ["P15", "OHS" + H], ["P1_%s1" % H], 128)
+        V(tt(t("TI" + H), t(W), p1[:, 1, :], A.mult), [W, "P1_%s1" % H], ["TI" + H], 128)
+        V(ts(t("GI" + H), t("TI" + H), 3, A.logical_shift_right, 4096, A.bitwise_and), ["TI" + H], ["GI" + H], 128)
+        V(tt(t("D2" + H), t("D1" + H), t("GI" + H), A.max), ["D1" + H, "GI" + H], ["D2" + H], 256)
+        V(ts(t("L2" + H), t("D2" + H), 1.0, A.subtract), ["D2" + H], ["L2" + H], 128)
+
+    def phase2(vt, h):
+        H = str(h)
+        W = "W%d%d" % (h, vt)
+        p0, p1, p3 = T["P0_" + H], T["P1_" + H], T["P3_" + H]
+        x = T["x2" + H]
+        kx = gather("x2", "L2" + H, h, SHARE["x2"])
+        S(act(t("F2" + H), t("D2" + H), AF.Sign, 3456.5, -1.0), ["D2" + H], ["F2" + H], 128)
+        P(mms([(p1[:, 2, :], t("LT"), t("F2" + H))]), ["LT", "F2" + H], ["P1_%s2" % H], 128)
+        P(mms([(p1[:, 3, :], t("IDF"), t(W)), (p1[:, 3, :], t("IBIG"), t("F2" + H))]), ["IDF", W, "IBIG", "F2" + H], ["P1_%s3" % H], 640)
+        V(ts(t("OHE" + H), p1[:, 2, :], t("THR"), A.is_ge), ["P1_%s2" % H, "THR"], ["OHE" + H], 128)
+        S(act(t("NOE" + H), t("OHE" + H), AF.Identity, 1.0, -1.0), ["OHE" + H], ["NOE" + H], 128)
+        S(act(t("W2" + H), p1[:, 3, :], AF.Relu, -BIG), ["P1_%s3" % H], ["W2" + H], 128)
+        V(cp(t("A2" + H), t("W2" + H)), ["W2" + H], ["A2" + H], 128)
+        ku = sums(h, 2, x, "F2" + H, SHARE["x2"], kx)
+        S(act(t("U32" + H), p3[:, 2, :], AF.Identity, t("B135"), 16.0), ku + ["B135"], ["U32" + H], 128)
+        S(act(t("Y" + H), p3[:, 2, :], AF.Identity, MAGIC, 1 / 16), ku, ["Y" + H], 128)
+        P(mms([(p0[:, 0:128], t("U32" + H), t("IDF"))]), ["U32" + H, "IDF"], ["P0_" + H], 512)
+        S(act(t("VB" + H), t("Y" + H), AF.Identity, MAGIC + 256, -1.0), ["Y" + H], ["VB" + H], 128)
+        argmax(h)
+        P(mms([(p3[:, 3, :], t("OHD" + H), t("IDENT"))]), ["OHD" + H, "IDENT"], ["P3_%s3" % H], 128)
+
+    def phase3(vt, h):
+        H = str(h)
+        p0, p1, p3 = T["P0_" + H], T["P1_" + H], T["P3_" + H]
+        x, z = T["x2" + H], T["z" + H]
+        kx = ["x2%d:%d" % (h, a) for e, a, b in SHARE["x2"]]
+        for q in range(2):
+            ms = range(8 * q, 8 * q + 8)
+
+            def kf(v, ms=ms):
+                for m in ms:
+                    r = v.tensor_tensor(z[:, m::16], x[:, m::16], p3[:, 3, :], A.mult)
+                return r
+            V(kf, kx + ["P3_%s3" % H], ["z%s:%d" % (H, q)], 8 * 128)
+
+            def yf(pe, q=q, ms=ms):
+                if q == 0:
+                    pe.matmul(p0[:, 0:128], t("CONSTL"), t("KC"), True, False)
+                for m in ms:
+                    r = pe.matmul(p0[:, m:128:16], z[:, m::16], t("E16"), False, m == 15)
+                return r
+            P(yf, ["CONSTL", "KC", "E16", "z%s:%d" % (H, q)], ["P0_" + H], 128 * (1 - q) + 8 * 64, q == 1)
+        argmax(h)
+        P(mms([(p1[:, 0, :], t("OHD" + H), t("IDENT"))]), ["OHD" + H, "IDENT"], ["P1_%s0" % H], 128)
+        V(tt(t("MBK" + H), p1[:, 0, :], t("D2" + H), A.mult), ["P1_%s0" % H, "D2" + H], ["MBK" + H], 128)
+        V(tt(t("MBA" + H), p1[:, 0, :], t("A2" + H), A.mult), ["P1_%s0" % H, "A2" + H], ["MBA" + H], 128)
+        S(act(t("OHK" + H), p1[:, 0, :], AF.Copy), ["P1_%s0" % H], ["OHK" + H], 128)
+        P(mms([(p1[:, 1, :], t("MBK" + H), t("BOF"))]), ["MBK" + H, "BOF"], ["P1_%s1" % H], 512)
+        V(tt(t("VM" + H), p1[:, 1, :], t("DQF"), A.mult), ["P1_%s1" % H, "DQF"], ["VM" + H], 128)
+        P(mms([(p1[:, 3, 0:8], t("VM" + H), t("SELC"))]), ["VM" + H, "SELC"], ["P1_%s3" % H], 256)
+        V(ts(t("LC" + H, 0, 8), p1[:, 3, 0:8], 1.0, A.subtract, 3455.0, A.min), ["P1_%s3" % H], ["LC" + H], 64)
+        V(cp(t("CU" + H), T.R[:].indirect(t("LC" + H, 0, 8))), ["Ra", "Rb", "LC" + H], ["CU" + H], 200)
+
+    def phase4(vt, h):
+        H = str(h)
+        p0, p1, p3 = T["P0_" + H], T["P1_" + H], T["P3_" + H]
+        xc, ax = T["xc" + H], T["ax" + H]
+        kx = gather("xc", "CU" + H, h, SHARE["xc"])
+        V(ts(t("CF" + H), t("CU" + H), 1.0, A.add), ["CU" + H], ["CF" + H], 128)
+        P(mms([(p1[:, 2, :], t("BOF"), t("MBA" + H)), (p1[:, 2, :], t("M64"), t("OHK" + H)), (p1[:, 2, :], t("P2"), t("OHE" + H)),
+               (p1[:, 2, :], t("INEG"), t("NOE" + H))]),
+          ["BOF", "MBA" + H, "M64", "OHK" + H, "P2", "OHE" + H, "INEG", "NOE" + H], ["P1_%s2" % H], 896)
+        last = vt == NV - 1
+        WN = ("SW%d%d" % (h, vt + 1)) if not last else "W2" + H
+        V(tt(t(WN), t("W2" + H), p1[:, 2, :], A.max), ["W2" + H, "P1_%s2" % H], [WN], 128)
+        if not last:
+            send(WN, "W%d%d" % (h, vt + 1), 6 * h + 2 * vt)
+        ks = P(mms([(p0[:, 0:128], t("CONSTL"), t("KS"))], True, False), ["CONSTL", "KS"], ["P0_" + H], 128)
+        def mf(v):
+            for j in range(12, 16):
+                r = v.tensor_tensor(ax[:, j, :], xc[:, j::16], t("VB" + H), A.max)
+            return r
+        V(mf, kx + ["VB" + H], ["ax%s:3" % H], 1024)
+
+        def lf(pe):
+            for j in range(12, 16):
+                pe.matmul(p0[:, j:128:16], xc[:, j::16], t("E16"), False, False)
+                r = pe.matmul(p0[:, j:128:16], t("VB" + H), t("E16"), False, False)
+            return r
+        parts = [P(lf, ["E16", "VB" + H] + kx, ["P0_%s#l" % H], 512, True, [ks])]
+
+        def gf(pe):
+            for j in range(12, 16):
+                r = pe.matmul(p0[:, j:128:16], ax[:, j, :], t("E32N"), False, False)
+            return r
+        parts.append(P(gf, ["E32N", "ax%s:3" % H], ["P0_%s#g" % H], 256, True, [ks]))
+        for b in range(3):
+            pb, kb = (p3, "P3_%s" % H) if b % 2 == 0 else (p1, "P1_%s" % H)
+
+            def df(pe, b=b, pb=pb):
+                for u in range(4):
+                    pe.matmul(pb[:, u, :], t("IDENT"), xc[:, 4 * b + u::16], True, False)
+                    r = pe.matmul(pb[:, u, :], t("NID"), t("VB" + H), False, True)
+                return r
+            P(df, ["IDENT", "NID", "VB" + H] + kx, [kb + str(u) for u in range(4)], 1024)
+            S(act(ax[:, 4 * b:4 * b + 4, :], pb[:, :, :], AF.Abs), [kb + str(u) for u in range(4)], ["ax%s:%d" % (H, b)], 512)
+
+            def sf(pe, b=b):
+                for j in range(4 * b, 4 * b + 4):
+                    r = pe.matmul(p0[:, j:128:16], ax[:, j, :], t("E16N"), False, j == 11)
+                return r
+            parts.append(P(sf, ["E16N", "ax%s:%d" % (H, b)], ["P0_%s#%d" % (H, b) if b < 2 else "P0_" + H], 256, True, [ks] if b < 2 else parts))
+        argmax(h)
+        P(mms([(p1[:, 0, :], t("OHD" + H), t("IDENT"))]), ["OHD" + H, "IDENT"], ["P1_%s0" % H], 128)
+        V(tt(t("MB2" + H), p1[:, 0, :], t("CF" + H), A.mult), ["P1_%s0" % H, "CF" + H], ["MB2" + H], 128)
+        P(mms([(p1[:, 1, :], t("I8P"), t("NOE" + H))], True, False), ["I8P", "NOE" + H], ["P1_%s1" % H], 128)
+        P(mms([(p1[:, 1, :], t("BOF"), t("MB2" + H))], False, True), ["BOF", "MB2" + H], ["P1_%s1" % H], 512, True)
+        V(tt(t("D3" + H), t("D2" + H), p1[:, 1, :], A.min), ["D2" + H, "P1_%s1" % H], ["D3" + H], 128)
+        if not last:
+            LN = "SLU%d%d" % (h, vt + 1)
+            V(ts(t(LN), t("D3" + H), 1.0, A.subtract), ["D3" + H], [LN], 128)
+            send(LN, "LU%d%d" % (h, vt + 1), 6 * h + 2 * vt + 1)
+        else:
+            V(ts(t("YP" + H), t("D3" + H), 1.0, A.subtract, 3456.0, A.min), ["D3" + H], ["YP" + H], 128)
+            dma("Y", T.yp[:, h * CH:h * CH + CH], t("YP" + H), ["YP" + H], [], 2.5)
+            V(cp(t("A2" + H), t("W2" + H)), ["W2" + H], ["A2" + H], 128)
+            V(tt(t("YQ" + H), t("W2" + H), t("A2" + H), A.subtract), ["W2" + H, "A2" + H], ["YQ" + H], 256)
+            V(ts(t("YR" + H), t("YQ" + H), 64.0, A.mult), ["YQ" + H], ["YR" + H], 128)
+            dma("Y", T.yq[:, h * CH:h * CH + CH], t("YR" + H), ["YR" + H], [], 2.5)
+
+    def send(src, dst, k):
+        mask, n = topo.mask(core, nxt), len(topo.engines(core, nxt))
+        rid, pid = topo.addr(nxt)[:2]
+        o = add("G", lambda: g.remote_dma(t(dst), t(src), T.sem["r%d" % k], T.sem["l%d" % k], pid, rid, mask), [src], [], 1.0,
+                sem="l%d" % k, need=n, comp=False)
+        add("N", None, [], [dst], 2.5, sem="r%d" % k, need=len(topo.engines(prv, core)), extra=[o], comp=False)
+
+    def dedup(vt, h):
+        H = str(h)
+        q2 = "P2_" + H
+        p2 = T[q2]
+        P(mms([(p2[:, 3, :], t("IDENT"), t("OHS" + H))]), ["IDENT", "OHS" + H], [q2 + "3"], 128)
+        V(tt(t("MBH" + H), p2[:, 3, :], t("DHI" + H), A.mult), [q2 + "3", "DHI" + H], ["MBH" + H], 128)
+        V(tt(t("MBL" + H), p2[:, 3, :], t("DLO" + H), A.mult), [q2 + "3", "DLO" + H], ["MBL" + H], 128)
+        P(mms([(p2[:, 1, :], t("ZA"), t("MBH" + H)), (p2[:, 1, :], t("ZB"), t("MBL" + H)), (p2[:, 1, :], t("ZC"), t("PNUM"))]),
+          ["MBH" + H, "MBL" + H, "ZA", "ZB", "ZC", "PNUM"], [q2 + "1"], 384)
+        S(act(t("Z" + H), p2[:, 1, :], AF.Copy), [q2 + "1"], ["Z" + H], 128)
+        P(mms([(p2[:, 0, :], t("Z" + H), t("BO01"))]), ["Z" + H, "BO01"], [q2 + "0"], 128)
+        P(mms([(p2[:, 2, :], t("ONE16"), t("ST" + H))]), ["ONE16", "ST" + H], [q2 + "2"], 128)
+        V(tt(t("VMD" + H), p2[:, 0, :], t("DQF"), A.mult), [q2 + "0", "DQF"], ["VMD" + H], 128)
+        if vt < NV - 1:
+            S(lambda s: s.activation(t("AA" + H), p2[:, 2, :], AF.Copy, accum_out=t("CNT", h, h + 1)), [q2 + "2"], ["AA" + H, "CNT" + H], 160)
+        P(mms([(p2[:, 1, 0:8], t("VMD" + H), t("SELC"))]), ["VMD" + H, "SELC"], [q2 + "1"], 256)
+        V(cp(t("DC", 8 * h, 8 * h + 8), p2[:, 1, 0:8]), [q2 + "1"], ["DC" + H], 64)
+        for w in range(8):
+            b = q2
+            o = T[b][:, w % 4, :]
+            sp, sn = t("SELP", w * 128, w * 128 + 128), t("SELN", w * 128, w * 128 + 128)
+            P(mms([(o, sp, t("Z" + H)), (o, t("Z" + H), sn)]), ["SELP", "SELN", "Z" + H], [b + str(w % 4)], 256)
+            if w % 4 == 3:
+                for u in range(w - 3, w + 1):
+                    V((lambda u, b: lambda v: v.tensor_reduce(t("RED" + H, u, u + 1), T[b][:, u % 4, :], AxisListType.X, A.min,
+                                                              apply_absolute_value=True))(u, b), [b + str(u % 4)], ["RED%s%d" % (H, u)], 128)
+        for w in range(8):
+            S(act(t("VMW" + H, 16 * w, 16 * w + 16), t("DQ", 0, 16), AF.Copy, 0.0, t("RED" + H, w, w + 1)), ["DQ", "RED%s%d" % (H, w)], ["VMW%s%d" % (H, w)], 16)
+        S(act(t("TM" + H), t("T32" + H), AF.Identity, MAGIC, 1 / 16), ["T32" + H], ["TM" + H], 128)
+        S(act(t("TFB" + H), t("TM" + H), AF.Identity, -MAGIC, 1.0), ["TM" + H], ["TFB" + H], 128)
+
+    def update(vt):
+        pa, pb = T.P2_0, T.P2_1
+        for h in range(2):
+            H = str(h)
+            P(mms([(pa[:, 3, 8 * h:8 * h + 8], t("VMW" + H), t("BO", 0, 128, 16)), (pa[:, 3, 8 * h:8 * h + 8], t("CONSTL"), t("K63"))]),
+              ["VMW%s%d" % (H, w) for w in range(8)] + ["BO", "CONSTL", "K63"], ["P2_03%d" % h], 128)
+        V(ts(t("GL"), t("DC"), 1.0, A.subtract), ["DC0", "DC1"], ["GL"], 64)
+        S(act(t("XS"), XALL.indirect(t("GL")), AF.Copy), XK + ["GL"], ["XS"], 400)
+        for h in range(2):
+            H = str(h)
+            P(mms([(pb[:, h, :], t("IDENT"), t("XS", 128 * h, 128 * h + 128)), (pb[:, h, :], t("IDENT"), t("TFB" + H))]),
+              ["IDENT", "XS", "TFB" + H], ["P2_1%d" % h], 256)
+        V(ts(t("XN"), pb[:, 0:2, :], 0.5, A.mult, 0.25 if vt < NV - 1 else -0.75, A.add), ["P2_10", "P2_11"], ["XN"], 256)
+        V(tt(t("WM"), pa[:, 3, 0:16], t("DC"), A.min), ["P2_030", "P2_031", "DC0", "DC1"], ["WM"], 64)
+        V(ts(t("LL"), t("WM"), 0.5, A.is_lt), ["WM"], ["LL"], 64)
+        V(tt(t("TT"), t("LL"), t("DUM"), A.mult), ["LL", "DUM"], ["TT"], 64)
+        V(tt(t("OFF"), t("TT"), t("DC"), A.max), ["TT", "DC0", "DC1"], ["OFF"], 64)
+        V(ts(t("SL"), t("OFF"), 1.0, A.subtract), ["OFF"], ["SL"], 64)
+        if vt < NV - 1:
+            V(tt(t("CI"), t("CNT", 0, 1), t("CNT", 1, 2), A.add), ["CNT0", "CNT1"], ["CI"], 64)
+            V(ts(t("CI2"), t("CI"), 255, A.bitwise_and), ["CI"], ["CI2"], 64)
+            V(ts(t("THETA"), t("CI2"), t("LIMF"), A.add, 120.0, A.subtract), ["CI2", "LIMF"], ["THETA"], 64)
+        dst, keys = (T.X[:], XK) if vt < NV - 1 else (T.Y[:], ["Y%d" % k for k in range(NP)] + ["Yz"])
+        for h in (1, 0):
+            V(cp(dst.indirect(t("SL", 8 * h, 8 * h + 8)), t("XN", 128 * h, 128 * h + 128)), ["SL", "XN"], keys, 128 * 3)
+
+    for vt in range(NV):
+        if vt == NV - 1:
+            V(lambda v: v.memset(T.Y[:, D:], 0.0), [], ["Yz"], 456)
+            for k in range(NP):
+                S(act(T.Y[:, k * PW:(k + 1) * PW], T.X[:, k * PW:(k + 1) * PW], AF.Identity, -1.0, 1.0), XK, ["Y%d" % k], PW)
+        for ph in (phase1, phase2, phase3):
+            for h in range(2):
+                now[0] = BONUS[2 * (phase1, phase2, phase3).index(ph) + h]
+                ph(vt, h)
+        now[0] = BONUS[8]
+        if vt == NV - 1:
+            for h in range(2):
+                dedup(vt, h)
+            update(vt)
+            for k in range(NP):
+                dma("Y", T.yx[:, k * PW:(k + 1) * PW], T.Y[:, k * PW:(k + 1) * PW], ["Y%d" % k], [], 4.0)
+        for h in range(2):
+            now[0] = BONUS[6 + h]
+            phase4(vt, h)
+        now[0] = BONUS[8]
+        if vt < NV - 1:
+            for h in range(2):
+                dedup(vt, h)
+            update(vt)
+
+    emit(g, T, ops, schedule(ops), QUEUE)
+
+
+WAKE, LOOK, IDLE = 0.12, 0.06, 0.0
+
+
+def schedule(ops):
+    n = len(ops)
+    succ = [[] for _ in range(n)]
+    for k, o in enumerate(ops):
+        for d in o["deps"]:
+            succ[d].append(k)
+    tail = [0.0] * n
+    for k in range(n - 1, -1, -1):
+        tail[k] = ops[k]["cost"] + max([tail[s] + WAKE for s in succ[k]] + [0.0])
+    for k in range(n):
+        tail[k] += ops[k]["bonus"]
+    left = [len(o["deps"]) for o in ops]
+    fin, free, order = [0.0] * n, {}, []
+    ready = {}
+    for k in range(n):
+        if left[k] == 0:
+            ready.setdefault(ops[k]["phys"], {})[k] = 0.0
+    while ready:
+        best = None
+        for e, lst in ready.items():
+            f = free.get(e, 0.0)
+            t0 = max(f, min(lst.values()))
+            if best is None or t0 < best[0]:
+                best = (t0, e)
+        t0, e = best
+        lst = ready[e]
+        k = max((tail[k] - IDLE * max(0.0, r - t0), -k) for k, r in lst.items() if r <= t0 + LOOK)[1] * -1
+        st = max(free.get(e, 0.0), lst.pop(k))
+        if not lst:
+            del ready[e]
+        o = ops[k]
+        fin[k] = st + o["cost"]
+        if e != "N":
+            free[e] = st + (o["cost"] if o["comp"] else (0.1 if o["eng"] != "G" else 1.0))
+        order.append(k)
+        for s in succ[k]:
+            left[s] -= 1
+            if left[s] == 0:
+                ready.setdefault(ops[s]["phys"], {})[s] = max([fin[d] + (WAKE if ops[s]["deps"][d] == "wait" else 0.0) for d in ops[s]["deps"]])
+    ops[0]["makespan"] = max(fin)
+    ops[0]["fin"] = dict(enumerate(fin))
+    return order
+
+
+def emit(g, T, ops, order, QUEUE):
+    know = {e: {} for e in ("V", "S", "T", "G", "Y")}
+    cnt = {}
+    for k in order:
+        o = ops[k]
+        e = o["phys"]
+        if e == "N":
+            o["sig"], o["kn"] = (o["sem"], o["need"]), {}
+            continue
+        q, kn = QUEUE[o["eng"]], know[e]
+        waits, src = {}, {}
+        for d in o["deps"]:
+            if o["deps"][d] == "wait":
+                s, v = ops[d]["sig"]
+                if kn.get(s, 0) < v and waits.get(s, 0) < v:
+                    waits[s], src[s] = v, d
+        for s in list(waits):
+            if any(s2 != s and ops[src[s2]]["kn"].get(s, 0) >= waits[s] for s2 in waits):
+                del waits[s]
+        for s in sorted(waits):
+            q.wait_ge(T.sem[s], waits[s])
+            for a, b in ops[src[s]]["kn"].items():
+                kn[a] = max(kn.get(a, 0), b)
+            kn[s] = max(kn.get(s, 0), waits[s])
+        ins = o["fn"]()
+        if o["comp"]:
+            s = "c" + e
+            cnt[s] = cnt.get(s, 0) + 1
+            ins.then_inc(T.sem[s], 1)
+            o["sig"] = (s, cnt[s])
+        else:
+            o["sig"] = (o["sem"], o["need"])
+            if o["eng"] != "G":
+                ins.then_inc(T.sem[o["sem"]], 16)
+        o["kn"] = dict(kn)
+    for s in sorted(cnt):
+        g.wait_ge(T.sem[s], cnt[s])
+    for o in ops:
+        if not o["comp"] and o["phys"] != "N":
+            g.wait_ge(T.sem[o["sig"][0]], o["sig"][1])

@@ -1,21 +1,24 @@
-import math
 from concourse.mybir import dt, AluOpType, AxisListType, ActivationFunctionType
 
 A = AluOpType
 AF = ActivationFunctionType
 N, D, NV, CH = 4, 3456, 4, 128
-PAD = 4112
-XW = PAD + 256
+PAD = 3472
+XW = PAD + 32
 MAGIC = 12582912.0
 BIG = 131072.0
 KK = 4194304.0
 NP = 4
 PW = D // NP
-HALF = (("S", 0, 64), ("V", 64, 128))
-SHARE = {"f0": (("S", 0, 32), ("V", 32, 64), ("S", 64, 96), ("V", 96, 128)), "f1": (("S", 0, 32), ("V", 32, 64), ("S", 64, 96), ("V", 96, 128)),
-         "a0": HALF, "a1": HALF, "x2": HALF, "xc": HALF}
-PRI = {}
-BONUS = [-4, -2, -2, 13, 18, 1, 0, 2, 0, 6]
+X1 = (("S", 0, 76), ("V", 76, 128))
+X1F = (("S", 0, 64), ("V", 64, 128))
+XC = (("S", 0, 76), ("V", 76, 128))
+X2 = (("S", 0, 64), ("V", 64, 128))
+ONS = "CX5"
+UR = "G"
+ZR = "SVVV"
+AR = "SVSV"
+BONUS = [0] * 10
 
 POOLS = {"float32": ("pf", 4), "bfloat16": ("pb", 2), "int32": ("pi", 4), "uint16": ("pu", 2)}
 TILES, SIZE = {}, {"float32": 0, "bfloat16": 0, "int32": 0, "uint16": 0}
@@ -27,49 +30,50 @@ def tile(name, dtype, cols):
     SIZE[dtype] += -(-cols // per) * per
 
 
-for _n, _c in (("ONES", 128), ("IDENT", 128), ("BO", 128), ("E16", 8), ("E16N", 8), ("E32N", 8), ("CONSTL", 128), ("KC", 128), ("KS", 128),
-               ("KM", 128), ("K8", 128), ("LT", 128), ("P15", 128), ("P2", 128), ("M64", 128), ("NBO", 128), ("BO4K", 128),
-               ("I8N", 128), ("IBIG", 128), ("NID", 128), ("ONE16", 128), ("K63", 8), ("K155", 128), ("PNUM", 128), ("ZC", 128), ("BO01", 128), ("INEG", 128), ("I8P", 128), ("SELP", 1024),
-               ("SELN", 1024), ("DQ", 128), ("ZA", 128), ("ZB", 128)):
+for _n in ("ONES", "IDENT", "BO", "CONSTL", "KS", "KC2", "K155", "LT", "P15", "M64", "BO8K", "N8K", "N4K", "IBIG", "NBIG", "D2M", "DPB",
+           "NID", "I16", "I256", "NHUGE"):
+    tile(_n, "bfloat16", 128)
+for _n, _c in (("DG", 128), ("FULL0", 8), ("FULL1", 8), ("E1", 8), ("E16", 8), ("E16N", 8), ("E32", 8), ("E32N", 8), ("EBN", 8), ("E164", 32), ("SEL", 2048), ("ZERO", 16), ("XS", 256), ("XB", 256), ("K775", 256), ("NDQ", 128),
+               ("AB", 400), ("MASK5", 400), ("SCN", 400), ("JUNK", 16)):
     tile(_n, "bfloat16", _c)
-for _n, _c in (("BOF", 128), ("MASK", 128), ("IDF", 128), ("DQF", 128), ("SELC", 8), ("DUM", 16), ("MCOL", 1), ("M64C", 1),
-               ("THR", 1), ("THR2", 1), ("B135", 1), ("PC15", 1), ("PC2", 1), ("LIMF", 1), ("THETA", 1), ("CNT", 2), ("RJ", 2048),
-               ("QROW", 128), ("MB1", 1), ("PB1", 1), ("R01", 1), ("WN", 1), ("WP", 1), ("M3", 1), ("M3B", 1), ("JB", 16), ("DC", 16), ("WM", 16), ("LL", 16), ("TT", 16), ("OFF", 16)):
+for _n, _c in (("BOF", 128), ("MASK", 128), ("MASKF", 144), ("IDF", 128), ("DQF", 128), ("ONESF", 128), ("SELC", 8), ("THE", 8), ("DUM", 16),
+               ("MCOL", 1), ("M64C", 1), ("DGC", 1), ("OHB", 1), ("B15", 1), ("PC15", 1), ("PC2", 1), ("LIMF", 1), ("TH", 1), ("CNT", 1),
+               ("RJ", 2048), ("QROW", 128), ("MB1", 1), ("PB1", 1), ("JB", 16), ("LL", 16), ("TT", 16), ("OFF", 16), ("POW", 16), ("TWO", 16),
+               ("SGN", 50), ("FN", 256), ("VI", 256), ("VV", 256), ("T1", 256), ("XM", 256)):
     tile(_n, "float32", _c)
-for _n, _c in (("MI", 1), ("MI2", 1), ("PCI", 1), ("PCI2", 1), ("LIMI", 1), ("CI", 1), ("CI2", 1), ("DI", 256), ("WI", 256), ("XN", 256)):
+for _n, _c in (("MI", 1), ("MI2", 1), ("LIMI", 1), ("CI", 1), ("CI2", 1), ("DI", 256), ("WI", 256), ("XN", 256)):
     tile(_n, "int32", _c)
-tile("XS", "bfloat16", 256)
-tile("GL", "uint16", 16)
 tile("SL", "uint16", 16)
 for _h in range(2):
-    for _n in ("F1", "DHI", "DLO", "FULL", "ST", "OHS", "F2", "OHE", "NOE", "OHK", "OHD", "MBH", "MBL", "VMW", "VB", "SG", "TFB", "Z"):
+    for _n in ("F1", "OHS", "KEEP", "OHE", "OHK", "OHD", "VB", "SG"):
         tile(_n + str(_h), "bfloat16", CH)
-    for _n in ("SC", "SCA", "D1", "D2", "T32", "U32", "Y", "W2", "MBK", "VM", "MBA", "CF", "MB2", "D3", "VMD", "TM", "AA", "F0",
-               "FN", "VI", "VV", "T1", "T2", "YP", "YQ", "YR"):
+    for _n in ("SC", "SCA", "RR", "D2", "U32", "Y", "W2", "MBK", "VM", "VMS", "MBA", "CF", "MB2", "D3", "WR", "YM", "YP", "YQ", "YR"):
         tile(_n + str(_h), "float32", CH)
-    for _n in ("TI", "GI", "A2"):
-        tile(_n + str(_h), "int32", CH)
-    tile("RED" + str(_h), "float32", 8)
-    for _n in ("L2", "CU"):
-        tile(_n + str(_h), "uint16", CH)
+    tile("CU" + str(_h), "uint16", CH)
+    tile("L2" + str(_h), "uint16", CH)
+    tile("TI" + str(_h), "int32", CH)
+    tile("GI" + str(_h), "int32", CH)
     tile("LC" + str(_h), "uint16", 16)
     for _t in range(NV):
         tile("LU%d%d" % (_h, _t), "uint16", CH)
-        tile("W%d%d" % (_h, _t), "float32", CH)
-    for _t in range(1, NV):
+        tile("DW%d%d" % (_h, _t), "float32", 2 * CH)
+    for _t in range(1, NV + 1):
         tile("SLU%d%d" % (_h, _t), "uint16", CH)
         tile("SW%d%d" % (_h, _t), "float32", CH)
 
-SCRATCH = {"X": ("sbuf", [128, XW], "bfloat16"), "Y": ("sbuf", [128, XW], "bfloat16"), "R": ("sbuf", [128, D], "int32")}
+SCRATCH = {"R": ("sbuf", [128, D], "int32"), "NB50": ("sbuf", [128, 4, 50], "float32"),
+           "TRI50": ("sbuf", [128, 4, 50], "bfloat16")}
+for _t in range(NV + 1):
+    SCRATCH["X%d" % _t] = ("sbuf", [128, XW], "bfloat16")
 for _d in POOLS:
     SCRATCH[POOLS[_d][0]] = ("sbuf", [128, SIZE[_d]], _d)
 for _h in range(2):
-    for _n in ("x1", "x2", "z", "xc"):
+    for _n in ("x1", "x2", "z", "xc", "ax"):
         SCRATCH[_n + str(_h)] = ("sbuf", [128, 16 * CH], "bfloat16")
-    SCRATCH["ax" + str(_h)] = ("sbuf", [128, 16, CH], "bfloat16")
-    SCRATCH["P0_" + str(_h)] = ("psum", [128, 512], "float32")
-    for _b in (1, 2, 3):
-        SCRATCH["P%d_%d" % (_b, _h)] = ("psum", [128, 4, CH], "float32")
+    SCRATCH["MBS" + str(_h)] = ("sbuf", [128, 4, 32], "float32")
+for _n in ("K0", "K1", "M0", "M1", "B0", "B1", "TB"):
+    SCRATCH[_n] = ("psum", [128, 512], "float32")
+SCRATCH["S5"] = ("psum", [128, 8, 64], "float32")
 
 SEMAPHORES = ["cV", "cS", "cT", "cG"] + ["d%d" % k for k in range(40)] + \
     ["r%d" % k for k in range(12)] + ["l%d" % k for k in range(12)]
@@ -87,11 +91,18 @@ def rank_program(g, core, T, topo):
         b = cols if b is None else b
         return T[pool][:, off + a:off + b:s] if s else T[pool][:, off + a:off + b]
 
+    def rev(name):
+        pool, off, cols = TILES[name]
+        return T[pool][:, off + cols - 1:(off - 1 if off else None):-1]
+
+    def slot(bank, j):
+        return T.S5[:, 2 * j:2 * j + 2, :] if bank == "S5" else T[bank][:, 128 * j:128 * j + 128]
+
     ops = []
-    last_w, readers, banks = {}, {}, {}
+    last_w, readers, banks, last_pe = {}, {}, {}, {}
     dcount, now = [0], [0.0]
 
-    def add(eng, fn, rd, wr, cost, sem=None, need=1, extra=(), comp=True, acc=False):
+    def add(eng, fn, rd, wr, cost, hold=None, sem=None, need=1, extra=(), comp=True, acc=False):
         k = len(ops)
         deps = {}
         phys = {"SD": "S"}.get(eng, eng)
@@ -111,18 +122,21 @@ def rank_program(g, core, T, topo):
                 dep(last_w[x], "waw")
             for o in readers.get(x, ()):
                 dep(o, "war")
-        for x in sorted(set(rd) | set(wr)):
-            if x[0] == "P" and x[2:3] == "_":
-                ep = banks.setdefault(x[:4], [phys, [], []])
-                if ep[0] != phys:
-                    ep[0], ep[1], ep[2] = phys, [], ep[1]
-                for o in ep[2]:
-                    dep(o, "bank")
-                if k not in ep[1]:
-                    ep[1].append(k)
+        for b in sorted(set(x[1:3] for x in list(rd) + list(wr) if x[0] == "@")):
+            ep = banks.setdefault(b, [phys, [], []])
+            if ep[0] != phys:
+                ep[0], ep[1], ep[2] = phys, [], ep[1]
+            for o in ep[2]:
+                dep(o, "bank")
+            ep[1].append(k)
+            if phys == "T":
+                if b in last_pe:
+                    deps.setdefault(last_pe[b], "order")
+                last_pe[b] = k
         for o in extra:
             deps.setdefault(o, "order")
-        ops.append(dict(eng=eng, phys=phys, comp=comp, fn=fn, deps=deps, cost=cost, sem=sem, need=need, name=(wr or rd)[0], base=now[0], bonus=now[0] + PRI.get((wr or rd)[0], 0)))
+        ops.append(dict(eng=eng, phys=phys, comp=comp, fn=fn, deps=deps, cost=cost, hold=cost if hold is None else hold, sem=sem, need=need,
+                        name=(wr or rd)[0], bonus=now[0]))
         for x in rd:
             readers.setdefault(x, []).append(k)
         for x in wr:
@@ -130,22 +144,30 @@ def rank_program(g, core, T, topo):
             readers[x] = []
         return k
 
-    def V(fn, rd, wr, n, c=0.83):
-        return add("V", lambda: fn(g.vector), rd, wr, 0.04 + max(n, 64) * c / 1000)
+    def V(fn, rd, wr, n):
+        return add("V", lambda: fn(g.vector), rd, wr, COST[0] + max(n, 64) * 0.83e-3)
 
     def S(fn, rd, wr, n):
-        return add("S", lambda: fn(g.scalar), rd, wr, 0.06 + max(n, 64) * 0.83 / 1000)
+        return add("S", lambda: fn(g.scalar), rd, wr, COST[1] + max(n, 64) * 0.83e-3)
 
-    def P(fn, rd, wr, n, acc=False, extra=()):
-        return add("T", lambda: fn(g.tensor), rd, wr, 0.05 + n * 0.45 / 1000, acc=acc, extra=extra)
+    def P(lst, rd, wr, n, start=True, stop=True, after=()):
+        def f():
+            for k, (o, l, x) in enumerate(lst):
+                r = g.tensor.matmul(o, l, x, start[k] if isinstance(start, list) else start and k == 0,
+                                    stop[k] if isinstance(stop, list) else stop and k == len(lst) - 1)
+            return r
+        return add("T", f, rd, wr, 0.06 + n * COST[2], hold=n * COST[2], acc=start is False, extra=after)
 
     def G(fn, rd, wr, n):
-        return add("G", lambda: fn(g), rd, wr, 0.17 + n * 1.66 / 1000)
+        return add("G", lambda: fn(g), rd, wr, 0.17 + n * 1.66e-3)
 
     def dma(eng, out, in_, rd, wr, lat):
         s = "d%d" % dcount[0]
         dcount[0] += 1
-        return add(eng, lambda: QUEUE[eng].dma_start(out, in_), rd, wr, lat, sem=s, need=16, comp=False)
+        k = add(eng, lambda: QUEUE[eng].dma_start(out, in_), rd, wr, lat, hold=0.05, sem=s, need=16, extra=loads.get(eng, []) if not rd else [], comp=False)
+        loads[eng] = [k]
+
+    loads = {}
 
     def ts(out, i0, s1, op0, s2=None, op1=None):
         if s2 is None:
@@ -158,407 +180,425 @@ def rank_program(g, core, T, topo):
     def cp(out, a):
         return lambda v: v.tensor_copy(out, a)
 
+    def ms(out, c):
+        return lambda v: v.memset(out, c)
+
+    def scan(out, a, b, op0, op1, first=0.0):
+        return lambda v: v.tensor_tensor_scan(out, a, b, first, op0, op1)
+
     def act(out, a, func=AF.Identity, bias=0.0, scale=1.0):
         return lambda s: s.activation(out, a, func, bias=bias, scale=scale)
 
-    def mms(lst, start=True, stop=True):
-        def f(pe):
-            r = None
-            for k, (o, l, x) in enumerate(lst):
-                r = pe.matmul(o, l, x, start and k == 0, stop and k == len(lst) - 1)
-            return r
-        return f
+    def sel(out, a, pattern, op, fill, base, mult):
+        return lambda q: q.affine_select(out, a, pattern, op, fill, base, mult)
 
-    dma("Y", t("WI"), T.why[:], [], ["WI"], 2.5)
-    dma("SD", t("DI"), T.drugs[:], [], ["DI"], 2.5)
+    def iota(out, pattern, base, mult):
+        return lambda q: q.iota(out, pattern, base, mult, allow_small_or_imprecise_dtypes=True)
+
+    now[0] = 100.0
+    dma("Y", t("WI"), T.why[:], [], ["WI"], 1.5 + DM * 1.3)
+    dma("SD", t("DI"), T.drugs[:], [], ["DI"], 1.5 + DM * 2.6)
+    dma("Y", t("LIMI"), T.lim[:], [], ["LIMI"], 1.6 + DM * 2.6)
     for k in range(NP):
-        dma("Y" if k % 2 == 0 else "SD", T.X[:, k * PW:(k + 1) * PW], T.eff[:, k * PW:(k + 1) * PW], [], ["Xr%d" % k], 4.0 + 1.2 * k)
-    dma("Y", t("LIMI"), T.lim[:], [], ["LIMI"], 3)
-    dma("Y", T.R[:, :D // 2], T.rem[:, :D // 2], [], ["Ra"], 11.0)
-    dma("Y", T.R[:, D // 2:], T.rem[:, D // 2:], [], ["Rb"], 11.0)
+        dma("Y" if k % 2 == 0 else "SD", T.X0[:, k * PW:(k + 1) * PW], T.eff[:, k * PW:(k + 1) * PW], [], ["Xr%d" % k], 1.6 + DM * (2.6 + 2.2 * (k + 1)))
+    dma("Y", T.R[:, :D // 2], T.rem[:, :D // 2], [], ["Ra"], 1.6 + DM * 20.3)
+    dma("Y", T.R[:, D // 2:], T.rem[:, D // 2:], [], ["Rb"], 1.6 + DM * 29.1)
+    XK = [["Xr%d" % k for k in range(NP)] + ["Xz"]] + [["X%d" % k] for k in range(1, NV + 1)]
 
-    LN2 = math.log(2.0)
-    V(lambda v: v.memset(t("ONES"), 1.0), [], ["ONES"], 64)
-    V(lambda v: v.memset(t("SELP"), 1.0), [], ["SELP"], 512)
-    V(lambda v: v.memset(T.X[:, D:], 0.0), [], ["Xz"], 456)
+    now[0] = 5.0
+    V(ms(t("ONES"), 1.0), [], ["ONES"], 64)
     G(lambda q: q.iota(t("MI"), [[0, 1]], 0, 1), [], ["MI"], 1)
+    G(sel(t("IDF"), t("ONES"), [[-1, 128]], A.is_equal, 0.0, 0, 1), ["ONES"], ["IDF"], 128)
     V(ts(t("MI2"), t("MI"), 15, A.bitwise_and), ["MI"], ["MI2"], 64)
     V(cp(t("MCOL"), t("MI2")), ["MI2"], ["MCOL"], 64)
-    G(lambda q: q.affine_select(t("IDENT"), t("ONES"), [[-1, 128]], A.is_equal, 0.0, 0, 1), ["ONES"], ["IDENT"], 128)
-    G(lambda q: q.affine_select(t("BO"), t("ONES"), [[-16, 8], [0, 16]], A.is_ge, 0.0, 0, 1), ["ONES"], ["BO"], 128)
-    G(lambda q: q.affine_select(t("BO"), t("BO"), [[16, 8], [0, 16]], A.is_ge, 0.0, 15, -1), ["BO"], ["BO"], 128)
-    G(lambda q: q.iota(t("QROW"), [[0, 8], [1, 16]], 0, 0, allow_small_or_imprecise_dtypes=True), [], ["QROW"], 128)
-    V(ts(t("DQ"), t("QROW"), t("MCOL"), A.is_equal), ["QROW", "MCOL"], ["DQ"], 128)
-    G(lambda q: q.affine_select(t("CONSTL"), t("ONES"), [[0, 128]], A.is_ge, 0.0, 1, -1), ["ONES"], ["CONSTL"], 128)
-    S(act(t("PC2"), t("MCOL"), AF.Exp, 0.0, LN2), ["MCOL"], ["PC2"], 1500)
-    V(cp(t("PCI2"), t("PC2")), ["PC2"], ["PCI2"], 64)
-    V(cp(t("PC2"), t("PCI2")), ["PCI2"], ["PC2"], 64)
-    S(act(t("PC15"), t("MCOL"), AF.Exp, 0.0, -LN2), ["MCOL"], ["PC15"], 64)
-    V(ts(t("PCI"), t("PC15"), 32768.0, A.mult), ["PC15"], ["PCI"], 64)
-    V(cp(t("PC15"), t("PCI")), ["PCI"], ["PC15"], 64)
-    S(act(t("DQF"), t("DQ"), AF.Copy), ["DQ"], ["DQF"], 128)
-    S(act(t("BOF"), t("BO"), AF.Copy), ["BO"], ["BOF"], 128)
+    S(act(t("IDENT"), t("IDF"), AF.Copy), ["IDF"], ["IDENT"], 128)
+    G(iota(t("QROW"), [[0, 8], [1, 16]], 0, 0), [], ["QROW"], 128)
+    V(ts(t("DQF"), t("QROW"), t("MCOL"), A.is_equal), ["QROW", "MCOL"], ["DQF"], 128)
+    V(ms(t("TWO"), 2.0), [], ["TWO"], 64)
+    V(ms(t("ZERO"), 0.0), [], ["ZERO"], 128)
+    V(scan(t("POW"), t("TWO"), t("ZERO", 0, 16), A.mult, A.add, 0.5), ["TWO", "ZERO"], ["POW"], 64)
+    V(tt(t("TT"), t("POW"), t("DQF", 0, 16), A.mult), ["POW", "DQF"], ["TT"], 64)
+    V(lambda v: v.tensor_reduce(t("PC2"), t("TT"), AxisListType.X, A.add), ["TT"], ["PC2"], 64)
     V(ts(t("MB1"), t("MCOL"), -BIG, A.mult, -BIG, A.add), ["MCOL"], ["MB1"], 64)
-    V(ts(t("PB1"), t("MCOL"), BIG, A.mult, BIG, A.add), ["MCOL"], ["PB1"], 64)
-    G(lambda q: q.iota(t("JB"), [[int(BIG) // 8, 16]], 0, 0, allow_small_or_imprecise_dtypes=True), [], ["JB"], 16)
-    V(ts(t("JB"), t("JB"), 8.0, A.mult, t("PB1"), A.subtract), ["JB", "PB1"], ["JB"], 64)
-    V(ts(t("JB"), t("JB"), BIG - 0.5, A.add, KK, A.mult), ["JB"], ["JB"], 64)
+    V(ts(t("JB"), t("QROW", 0, 16), t("MCOL"), A.subtract, BIG, A.mult), ["QROW", "MCOL"], ["JB"], 64)
+    V(ts(t("JB"), t("JB"), -0.5, A.add, KK, A.mult), ["JB"], ["JB"], 64)
 
-    for h in range(2):
-        H = str(h)
-        now[0] = BONUS[9] * (1 - h)
-        DI = t("DI", h * CH, h * CH + CH)
-        WI = t("WI", h * CH, h * CH + CH)
-        V(ts(t("FN" + H), WI, t("MCOL"), A.not_equal), ["WI", "MCOL"], ["FN" + H], 128)
-        V(ts(t("VI" + H), WI, 1.0, A.add, BIG, A.mult), ["WI"], ["VI" + H], 128)
-        V(tt(t("VI" + H), t("VI" + H), t("FN" + H), A.mult), ["VI" + H, "FN" + H], ["VI" + H], 256)
-        V(ts(t("VV" + H), t("VI" + H), t("MB1"), A.add, t("PC2"), A.add), ["VI" + H, "MB1", "PC2"], ["VV" + H], 128)
-        V(cp(t("LU%d0" % h), DI), ["DI"], ["LU%d0" % h], 128)
-        V(ts(t("T2" + H), WI, 1 / 64, A.mult), ["WI"], ["T2" + H], 128)
-    now[0] = 0.0
+    V(ts(t("FN"), t("WI"), t("MCOL"), A.not_equal), ["WI", "MCOL"], ["FN"], 256)
+    V(ts(t("VI"), t("WI"), 1.0, A.add, BIG, A.mult), ["WI"], ["VI"], 256)
+    V(tt(t("VI"), t("VI"), t("FN"), A.mult), ["VI", "FN"], ["VI"], 512)
+    V(ts(t("VV"), t("VI"), t("MB1"), A.add, t("PC2"), A.add), ["VI", "MB1", "PC2"], ["VV0", "VV1"], 256)
     for j in range(15, -1, -1):
         RJ = "RJ%d" % j
         rj = t("RJ", j * 128, j * 128 + 128)
-        S(act(rj, t("BOF"), AF.Copy, 0.0, t("DQF", j, j + 1)), ["BOF", "DQF"], [RJ], 128)
-        G((lambda rj: lambda q: q.affine_select(rj, rj, [[1, 128]], A.not_equal, 1.0, 0, -1))(rj), [RJ], [RJ], 128)
+        now[0] = 5.0
+        G(sel(rj, t("IDF"), [[-16, 8], [0, 16]], A.not_equal, 1.0, -j, 1), ["IDF"], [RJ], 128)
         for h in range(2):
             H = str(h)
             now[0] = BONUS[9] * (1 - h)
-            o, key = T["P1_" + H][:, 0, :], "P1_%s0" % H
-            S(act(t("SG" + H), t("VV" + H), AF.Relu, t("JB", j, j + 1), -KK), ["VV" + H, "JB"], ["SG" + H], 128)
-            P(mms([(o, rj, t("VV" + H))], True, False), [RJ, "VV" + H], [key], 512)
-            P(mms([(o, t("IDENT"), t("SG" + H))], False, True), ["IDENT", "SG" + H], [key], 128, True)
-            V(tt(t("VV" + H), t("VV" + H), o, A.min), ["VV" + H, key], ["VV" + H], 128)
-    for h in range(2):
-        H = str(h)
-        now[0] = BONUS[9] * (1 - h)
-        S(act(t("T1" + H), t("VV" + H), AF.Identity, t("PB1"), 1.0), ["VV" + H, "PB1"], ["T1" + H], 128)
-        V(tt(t("W%d0" % h), t("T1" + H), t("T2" + H), A.add), ["T1" + H, "T2" + H], ["W%d0" % h], 256)
-
+            bank = ("S5", "TB")[h]
+            o, key, vv = slot(bank, 0), "@%s:c" % bank, t("VV", h * CH, h * CH + CH)
+            S(act(t("SG" + H), vv, AF.Relu, t("JB", j, j + 1), -KK), ["VV" + H, "JB"], ["SG" + H], 128)
+            P([(o, rj, vv)], [RJ, "VV" + H], [key], 512, True, False)
+            P([(o, t("IDENT"), t("SG" + H))], ["IDENT", "SG" + H], [key], 128, False, True)
+            V(tt(vv, vv, o, A.min), ["VV" + H, key], ["VV" + H], 128)
     now[0] = 0.0
+    V(ts(t("PB1"), t("MCOL"), BIG, A.mult), ["MCOL"], ["PB1"], 64)
+    S(act(t("DPB"), t("IDENT"), AF.Copy, 0.0, t("PB1")), ["IDENT", "PB1"], ["DPB"], 128)
+    S(act(t("IBIG"), t("IDENT"), AF.Copy, 0.0, BIG), ["IDENT"], ["IBIG"], 128)
+    V(ts(t("T1"), t("WI"), 1 / 64, A.mult, 1 / 64, A.add), ["WI"], ["T1"], 256)
+    for h in range(2):
+        H, c = str(h), (h * CH, h * CH + CH)
+        V(cp(t("LU%d0" % h), t("DI", *c)), ["DI"], ["LU%d0" % h], 128)
+        V(ts(t("F1" + H), t("LU%d0" % h), D - 0.5, A.is_lt), ["LU%d0" % h], ["F1" + H], 64)
+        bank = ("S5", "TB")[h]
+        o, key = slot(bank, 1), "@%s:w" % bank
+        P([(o, t("IDF"), t("VV", *c)), (o, t("DPB"), t("ONES")), (o, t("IBIG"), t("F1" + H)), (o, t("IDF"), t("T1", *c))],
+          ["IDF", "VV" + H, "DPB", "ONES", "IBIG", "F1" + H, "T1"], [key], 1280)
+        S(act(t("DW%d0" % h, CH), o, AF.Relu), [key], ["W%d0" % h], 128)
 
-    V(ts(t("E16"), t("BO", 0, 128, 16), 16.0, A.mult), ["BO"], ["E16"], 64)
-    V(ts(t("E16N"), t("BO", 0, 128, 16), -16.0, A.mult), ["BO"], ["E16N"], 64)
-    V(ts(t("E32N"), t("BO", 0, 128, 16), -32.0, A.mult), ["BO"], ["E32N"], 64)
-    V(cp(t("SELC"), t("BO", 0, 128, 16)), ["BO"], ["SELC"], 64)
-    G(lambda q: q.iota(t("KC"), [[0, 8], [-1, 16]], 15, 0, allow_small_or_imprecise_dtypes=True), [], ["KC"], 128)
-    G(lambda q: q.affine_select(t("KS"), t("KC"), [[0, 128]], A.is_ge, 131072.0, 0, -1), ["KC"], ["KS"], 128)
-    G(lambda q: q.affine_select(t("KC"), t("KC"), [[0, 128]], A.is_ge, 0.0, 0, -1), ["KC"], ["KC"], 128)
-    EPS = 2.0 ** -8
-    G(lambda q: q.affine_select(t("LT"), t("BO"), [[1, 128]], A.is_gt, EPS, 0, -1), ["BO"], ["LT"], 128)
-    G(lambda q: q.affine_select(t("LT"), t("LT"), [[1, 128]], A.not_equal, -32.0, 0, -1), ["LT"], ["LT"], 128)
-    V(tt(t("LT"), t("LT"), t("BO"), A.mult), ["LT", "BO"], ["LT"], 256)
-    V(ts(t("THR"), t("MCOL"), 0.5, A.subtract, EPS / 2, A.max), ["MCOL"], ["THR"], 64)
-    V(ts(t("THR"), t("THR"), 2.0, A.mult), ["THR"], ["THR"], 64)
-    V(ts(t("THR2"), t("MCOL"), EPS - 1, A.mult, 32 - 15 * EPS, A.add), ["MCOL"], ["THR2"], 64)
-    V(tt(t("THR"), t("THR"), t("THR2"), A.add), ["THR", "THR2"], ["THR"], 64)
-    V(ts(t("M64C"), t("MCOL"), 1 / 64, A.mult), ["MCOL"], ["M64C"], 64)
-    for nm, src, sc in (("P15", "BO", "PC15"), ("P2", "BO", "PC2"), ("M64", "BO", "M64C"), ("NBO", "BO", -0.5), ("BO4K", "BO", 4096.0),
-                        ("I8P", "IDENT", 8192.0), ("INEG", "IDENT", -BIG), ("IBIG", "IDENT", BIG), ("NID", "IDENT", -1.0), ("IDF", "IDENT", 1.0)):
-        S(act(t(nm), t(src), AF.Copy, 0.0, t(sc) if sc in TILES else sc), [src] + ([sc] if sc in TILES else []), [nm], 128)
-    for k, nm in enumerate(("ZA", "ZB")):
-        G((lambda k, nm: lambda q: q.affine_select(t(nm), t("BO"), [[0, 8], [1, 16]], A.is_equal, 0.0, -k, 0))(k, nm), ["BO"], [nm], 128)
-    V(lambda v: v.memset(t("ONE16"), 1 / 16), [], ["ONE16"], 64)
-    V(ts(t("B135"), t("MCOL"), -1.0, A.mult, 135.0, A.add), ["MCOL"], ["B135"], 64)
-    V(lambda v: v.memset(t("MASK"), 1.0), [], ["MASK"], 128)
-    V(lambda v: v.memset(t("MASK", 0, 128, 16), 0.0), [], ["MASK"], 64)
-    V(lambda v: v.memset(t("K63"), -31.5), [], ["K63"], 64)
-    V(lambda v: v.memset(t("K155"), -7.75), [], ["K155"], 64)
-    G(lambda q: q.iota(t("PNUM"), [[1, 128]], 0, 0, allow_small_or_imprecise_dtypes=True), [], ["PNUM"], 128)
-    G(lambda q: q.affine_select(t("PNUM"), t("PNUM"), [[0, 128]], A.is_ge, 1.0, 0, -1), ["PNUM"], ["PNUM"], 128)
-    V(lambda v: v.memset(t("ZC"), 0.0), [], ["ZC"], 64)
-    for r, m in ((0, 2), (1, 3)):
-        G((lambda r, m: lambda q: q.affine_select(t("ZC"), t("ZC"), [[0, 8], [1, 16]], A.not_equal, 1.0, 64 * r - m, -64))(r, m), ["ZC"], ["ZC"], 128)
-    V(ts(t("R01"), t("MCOL"), 1.5, A.is_lt), ["MCOL"], ["R01"], 64)
-    V(ts(t("BO01"), t("BO"), t("R01"), A.mult), ["BO", "R01"], ["BO01"], 64)
-    V(ts(t("WN"), t("R01"), -255.0, A.mult, -1.0, A.add), ["R01"], ["WN"], 64)
-    V(ts(t("M3"), t("MCOL"), 2.5, A.is_lt), ["MCOL"], ["M3"], 64)
-    V(tt(t("WN"), t("WN"), t("M3"), A.mult), ["WN", "M3"], ["WN"], 64)
-    V(ts(t("M3B"), t("MCOL"), 3.0, A.is_equal, 64.0, A.mult), ["MCOL"], ["M3B"], 64)
-    V(tt(t("WP"), t("M3B"), t("WN"), A.subtract), ["M3B", "WN"], ["WP"], 64)
-    G(lambda q: q.affine_select(t("SELP"), t("SELP"), [[-16, 8], [0, 128]], A.is_ge, 0.0, 0, 1), ["SELP"], ["SELP"], 1024)
-    G(lambda q: q.affine_select(t("SELP"), t("SELP"), [[16, 8], [0, 128]], A.is_ge, 0.0, 15, -1), ["SELP"], ["SELP"], 1024)
-    S(act(t("SELN"), t("SELP"), AF.Copy, 0.0, t("WN")), ["SELP", "WN"], ["SELN"], 1024)
-    S(act(t("SELP"), t("SELP"), AF.Copy, 0.0, t("WP")), ["SELP", "WP"], ["SELP"], 1024)
-    G(lambda q: q.iota(t("DUM"), [[16, 16]], PAD + 1, 0, allow_small_or_imprecise_dtypes=True), [], ["DUM"], 16)
-    V(ts(t("DUM"), t("DUM"), t("MCOL"), A.add), ["DUM", "MCOL"], ["DUM"], 64)
-    for k in range(NP):
-        sl = T.X[:, k * PW:(k + 1) * PW]
-        V(ts(sl, sl, 1.0, A.add), ["Xr%d" % k], ["Xr%d" % k], PW / 2)
+    V(ms(T.X0[:, D:], 0.0), [], ["Xz"], 64)
+    G(sel(t("BO"), t("ONES"), [[-16, 8], [0, 16]], A.is_ge, 0.0, 0, 1), ["ONES"], ["BO"], 128)
+    G(sel(t("BO"), t("BO"), [[16, 8], [0, 16]], A.is_ge, 0.0, 15, -1), ["BO"], ["BO"], 128)
+    G(sel(t("CONSTL"), t("ONES"), [[0, 128]], A.is_ge, 0.0, 1, -1), ["ONES"], ["CONSTL"], 128)
+    E = t("BO", 0, 128, 16)
+    for nm, sc in (("E1", 1.0), ("E16", 16.0), ("E16N", -16.0), ("E32", 32.0), ("E32N", -32.0), ("EBN", -BIG), ("SELC", 1.0)):
+        V(ts(t(nm), E, sc, A.mult), ["BO"], [nm], 64)
+    V(ts(t("E164"), t("BO", 0, 128, 4), 16.0, A.mult), ["BO"], ["E164"], 64)
+    G(iota(t("KS"), [[0, 8], [-1, 16]], 15, 0), [], ["KS"], 128)
+    G(sel(t("KS"), t("KS"), [[0, 128]], A.is_ge, BIG, 0, -1), ["KS"], ["KS"], 128)
+    V(ts(t("KC2"), t("QROW"), 0.5, A.mult, -8.0, A.add), ["QROW"], ["KC2"], 128)
+    V(ms(t("K155"), -3.75), [], ["K155"], 64)
+    V(ms(t("K775"), -7.75), [], ["K775"], 128)
+    V(ts(t("NDQ"), t("DQF"), BIG, A.mult, -BIG, A.add), ["DQF"], ["NDQ"], 128)
+    G(sel(t("LT"), t("BO"), [[1, 128]], A.is_gt, 0.0, 0, -1), ["BO"], ["LT"], 128)
+    G(sel(t("LT"), t("LT"), [[1, 128]], A.not_equal, -32.0, 0, -1), ["LT"], ["LT"], 128)
+    V(ts(t("OHB"), t("MCOL"), -1.0 if UR == "G" else -2.0, A.mult, 1.0 if UR == "G" else 33.0, A.add), ["MCOL"], ["OHB"], 64)
+    V(ts(t("M64C"), t("MCOL"), 1 / 64, A.mult, 1 / 64, A.add), ["MCOL"], ["M64C"], 64)
+    V(ts(t("DGC"), t("MCOL"), -1.0, A.mult, 16.0, A.add), ["MCOL"], ["DGC"], 64)
+    V(ts(t("B15"), t("MCOL"), -1.0, A.mult, 135.0, A.add), ["MCOL"], ["B15"], 64)
+    V(ms(t("TWO"), 0.5), [], ["TWO"], 64)
+    V(scan(t("POW"), t("TWO"), t("ZERO", 0, 16), A.mult, A.add, 65536.0 if UR == "G" else 1.0), ["TWO", "ZERO"], ["POW"], 64)
+    V(tt(t("TT"), t("POW"), t("DQF", 0, 16), A.mult), ["POW", "DQF"], ["TT"], 64)
+    V(lambda v: v.tensor_reduce(t("PC15"), t("TT"), AxisListType.X, A.add), ["TT"], ["PC15"], 64)
+    for nm, src, sc in (("DG", "IDENT", "DGC"), ("P15", "BO", "PC15"), ("BOF", "BO", 1.0), ("M64", "BO", "M64C"), ("BO8K", "BO", 8192.0),
+                        ("NBIG", "BO", -BIG - MAGIC), ("N8K", "IDENT", -8192.0), ("N4K", "IDENT", -4096.0),
+                        ("D2M", "IDENT", "PC2"), ("NID", "IDENT", -1.0), ("I16", "IDENT", 16.0), ("I256", "IDENT", 1 / 256),
+                        ("NHUGE", "IDENT", -BIG * 65536)):
+        if nm != "I256" or "S" in UR + ZR:
+            S(act(t(nm, 0, 128), t(src), AF.Copy, 0.0, t(sc) if sc in TILES else sc), [src] + ([sc] if sc in TILES else []), [nm], 128)
+    V(ms(t("ONESF"), 1.0), [], ["ONESF"], 128)
+    V(ms(t("MASK"), 1.0), [], ["MASK"], 128)
+    V(ms(t("MASK", 0, 128, 16), 0.0), [], ["MASK"], 64)
+    for q in range(4 * (UR != "G")):
+        G(lambda e, q=q: e.iota(t("SEL", 512 * q, 512 * q + 512), [[4, 4], [16, 8], [0, 16]], q, -1, allow_small_or_imprecise_dtypes=True),
+          [], ["SEL%d" % q], 512)
+        V(ts(t("SEL", 512 * q, 512 * q + 512), t("SEL", 512 * q, 512 * q + 512), 0.0, A.is_equal), ["SEL%d" % q], ["SEL%d" % q], 256)
+    V(ms(t("SGN"), -1.0), [], ["SGN"], 64)
+    V(ms(t("SGN", 16, 50, 33), 1.0), [], ["SGN"], 64)
+    for r in range(4):
+        V(ts(T.NB50[:, r, 0:17], t("SGN", 0, 17), t("SELC", 2 * r, 2 * r + 1), A.mult), ["SGN", "SELC"], ["NB%da" % r], 64)
+        V(ts(T.NB50[:, r, 17:50], t("SGN", 17, 50), t("SELC", 2 * r + 1, 2 * r + 2), A.mult), ["SGN", "SELC"], ["NB%db" % r], 64)
+    NB = ["NB%d%s" % (r, c) for r in range(4) for c in "ab"]
+    V(ms(T.TRI50[:], 0.0), [], ["TRI50"], 100)
+    for a in (0, 17):
+        V(ts(T.TRI50[:, :, a:a + 16], t("QROW", 0, 64), t("MCOL"), A.is_ge, 8192.0, A.mult), ["QROW", "MCOL", "TRI50"], ["TRI50"], 64)
+    V(ms(t("MASK5"), 0.0), [], ["MASK5"], 200)
+    for b in range(2):
+        V(ms(t("MASK5", 17 * b, 400, 50), 16384.0), [], ["MASK5"], 64)
+        V(ts(t("DUM", b, b + 1), t("MCOL"), PAD + 1.0 + 16 * b, A.add), ["MCOL"], ["DUM%d" % b], 64)
     V(cp(t("LIMF"), t("LIMI")), ["LIMI"], ["LIMF"], 64)
-    V(ts(t("THETA"), t("LIMF"), 120.0, A.subtract), ["LIMF"], ["THETA"], 64)
-    XK = ["Xr%d" % k for k in range(NP)] + ["Xz"]
-    XALL = T.X[:]
+    V(ts(t("TH"), t("LIMF"), BIG / 16, A.mult), ["LIMF"], ["TH"], 64)
+    V(ts(t("THE"), t("SELC"), t("TH"), A.mult), ["SELC", "TH"], ["THE"], 64)
 
-    def gather(dst, lst, h, plan):
+    def gather(dst, lst, h, vt, plan):
         w = []
         for (e, a, b) in plan:
-            if a < b:
-                key = "%s%d:%d" % (dst, h, a)
-                o, s = T[dst + str(h)][:, 16 * a:16 * b], XALL.indirect(t(lst, a, b))
-                if e == "S":
-                    S(act(o, s, AF.Copy), XK + [lst], [key], 16 * (b - a) * 1.5)
-                else:
-                    V(cp(o, s), XK + [lst], [key], 16 * (b - a) * 1.5)
-                w.append(key)
+            key = "%s%d:%d" % (dst, h, a)
+            o, s = T[dst + str(h)][:, 16 * a:16 * b], T["X%d" % vt][:].indirect(t(lst, a, b))
+            (S if e == "S" else V)(act(o, s, AF.Copy) if e == "S" else cp(o, s), XK[vt] + [lst], [key, dst + str(h) + "w%d" % a], 16 * (b - a) * 1.56)
+            w.append(key)
         return w
 
-    def sums(h, slot, x, f, plan, kx):
+    def argmax(h, kill=None, kl=None):
         H = str(h)
-        for (e, a, b), key in zip(plan, kx):
-            o = T["P3_" + H][:, slot, a:b]
-            P(mms([(o, t("IDENT"), x[:, 16 * a + m:16 * b:16]) for m in range(16)] + [(o, t("NBO"), t(f, a, b)), (o, t("CONSTL"), t("K155", a, b))]),
-              ["IDENT", "NBO", "CONSTL", "K155", f, key], ["P3_%s%d" % (H, slot)] if a == 0 else ["P3_%s%d+%d" % (H, slot, a)], 18 * max(64, b - a))
-        return ["P3_%s%d" % (H, slot)] + ["P3_%s%d+%d" % (H, slot, a) for e, a, b in plan if a]
+        src, k16 = "@K%s:k" % H, slot("K" + H, 0)
+        V(scan(t("SCA" + H), t("MASK"), k16, A.mult, A.max), [src, "MASK"], ["SCA" + H], 128)
+        if kill is not None:
+            V(tt(t("SCA" + H, 15, 128, 16), t("SCA" + H, 15, 128, 16), kill, A.max), [kl, "SCA" + H], ["SCA" + H], 64)
+        V(scan(rev("SC" + H), t("MASK"), rev("SCA" + H), A.mult, A.max), ["SCA" + H, "MASK"], ["SC" + H], 128)
+        V(tt(t("OHD" + H), k16, t("SC" + H), A.is_equal), [src, "SC" + H], ["OHD" + H], 128)
 
-    def argmax(h):
-        H = str(h)
-        src, p0 = "P0_" + H, T["P0_" + H]
-        V(lambda v: v.tensor_tensor_scan(t("SCA" + H), t("MASK"), p0[:, 0:128], 0.0, A.mult, A.max), [src, "MASK"], ["SCA" + H], 128)
-        V(lambda v: v.tensor_tensor_scan(t("SC" + H)[:, ::-1], t("MASK"), t("SCA" + H)[:, ::-1], 0.0, A.mult, A.max), ["SCA" + H, "MASK"], ["SC" + H], 128)
-        V(tt(t("OHD" + H), p0[:, 0:128], t("SC" + H), A.is_equal), [src, "SC" + H], ["OHD" + H], 128)
+    def row(x, m):
+        k = 4 * (m % 4) + m // 4
+        return x[:, 128 * k:128 * k + 128]
+
+    def four(out, x, b, y, op):
+        def f(v):
+            for m in range(b, 16, 4):
+                r = v.tensor_tensor(row(out, m), x[:, m::16], y, op)
+            return r
+        return f
+
+    kx1, kx2 = {}, {}
 
     def phase1(vt, h):
         H = str(h)
-        LU, W = "LU%d%d" % (h, vt), "W%d%d" % (h, vt)
-        p0, p1, p3 = T["P0_" + H], T["P1_" + H], T["P3_" + H]
-        x = T["x1" + H]
-        kx = gather("x1", LU, h, SHARE[("a" if vt else "f") + H])
-        V(ts(t("D1" + H), t(LU), 1.0, A.add), [LU], ["D1" + H], 128)
-        S(act(t("F1" + H), t("D1" + H), AF.Sign, 3456.5, -1.0), ["D1" + H], ["F1" + H], 128)
-        S(act(t("DHI" + H), t("D1" + H), AF.Copy), ["D1" + H], ["DHI" + H], 128)
-        V(tt(t("DLO" + H), t("D1" + H), t("DHI" + H), A.subtract), ["D1" + H, "DHI" + H], ["DLO" + H], 256)
-        P(mms([(p1[:, 3, :], t("BO"), t("F1" + H))]), ["BO", "F1" + H], ["P1_%s3" % H], 128)
-        S(act(t("FULL" + H), p1[:, 3, :], AF.Relu, -15.0), ["P1_%s3" % H], ["FULL" + H], 128)
-        P(mms([(p0[:, 0:128], t("CONSTL"), t("KC"))] + [(p0[:, m:128:16], x[:, m::16], t("E16")) for m in range(16)]),
-          ["CONSTL", "KC", "E16"] + kx, ["P0_" + H], 128 + 16 * 64)
-        argmax(h)
-        kt = sums(h, 0, x, "F1" + H, SHARE[("a" if vt else "f") + H], kx)
-        S(act(t("T32" + H), p3[:, 0, :], AF.Copy), kt, ["T32" + H], 128)
-        P(mms([(p3[:, 1, :], t("BOF"), t("T32" + H)), (p3[:, 1, :], t("BO4K"), t("FULL" + H))]),
-          ["BOF", "T32" + H, "BO4K", "FULL" + H], ["P3_%s1" % H], 640)
-        V(ts(t("ST" + H), p3[:, 1, :], t("THETA"), A.is_ge), ["P3_%s1" % H, "THETA"], ["ST" + H], 128)
-        P(mms([(p1[:, 0, :], t("OHD" + H), t("IDENT"))]), ["OHD" + H, "IDENT"], ["P1_%s0" % H], 128)
-        V(tt(t("OHS" + H), p1[:, 0, :], t("ST" + H), A.mult), ["P1_%s0" % H, "ST" + H], ["OHS" + H], 128)
-        P(mms([(p1[:, 1, :], t("P15"), t("OHS" + H))]), ["P15", "OHS" + H], ["P1_%s1" % H], 128)
-        V(tt(t("TI" + H), t(W), p1[:, 1, :], A.mult), [W, "P1_%s1" % H], ["TI" + H], 128)
-        V(ts(t("GI" + H), t("TI" + H), 3, A.logical_shift_right, 4096, A.bitwise_and), ["TI" + H], ["GI" + H], 128)
-        V(tt(t("D2" + H), t("D1" + H), t("GI" + H), A.max), ["D1" + H, "GI" + H], ["D2" + H], 256)
-        V(ts(t("L2" + H), t("D2" + H), 1.0, A.subtract), ["D2" + H], ["L2" + H], 128)
+        LU, DW = "LU%d%d" % (h, vt), "DW%d%d" % (h, vt)
+        DF, W = "DF%d%d" % (h, vt), "W%d%d" % (h, vt)
+        K, M, B, x = T["K" + H], "M" + H, "B" + H, T["x1" + H]
+        kx = kx1[h] = gather("x1", LU, h, vt, X1 if vt else X1F)
+        V(ts(t(DW, 0, CH), t(LU), 1.0, A.add), [LU], [DF], 128)
+        S(act(t("WR" + H), t(DW, CH), AF.Identity, MAGIC), [W], ["WR" + H], 128)
+        if vt:
+            V(ts(t("F1" + H), t(LU), D - 0.5, A.is_lt), [LU], ["F1" + H], 64)
+        P([(T[M][:, 0:8], t("F1" + H), t("E1"))], ["F1" + H, "E1"], ["@%s:e" % M], 64)
+        S(act(t("FULL" + H), T[M][:, 0:8], AF.Relu, -15.0), ["@%s:e" % M], ["FULL" + H], 8)
+        kk, kill, kl = "@K%s:k" % H, T[M][:, 8:16], "@%s:kill" % M
+        P([(K[:, 0:128], t("F1" + H), t("DG"))], ["F1" + H, "DG"], [kk], 128, True, False)
+        P([(kill, t("ONESF"), t("THE")), (kill, t("NHUGE"), t("FULL" + H))], ["ONESF", "THE", "NHUGE", "FULL" + H], [kl], 320, True, False)
+        first = P([(K[:, m:128:16], x[:, m::16], t("E32")) for m in range(16)], ["E32"] + kx, [kk], 1024, False, True)
+        P([(kill, x[:, m::16], t("EBN")) for m in range(16)], ["EBN"] + kx, [kl], 1024, False, True, [first])
+        argmax(h, kill, kl)
+        if UR == "G":
+            P([(slot(M, 3), t("IDF"), t(DW, CH))], ["IDF", W], ["@%s:1" % M], 512, True, False)
+        else:
+            P([(T[M][:, 256:512], t("IDF"), t(DW)), (slot(M, 1), t("LT"), t("F1" + H))], ["IDF", DF, W, "LT", "F1" + H], ["@%s:1" % M], 1152, True, False)
+        P([(slot(B, 0), t("OHD" + H), t("IDENT"))], ["OHD" + H, "IDENT"], ["@%s:0" % B], 128)
+        S(act(t("OHS" + H), slot(B, 0), AF.Copy), ["@%s:0" % B], ["OHS" + H], 128)
+        V(tt(T["MBS" + H][:], slot(B, 0), t(DW, 0, CH), A.mult), ["@%s:0" % B, DF], ["MBS" + H], 128)
+        B = "K" + H
+        P([(slot(B, 0), t("P15"), t("OHS" + H))], ["P15", "OHS" + H], ["@%s:0" % B], 128)
+        if UR == "G":
+            V(tt(t("TI" + H), t(DW, CH), slot(B, 0), A.mult), [W, "@%s:0" % B], ["TI" + H], 128)
+            V(ts(t("GI" + H), t("TI" + H), 3, A.logical_shift_right, 4096, A.bitwise_and), ["TI" + H], ["GI" + H], 128)
+            V(tt(t("D2" + H), t(DW, 0, CH), t("GI" + H), A.max), [DF, "GI" + H], ["D2" + H], 256)
+            V(ts(t("L2" + H), t("D2" + H), 1.0, A.subtract, float(D), A.min), ["D2" + H], ["L2" + H], 128)
+            V(ts(t("KEEP" + H), t("L2" + H), D - 0.5, A.is_lt), ["L2" + H], ["KEEP" + H], 64)
+            return
+        V(tt(slot(B, 1), t(DW, CH), slot(B, 0), A.mult), [W, "@%s:0" % B], ["@%s:1" % B], 128)
+        V(ts(t("RR" + H), slot(B, 1), MAGIC, A.add, MAGIC, A.subtract), ["@%s:1" % B], ["RR" + H], 128)
+        V(tt(t("KEEP" + H), t("RR" + H), slot(B, 1), A.is_le), ["RR" + H, "@%s:1" % B], ["KEEP" + H], 128)
 
     def phase2(vt, h):
         H = str(h)
-        W = "W%d%d" % (h, vt)
-        p0, p1, p3 = T["P0_" + H], T["P1_" + H], T["P3_" + H]
-        x = T["x2" + H]
-        kx = gather("x2", "L2" + H, h, SHARE["x2"])
-        S(act(t("F2" + H), t("D2" + H), AF.Sign, 3456.5, -1.0), ["D2" + H], ["F2" + H], 128)
-        P(mms([(p1[:, 2, :], t("LT"), t("F2" + H))]), ["LT", "F2" + H], ["P1_%s2" % H], 128)
-        P(mms([(p1[:, 3, :], t("IDF"), t(W)), (p1[:, 3, :], t("IBIG"), t("F2" + H))]), ["IDF", W, "IBIG", "F2" + H], ["P1_%s3" % H], 640)
-        V(ts(t("OHE" + H), p1[:, 2, :], t("THR"), A.is_ge), ["P1_%s2" % H, "THR"], ["OHE" + H], 128)
-        S(act(t("NOE" + H), t("OHE" + H), AF.Identity, 1.0, -1.0), ["OHE" + H], ["NOE" + H], 128)
-        S(act(t("W2" + H), p1[:, 3, :], AF.Relu, -BIG), ["P1_%s3" % H], ["W2" + H], 128)
-        V(cp(t("A2" + H), t("W2" + H)), ["W2" + H], ["A2" + H], 128)
-        ku = sums(h, 2, x, "F2" + H, SHARE["x2"], kx)
-        S(act(t("U32" + H), p3[:, 2, :], AF.Identity, t("B135"), 16.0), ku + ["B135"], ["U32" + H], 128)
-        S(act(t("Y" + H), p3[:, 2, :], AF.Identity, MAGIC, 1 / 16), ku, ["Y" + H], 128)
-        P(mms([(p0[:, 0:128], t("U32" + H), t("IDF"))]), ["U32" + H, "IDF"], ["P0_" + H], 512)
-        S(act(t("VB" + H), t("Y" + H), AF.Identity, MAGIC + 256, -1.0), ["Y" + H], ["VB" + H], 128)
+        K, M, x, x2, keep = T["K" + H], "M" + H, T["x1" + H], T["x2" + H], t("KEEP" + H)
+
+        def mask(b):
+            bank = "BK"[b % 2] + H
+            key = "@%s:w" % bank
+            rows = [(T[bank][:, u::4], t("SEL", 128 * (4 * b + u), 128 * (4 * b + u + 1)), keep) for u in range(4)]
+            if UR[b] == "V":
+                P(rows, ["SEL%d" % b, "KEEP" + H], [key], 512, [True] * 4, [True] * 4)
+                V(tt(x2[:, b::4], x[:, b::4], T[bank][:], A.mult), kx1[h] + [key], ["x2%s:%d" % (H, b)], 512)
+            else:
+                P([(T[bank][:], t("I256"), x[:, b::4])] + rows, ["SEL%d" % b, "KEEP" + H, "I256"] + kx1[h], [key], 1024)
+                S(act(x2[:, b::4], T[bank][:], AF.Relu, -256.0, 256.0), [key], ["x2%s:%d" % (H, b)], 512)
+        if UR == "G":
+            kx2[h] = gather("x2", "L2" + H, h, vt, X2)
+            P([(slot(M, 3), t("IBIG"), keep)], ["IBIG", "KEEP" + H], ["@%s:1" % M], 128, False, True)
+            P([(slot(M, 1), t("LT"), keep)], ["LT", "KEEP" + H], ["@%s:2" % M], 128)
+            S(act(t("OHE" + H), slot(M, 1), AF.Relu, t("OHB")), ["@%s:2" % M, "OHB"], ["OHE" + H], 128)
+            S(act(t("W2" + H), slot(M, 3), AF.Relu, -BIG), ["@%s:1" % M], ["W2" + H], 128)
+            u, ku = slot("B" + H, 0), "@B%s:u" % H
+            P([(u, t("CONSTL"), t("K155"))], ["CONSTL", "K155"], [ku], 128, True, False)
+            pieces = sorted(zip(X2, kx2[h]), key=lambda x: x[0][2] - x[0][1])
+            for (e, a, b), key in pieces:
+                P([(T["B" + H][:, a:b], t("IDENT"), x2[:, 16 * a + m:16 * b:16]) for m in range(16)], ["IDENT", key], [ku], 16 * max(64, b - a),
+                  False, key == pieces[-1][1])
+        else:
+            kx2[h] = []
+            mask(0)
+            mask(1)
+            P([(slot(M, 1), t("LT"), keep), (slot(M, 2), t("N4K"), keep), (slot(M, 3), t("IBIG"), keep)],
+              ["LT", "N4K", "IBIG", "KEEP" + H], ["@%s:1" % M], 384, False, True)
+            S(act(t("OHE" + H), slot(M, 1), AF.Relu, t("OHB")), ["@%s:1" % M, "OHB"], ["OHE" + H], 128)
+            S(act(t("D2" + H), slot(M, 2), AF.Identity, 4096.0), ["@%s:1" % M], ["D2" + H], 128)
+            S(act(t("W2" + H), slot(M, 3), AF.Relu, -BIG), ["@%s:1" % M], ["W2" + H], 128)
+            mask(2)
+            mask(3)
+            u, ku = slot(M, 0), "@%s:0" % M
+            for b in range(4):
+                P([(u, t("CONSTL"), t("K155"))] * (b == 0) + [(u, t("IDENT"), x2[:, m::16]) for m in range(b, 16, 4)],
+                  ["CONSTL", "K155", "IDENT", "x2%s:%d" % (H, b)], [ku], 512 + 128 * (b == 0), b == 0, b == 3)
+        S(act(t("U32" + H), u, AF.Identity, t("B15"), 16.0), [ku, "B15"], ["U32" + H], 128)
+        S(act(t("Y" + H), u, AF.Identity, MAGIC, 1 / 16), [ku], ["Y" + H], 128)
+        P([(K[:, 0:128], t("U32" + H), t("IDF"))], ["U32" + H, "IDF"], ["@K%s:k" % H], 512)
+        S(act(t("VB" + H), t("Y" + H), AF.Identity, MAGIC + 255, -1.0), ["Y" + H], ["VB" + H], 128)
         argmax(h)
-        P(mms([(p3[:, 3, :], t("OHD" + H), t("IDENT"))]), ["OHD" + H, "IDENT"], ["P3_%s3" % H], 128)
 
     def phase3(vt, h):
         H = str(h)
-        p0, p1, p3 = T["P0_" + H], T["P1_" + H], T["P3_" + H]
-        x, z = T["x2" + H], T["z" + H]
-        kx = ["x2%d:%d" % (h, a) for e, a, b in SHARE["x2"]]
-        for q in range(2):
-            ms = range(8 * q, 8 * q + 8)
-
-            def kf(v, ms=ms):
-                for m in ms:
-                    r = v.tensor_tensor(z[:, m::16], x[:, m::16], p3[:, 3, :], A.mult)
-                return r
-            V(kf, kx + ["P3_%s3" % H], ["z%s:%d" % (H, q)], 8 * 128)
-
-            def yf(pe, q=q, ms=ms):
-                if q == 0:
-                    pe.matmul(p0[:, 0:128], t("CONSTL"), t("KC"), True, False)
-                for m in ms:
-                    r = pe.matmul(p0[:, m:128:16], z[:, m::16], t("E16"), False, m == 15)
-                return r
-            P(yf, ["CONSTL", "KC", "E16", "z%s:%d" % (H, q)], ["P0_" + H], 128 * (1 - q) + 8 * 64, q == 1)
+        DW = "DW%d%d" % (h, vt)
+        DF = "DF%d%d" % (h, vt)
+        K, M, B, x2, z = T["K" + H], "M" + H, "B" + H, T["x2" + H], T["z" + H]
+        kk = "@K%s:k" % H
+        P([(slot(B, 0), t("OHD" + H), t("IDENT"))], ["OHD" + H, "IDENT"], ["@%s:w" % B], 128)
+        if UR == "G":
+            P([(K[:, 0:128], t("KEEP" + H), t("DG"))], ["KEEP" + H, "DG"], [kk], 128, True, False)
+        else:
+            P([(K[:, 0:128], t("F1" + H), t("DG")), (K[:, 0:128], t("KEEP" + H), t("DG")), (K[:, 0:128], t("CONSTL"), t("KC2"))],
+              ["F1" + H, "KEEP" + H, "DG", "CONSTL", "KC2"], [kk], 384, True, False)
+        for b in range(4):
+            if ZR[b] == "V":
+                V(four(z, x2, b, slot(B, 0), A.mult), kx2[h] + ["@%s:w" % B], ["z%s:%d" % (H, b)], 512 + 3 * COST[0] / 0.83e-3)
+            else:
+                P([(slot(M, u), t("I256"), x2[:, 4 * u + b::16]) for u in range(4)], kx2[h] + ["I256"], ["@%s:w" % M], 512, True, False)
+                P([(slot(M, u), t("OHD" + H), t("IDENT")) for u in range(4)], ["OHD" + H, "IDENT"], ["@%s:w" % M], 512, False, True)
+                S(act(z[:, 512 * b:512 * b + 512], T[M][:], AF.Relu, -256.0, 256.0), ["@%s:w" % M], ["z%s:%d" % (H, b)], 512)
+        for b in range(4):
+            P([(K[:, m:128:16], row(z, m), t("E32")) for m in range(b, 16, 4)], ["E32", "z%s:%d" % (H, b)], [kk], 256, False, b == 3)
         argmax(h)
-        P(mms([(p1[:, 0, :], t("OHD" + H), t("IDENT"))]), ["OHD" + H, "IDENT"], ["P1_%s0" % H], 128)
-        V(tt(t("MBK" + H), p1[:, 0, :], t("D2" + H), A.mult), ["P1_%s0" % H, "D2" + H], ["MBK" + H], 128)
-        V(tt(t("MBA" + H), p1[:, 0, :], t("A2" + H), A.mult), ["P1_%s0" % H, "A2" + H], ["MBA" + H], 128)
-        S(act(t("OHK" + H), p1[:, 0, :], AF.Copy), ["P1_%s0" % H], ["OHK" + H], 128)
-        P(mms([(p1[:, 1, :], t("MBK" + H), t("BOF"))]), ["MBK" + H, "BOF"], ["P1_%s1" % H], 512)
-        V(tt(t("VM" + H), p1[:, 1, :], t("DQF"), A.mult), ["P1_%s1" % H, "DQF"], ["VM" + H], 128)
-        P(mms([(p1[:, 3, 0:8], t("VM" + H), t("SELC"))]), ["VM" + H, "SELC"], ["P1_%s3" % H], 256)
-        V(ts(t("LC" + H, 0, 8), p1[:, 3, 0:8], 1.0, A.subtract, 3455.0, A.min), ["P1_%s3" % H], ["LC" + H], 64)
+        P([(slot(M, 0), t("OHD" + H), t("IDENT"))], ["OHD" + H, "IDENT"], ["@%s:0" % M], 128)
+        V(tt(t("MBK" + H), slot(M, 0), t(DW, 0, CH), A.mult), ["@%s:0" % M, DF], ["MBK" + H], 128)
+        V(tt(t("MBA" + H), slot(M, 0), t("WR" + H), A.mult), ["@%s:0" % M, "WR" + H], ["MBA" + H], 128)
+        S(act(t("OHK" + H), slot(M, 0), AF.Copy), ["@%s:0" % M], ["OHK" + H], 128)
+        if "K" in ONS:
+            P([(slot(B, 0), t("IDENT"), t("NDQ"))], ["IDENT", "NDQ"], ["@%s:0" % B], 128, True, False)
+            P([(slot(B, 0), t("MBK" + H), t("BOF"))], ["MBK" + H, "BOF"], ["@%s:0" % B], 512, False, True)
+            S(act(t("VM" + H), slot(B, 0), AF.Relu), ["@%s:0" % B], ["VM" + H], 128)
+        else:
+            P([(slot(B, 0), t("MBK" + H), t("BOF"))], ["MBK" + H, "BOF"], ["@%s:0" % B], 512)
+            V(tt(t("VM" + H), slot(B, 0), t("DQF"), A.mult), ["@%s:0" % B, "DQF"], ["VM" + H], 128)
+        P([(T[B][:, 128:136], t("VM" + H), t("SELC"))], ["VM" + H, "SELC"], ["@%s:1" % B], 256)
+        V(ts(t("LC" + H, 0, 8), T[B][:, 128:136], 1.0, A.subtract, D - 1.0, A.min), ["@%s:1" % B], ["LC" + H], 64)
         V(cp(t("CU" + H), T.R[:].indirect(t("LC" + H, 0, 8))), ["Ra", "Rb", "LC" + H], ["CU" + H], 200)
 
     def phase4(vt, h):
         H = str(h)
-        p0, p1, p3 = T["P0_" + H], T["P1_" + H], T["P3_" + H]
-        xc, ax = T["xc" + H], T["ax" + H]
-        kx = gather("xc", "CU" + H, h, SHARE["xc"])
-        V(ts(t("CF" + H), t("CU" + H), 1.0, A.add), ["CU" + H], ["CF" + H], 128)
-        P(mms([(p1[:, 2, :], t("BOF"), t("MBA" + H)), (p1[:, 2, :], t("M64"), t("OHK" + H)), (p1[:, 2, :], t("P2"), t("OHE" + H)),
-               (p1[:, 2, :], t("INEG"), t("NOE" + H))]),
-          ["BOF", "MBA" + H, "M64", "OHK" + H, "P2", "OHE" + H, "INEG", "NOE" + H], ["P1_%s2" % H], 896)
+        K, M, B, xc, ax = T["K" + H], "M" + H, "B" + H, T["xc" + H], T["ax" + H]
+        kk, SW, vb = "@K%s:k" % H, "SW%d%d" % (h, vt + 1), t("VB" + H)
         last = vt == NV - 1
-        WN = ("SW%d%d" % (h, vt + 1)) if not last else "W2" + H
-        V(tt(t(WN), t("W2" + H), p1[:, 2, :], A.max), ["W2" + H, "P1_%s2" % H], [WN], 128)
-        if not last:
-            send(WN, "W%d%d" % (h, vt + 1), 6 * h + 2 * vt)
-        ks = P(mms([(p0[:, 0:128], t("CONSTL"), t("KS"))], True, False), ["CONSTL", "KS"], ["P0_" + H], 128)
-        def mf(v):
-            for j in range(12, 16):
-                r = v.tensor_tensor(ax[:, j, :], xc[:, j::16], t("VB" + H), A.max)
-            return r
-        V(mf, kx + ["VB" + H], ["ax%s:3" % H], 1024)
-
-        def lf(pe):
-            for j in range(12, 16):
-                pe.matmul(p0[:, j:128:16], xc[:, j::16], t("E16"), False, False)
-                r = pe.matmul(p0[:, j:128:16], t("VB" + H), t("E16"), False, False)
-            return r
-        parts = [P(lf, ["E16", "VB" + H] + kx, ["P0_%s#l" % H], 512, True, [ks])]
-
-        def gf(pe):
-            for j in range(12, 16):
-                r = pe.matmul(p0[:, j:128:16], ax[:, j, :], t("E32N"), False, False)
-            return r
-        parts.append(P(gf, ["E32N", "ax%s:3" % H], ["P0_%s#g" % H], 256, True, [ks]))
-        for b in range(3):
-            pb, kb = (p3, "P3_%s" % H) if b % 2 == 0 else (p1, "P1_%s" % H)
-
-            def df(pe, b=b, pb=pb):
-                for u in range(4):
-                    pe.matmul(pb[:, u, :], t("IDENT"), xc[:, 4 * b + u::16], True, False)
-                    r = pe.matmul(pb[:, u, :], t("NID"), t("VB" + H), False, True)
-                return r
-            P(df, ["IDENT", "NID", "VB" + H] + kx, [kb + str(u) for u in range(4)], 1024)
-            S(act(ax[:, 4 * b:4 * b + 4, :], pb[:, :, :], AF.Abs), [kb + str(u) for u in range(4)], ["ax%s:%d" % (H, b)], 512)
-
-            def sf(pe, b=b):
-                for j in range(4 * b, 4 * b + 4):
-                    r = pe.matmul(p0[:, j:128:16], ax[:, j, :], t("E16N"), False, j == 11)
-                return r
-            parts.append(P(sf, ["E16N", "ax%s:%d" % (H, b)], ["P0_%s#%d" % (H, b) if b < 2 else "P0_" + H], 256, True, [ks] if b < 2 else parts))
-        argmax(h)
-        P(mms([(p1[:, 0, :], t("OHD" + H), t("IDENT"))]), ["OHD" + H, "IDENT"], ["P1_%s0" % H], 128)
-        V(tt(t("MB2" + H), p1[:, 0, :], t("CF" + H), A.mult), ["P1_%s0" % H, "CF" + H], ["MB2" + H], 128)
-        P(mms([(p1[:, 1, :], t("I8P"), t("NOE" + H))], True, False), ["I8P", "NOE" + H], ["P1_%s1" % H], 128)
-        P(mms([(p1[:, 1, :], t("BOF"), t("MB2" + H))], False, True), ["BOF", "MB2" + H], ["P1_%s1" % H], 512, True)
-        V(tt(t("D3" + H), t("D2" + H), p1[:, 1, :], A.min), ["D2" + H, "P1_%s1" % H], ["D3" + H], 128)
-        if not last:
-            LN = "SLU%d%d" % (h, vt + 1)
-            V(ts(t(LN), t("D3" + H), 1.0, A.subtract), ["D3" + H], [LN], 128)
-            send(LN, "LU%d%d" % (h, vt + 1), 6 * h + 2 * vt + 1)
+        kx = gather("xc", "CU" + H, h, vt, XC)
+        if "C" in ONS:
+            S(act(t("CF" + H), T.R[:].indirect(t("LC" + H, 0, 8)), AF.Identity, 1.0), ["Ra", "Rb", "LC" + H], ["CF" + H], 200)
         else:
-            V(ts(t("YP" + H), t("D3" + H), 1.0, A.subtract, 3456.0, A.min), ["D3" + H], ["YP" + H], 128)
-            dma("Y", T.yp[:, h * CH:h * CH + CH], t("YP" + H), ["YP" + H], [], 2.5)
-            V(cp(t("A2" + H), t("W2" + H)), ["W2" + H], ["A2" + H], 128)
-            V(tt(t("YQ" + H), t("W2" + H), t("A2" + H), A.subtract), ["W2" + H, "A2" + H], ["YQ" + H], 256)
-            V(ts(t("YR" + H), t("YQ" + H), 64.0, A.mult), ["YQ" + H], ["YR" + H], 128)
+            V(ts(t("CF" + H), t("CU" + H), 1.0, A.add), ["CU" + H], ["CF" + H], 128)
+        o = slot(M, 3)
+        P([(o, t("BOF"), t("MBA" + H)), (o, t("NBIG"), t("OHK" + H)), (o, t("IBIG"), t("OHE" + H)), (o, t("D2M"), t("OHE" + H)), (o, t("M64"), t("OHK" + H))],
+          ["BOF", "MBA" + H, "D2M", "OHE" + H, "IBIG", "NBIG", "OHK" + H, "M64"], ["@%s:3" % M], 1024)
+        V(tt(t(SW), t("W2" + H), o, A.max), ["W2" + H, "@%s:3" % M], [SW], 128)
+        if not last:
+            send(t(SW), t("DW%d%d" % (h, vt + 1), CH), SW, "W%d%d" % (h, vt + 1), 6 * h + 2 * vt + 1, COST[4])
+        else:
+            V(ts(t("YM" + H), t(SW), MAGIC, A.add, MAGIC, A.subtract), [SW], ["YM" + H], 128)
+            V(tt(t("YQ" + H), t(SW), t("YM" + H), A.subtract), ["YM" + H, SW], ["YQ" + H], 256)
+            S(act(t("YR" + H), t("YQ" + H), AF.Relu, -1.0, 64.0), ["YQ" + H], ["YR" + H], 128)
             dma("Y", T.yq[:, h * CH:h * CH + CH], t("YR" + H), ["YR" + H], [], 2.5)
+        P([(K[:, 0:128], t("CONSTL"), t("KS"))] + [(K[:, b:128:4], vb, t("E164")) for b in range(4) if AR[b] == "V"],
+          ["CONSTL", "KS", "VB" + H, "E164"], [kk], 128 + 64 * AR.count("V"), True, False)
+        if "V" in AR:
+            P([(slot(B, 0), t("IDENT"), vb)], ["IDENT", "VB" + H], ["@%s:w" % B], 128)
+        sbank = [M, M] if "V" in AR else [M, B]
+        for b in range(4):
+            ka = "ax%s:%d" % (H, b)
+            if AR[b] == "V":
+                V(four(ax, xc, b, slot(B, 0), A.max), kx + ["@%s:w" % B], [ka], 512 + 3 * COST[0] / 0.83e-3)
+            else:
+                bank = sbank[b % 2]
+                P([(slot(bank, u), t("NID"), vb) for u in range(4)], ["NID", "VB" + H], ["@%s:w" % bank], 512, True, False)
+                P([(slot(bank, u), t("IDENT"), xc[:, 4 * u + b::16]) for u in range(4)], ["IDENT"] + kx, ["@%s:w" % bank], 512, False, True)
+                S(act(ax[:, 512 * b:512 * b + 512], T[bank][:], AF.Abs), ["@%s:w" % bank], [ka], 512)
+        vs = [j for j in range(16) if AR[j % 4] == "V"]
+        if vs:
+            P([(K[:, j:128:16], xc[:, j::16], t("E16")) for j in vs], ["E16"] + kx, [kk], 64 * len(vs), False, False)
+        for b in range(4):
+            P([(K[:, j:128:16], row(ax, j), t("E32N" if AR[b] == "V" else "E16N")) for j in range(b, 16, 4)],
+              ["E32N", "E16N", "ax%s:%d" % (H, b)], [kk], 256, False, b == 3)
+        o = slot(B, 1)
+        P([(o, t("BO8K"), t("OHK" + H)), (o, t("N8K"), t("OHE" + H))], ["BO8K", "N8K", "OHK" + H, "OHE" + H], ["@%s:1" % B], 256, True, False)
+        argmax(h)
+        P([(slot(M, 0), t("OHD" + H), t("IDENT"))], ["OHD" + H, "IDENT"], ["@%s:0" % M], 128)
+        V(tt(t("MB2" + H), slot(M, 0), t("CF" + H), A.mult), ["@%s:0" % M, "CF" + H], ["MB2" + H], 128)
+        P([(o, t("BOF"), t("MB2" + H))], ["BOF", "MB2" + H], ["@%s:1" % B], 512, False, True)
+        V(tt(t("D3" + H), t("D2" + H), o, A.min), ["D2" + H, "@%s:1" % B], ["D3" + H], 128)
+        if not last:
+            LN, LU = "SLU%d%d" % (h, vt + 1), "LU%d%d" % (h, vt + 1)
+            V(ts(t(LN), t("D3" + H), 1.0, A.subtract, float(D), A.min), ["D3" + H], [LN], 128)
+            send(t(LN), t(LU), LN, LU, 6 * h + 2 * vt, COST[3])
+        else:
+            V(ts(t("YP" + H), t("D3" + H), 1.0, A.subtract, float(D), A.min), ["D3" + H], ["YP" + H], 128)
+            dma("Y", T.yp[:, h * CH:h * CH + CH], t("YP" + H), ["YP" + H], [], 2.5)
 
-    def send(src, dst, k):
+    def send(src, dst, rd, wr, k, lat):
         mask, n = topo.mask(core, nxt), len(topo.engines(core, nxt))
         rid, pid = topo.addr(nxt)[:2]
-        o = add("G", lambda: g.remote_dma(t(dst), t(src), T.sem["r%d" % k], T.sem["l%d" % k], pid, rid, mask), [src], [], 1.0,
+        o = add("G", lambda: g.remote_dma(dst, src, T.sem["r%d" % k], T.sem["l%d" % k], pid, rid, mask), [rd], ["sent:" + rd], 1.0, hold=0.6,
                 sem="l%d" % k, need=n, comp=False)
-        add("N", None, [], [dst], 2.5, sem="r%d" % k, need=len(topo.engines(prv, core)), extra=[o], comp=False)
+        add("N", None, [], [wr], lat, sem="r%d" % k, need=len(topo.engines(prv, core)), extra=[o], comp=False)
 
-    def dedup(vt, h):
+    def pairs(vt, h):
         H = str(h)
-        q2 = "P2_" + H
-        p2 = T[q2]
-        P(mms([(p2[:, 3, :], t("IDENT"), t("OHS" + H))]), ["IDENT", "OHS" + H], [q2 + "3"], 128)
-        V(tt(t("MBH" + H), p2[:, 3, :], t("DHI" + H), A.mult), [q2 + "3", "DHI" + H], ["MBH" + H], 128)
-        V(tt(t("MBL" + H), p2[:, 3, :], t("DLO" + H), A.mult), [q2 + "3", "DLO" + H], ["MBL" + H], 128)
-        P(mms([(p2[:, 1, :], t("ZA"), t("MBH" + H)), (p2[:, 1, :], t("ZB"), t("MBL" + H)), (p2[:, 1, :], t("ZC"), t("PNUM"))]),
-          ["MBH" + H, "MBL" + H, "ZA", "ZB", "ZC", "PNUM"], [q2 + "1"], 384)
-        S(act(t("Z" + H), p2[:, 1, :], AF.Copy), [q2 + "1"], ["Z" + H], 128)
-        P(mms([(p2[:, 0, :], t("Z" + H), t("BO01"))]), ["Z" + H, "BO01"], [q2 + "0"], 128)
-        P(mms([(p2[:, 2, :], t("ONE16"), t("ST" + H))]), ["ONE16", "ST" + H], [q2 + "2"], 128)
-        V(tt(t("VMD" + H), p2[:, 0, :], t("DQF"), A.mult), [q2 + "0", "DQF"], ["VMD" + H], 128)
-        if vt < NV - 1:
-            S(lambda s: s.activation(t("AA" + H), p2[:, 2, :], AF.Copy, accum_out=t("CNT", h, h + 1)), [q2 + "2"], ["AA" + H, "CNT" + H], 160)
-        P(mms([(p2[:, 1, 0:8], t("VMD" + H), t("SELC"))]), ["VMD" + H, "SELC"], [q2 + "1"], 256)
-        V(cp(t("DC", 8 * h, 8 * h + 8), p2[:, 1, 0:8]), [q2 + "1"], ["DC" + H], 64)
-        for w in range(8):
-            b = q2
-            o = T[b][:, w % 4, :]
-            sp, sn = t("SELP", w * 128, w * 128 + 128), t("SELN", w * 128, w * 128 + 128)
-            P(mms([(o, sp, t("Z" + H)), (o, t("Z" + H), sn)]), ["SELP", "SELN", "Z" + H], [b + str(w % 4)], 256)
-            if w % 4 == 3:
-                for u in range(w - 3, w + 1):
-                    V((lambda u, b: lambda v: v.tensor_reduce(t("RED" + H, u, u + 1), T[b][:, u % 4, :], AxisListType.X, A.min,
-                                                              apply_absolute_value=True))(u, b), [b + str(u % 4)], ["RED%s%d" % (H, u)], 128)
-        for w in range(8):
-            S(act(t("VMW" + H, 16 * w, 16 * w + 16), t("DQ", 0, 16), AF.Copy, 0.0, t("RED" + H, w, w + 1)), ["DQ", "RED%s%d" % (H, w)], ["VMW%s%d" % (H, w)], 16)
-        S(act(t("TM" + H), t("T32" + H), AF.Identity, MAGIC, 1 / 16), ["T32" + H], ["TM" + H], 128)
-        S(act(t("TFB" + H), t("TM" + H), AF.Identity, -MAGIC, 1.0), ["TM" + H], ["TFB" + H], 128)
+        x, mbs, dd = T["x1" + H], T["MBS" + H], T.S5
+        if h == 0:
+            P([(T.TB[:, 0:256], t("CONSTL"), t("K775"))], ["CONSTL", "K775"], ["@TB:t"], 256, True, False)
+        for b in range(4):
+            P([(slot("TB", h), t("IDENT"), x[:, m::16]) for m in range(b, 16, 4)], ["IDENT"] + kx1[h], ["@TB:t"], 512, False, False)
+        P([(slot("S5", 2 * h), t("IDENT"), t("NDQ"))] * ("5" in ONS) + [(slot("S5", 2 * h), mbs[:], t("BOF"))], ["MBS" + H, "BOF", "IDENT", "NDQ"],
+          ["@S5:c" + H], 512 + 128 * ("5" in ONS))
+        if "5" in ONS:
+            S(act(t("VMS" + H), slot("S5", 2 * h), AF.Relu), ["@S5:c" + H], ["VMS" + H], 128)
+        else:
+            V(tt(t("VMS" + H), slot("S5", 2 * h), t("DQF"), A.mult), ["@S5:c" + H, "DQF"], ["VMS" + H], 128)
+        r = slice(4 * h, 4 * h + 4)
+        P([(dd[:, r, 0:50], t("VMS" + H), T.NB50[:]), (dd[:, r, 0:50], t("IDENT"), T.TRI50[:]), (dd[:, r, 0:16], t("BOF"), mbs[:, :, 0:16]),
+           (dd[:, r, 17:33], t("BOF"), mbs[:, :, 16:32]), (dd[:, r, 33:49], t("BOF"), mbs[:, :, 0:16])],
+          ["VMS" + H, "IDENT", "TRI50", "BOF", "MBS" + H] + NB, ["@S5:d" + H], 1768)
 
     def update(vt):
-        pa, pb = T.P2_0, T.P2_1
-        for h in range(2):
-            H = str(h)
-            P(mms([(pa[:, 3, 8 * h:8 * h + 8], t("VMW" + H), t("BO", 0, 128, 16)), (pa[:, 3, 8 * h:8 * h + 8], t("CONSTL"), t("K63"))]),
-              ["VMW%s%d" % (H, w) for w in range(8)] + ["BO", "CONSTL", "K63"], ["P2_03%d" % h], 128)
-        V(ts(t("GL"), t("DC"), 1.0, A.subtract), ["DC0", "DC1"], ["GL"], 64)
-        S(act(t("XS"), XALL.indirect(t("GL")), AF.Copy), XK + ["GL"], ["XS"], 400)
-        for h in range(2):
-            H = str(h)
-            P(mms([(pb[:, h, :], t("IDENT"), t("XS", 128 * h, 128 * h + 128)), (pb[:, h, :], t("IDENT"), t("TFB" + H))]),
-              ["IDENT", "XS", "TFB" + H], ["P2_1%d" % h], 256)
-        V(ts(t("XN"), pb[:, 0:2, :], 0.5, A.mult, 0.25 if vt < NV - 1 else -0.75, A.add), ["P2_10", "P2_11"], ["XN"], 256)
-        V(tt(t("WM"), pa[:, 3, 0:16], t("DC"), A.min), ["P2_030", "P2_031", "DC0", "DC1"], ["WM"], 64)
-        V(ts(t("LL"), t("WM"), 0.5, A.is_lt), ["WM"], ["LL"], 64)
-        V(tt(t("TT"), t("LL"), t("DUM"), A.mult), ["LL", "DUM"], ["TT"], 64)
-        V(tt(t("OFF"), t("TT"), t("DC"), A.max), ["TT", "DC0", "DC1"], ["OFF"], 64)
-        V(ts(t("SL"), t("OFF"), 1.0, A.subtract), ["OFF"], ["SL"], 64)
+        dc, kd = T.S5[:, :, 16:50:33], ["@S5:d0", "@S5:d1"]
+        S(act(t("AB"), T.S5[:, :, 0:50], AF.Abs), kd, ["AB"], 400)
         if vt < NV - 1:
-            V(tt(t("CI"), t("CNT", 0, 1), t("CNT", 1, 2), A.add), ["CNT0", "CNT1"], ["CI"], 64)
+            S(lambda s: s.activation(t("JUNK"), dc, AF.Sign, accum_out=t("CNT")), kd, ["JUNK", "CNT"], 40)
+        V(scan(t("SCN"), t("MASK5"), t("AB"), A.add, A.min), ["MASK5", "AB"], ["SCN"], 200)
+        for b in range(2):
+            V(ts(t("LL", b, 16, 2), t("SCN", 16 + 33 * b, 400, 50), 0.5, A.is_lt, t("DUM", b, b + 1), A.mult), ["SCN", "DUM%d" % b], ["LL%d" % b], 64)
+        V(tt(t("OFF"), t("LL"), dc, A.max), ["LL0", "LL1"] + kd, ["OFF"], 64)
+        V(ts(t("SL"), t("OFF"), 1.0, A.subtract), ["OFF"], ["SL"], 64)
+        S(act(t("XS"), T["X%d" % vt][:].indirect(t("SL")), AF.Copy), XK[vt] + ["SL"], ["XS"], 400)
+        P([(T.TB[:, 0:256], t("I16"), t("XS"))], ["I16", "XS"], ["@TB:t"], 256, False, True)
+        if "X" in ONS:
+            S(act(t("XM"), T.TB[:, 0:256], AF.Identity, MAGIC, 1 / 32), ["@TB:t"], ["XM"], 256)
+            S(act(t("XB"), t("XM"), AF.Identity, -MAGIC), ["XM"], ["XN"], 256)
+        else:
+            V(ts(t("XN"), T.TB[:, 0:256], 1 / 32, A.mult), ["@TB:t"], ["XN"], 256)
+        if vt < NV - 1:
+            P([(T.S5[:, 0, 56:57], t("ONESF"), t("CNT"))], ["ONESF", "CNT"], ["@S5:n"], 256)
+            V(cp(t("CI"), T.S5[:, 0, 56:57]), ["@S5:n"], ["CI"], 64)
             V(ts(t("CI2"), t("CI"), 255, A.bitwise_and), ["CI"], ["CI2"], 64)
-            V(ts(t("THETA"), t("CI2"), t("LIMF"), A.add, 120.0, A.subtract), ["CI2", "LIMF"], ["THETA"], 64)
-        dst, keys = (T.X[:], XK) if vt < NV - 1 else (T.Y[:], ["Y%d" % k for k in range(NP)] + ["Yz"])
-        for h in (1, 0):
-            V(cp(dst.indirect(t("SL", 8 * h, 8 * h + 8)), t("XN", 128 * h, 128 * h + 128)), ["SL", "XN"], keys, 128 * 3)
+            V(ts(t("TH"), t("CI2"), t("LIMF"), A.add, BIG / 16, A.mult), ["CI2", "LIMF"], ["TH"], 64)
+            V(ts(t("THE"), t("SELC"), t("TH"), A.mult), ["SELC", "TH"], ["THE"], 64)
+        for r in range(7, -1, -1):
+            V(cp(T["X%d" % (vt + 1)][:].indirect(t("SL", 2 * r, 2 * r + 2)), t("XB" if "X" in ONS else "XN", 32 * r, 32 * r + 32)),
+              ["SL", "XN"], XK[vt + 1], 32 * 3.8)
 
     for vt in range(NV):
-        if vt == NV - 1:
-            V(lambda v: v.memset(T.Y[:, D:], 0.0), [], ["Yz"], 456)
-            for k in range(NP):
-                S(act(T.Y[:, k * PW:(k + 1) * PW], T.X[:, k * PW:(k + 1) * PW], AF.Identity, -1.0, 1.0), XK, ["Y%d" % k], PW)
-        for ph in (phase1, phase2, phase3):
-            for h in range(2):
-                now[0] = BONUS[2 * (phase1, phase2, phase3).index(ph) + h]
-                ph(vt, h)
-        now[0] = BONUS[8]
-        if vt == NV - 1:
-            for h in range(2):
-                dedup(vt, h)
-            update(vt)
-            for k in range(NP):
-                dma("Y", T.yx[:, k * PW:(k + 1) * PW], T.Y[:, k * PW:(k + 1) * PW], ["Y%d" % k], [], 4.0)
+        now[0] = 0.0
+        dma("Y", T["X%d" % (vt + 1)][:], T["X%d" % vt][:], XK[vt] + ["sent:SLU%d%d" % (h, vt) for h in range(2)], XK[vt + 1], 2.0 + 9 * DM)
         for h in range(2):
-            now[0] = BONUS[6 + h]
-            phase4(vt, h)
+            now[0] = BONUS[h]
+            phase1(vt, h)
         now[0] = BONUS[8]
-        if vt < NV - 1:
+        for h in range(2):
+            pairs(vt, h)
+        update(vt)
+        if vt == NV - 1:
+            for k in range(NP):
+                dma("Y", T.yx[:, k * PW:(k + 1) * PW], T["X%d" % NV][:, k * PW:(k + 1) * PW], XK[NV], [], 2.0 + DM * 2.2 * (k + 1))
+        for ph in (phase2, phase3, phase4):
             for h in range(2):
-                dedup(vt, h)
-            update(vt)
+                now[0] = BONUS[2 * (phase1, phase2, phase3, phase4).index(ph) + h]
+                ph(vt, h)
 
-    emit(g, T, ops, schedule(ops), QUEUE)
+    if rank == 0 or "order" not in INFO:
+        INFO["order"] = schedule(ops)
+    emit(g, T, ops, INFO["order"], QUEUE)
 
 
-WAKE, LOOK, IDLE = 0.12, 0.06, 0.0
+WAKE, PASSES, LOOK, GAP, MARGIN = 0.14, 3, 0.06, 0.2, 1.5
+COST = [0.005, 0.01, 0.45e-3, 2.4, 3.3]
+LEAD = 3.0
+DM = 0.6
+INFO = {}
 
 
 def schedule(ops):
@@ -569,39 +609,87 @@ def schedule(ops):
             succ[d].append(k)
     tail = [0.0] * n
     for k in range(n - 1, -1, -1):
-        tail[k] = ops[k]["cost"] + max([tail[s] + WAKE for s in succ[k]] + [0.0])
+        o = ops[k]
+        tail[k] = max([tail[s] + (o["cost"] + WAKE if ops[s]["deps"][k] == "wait" else o["cost"] if ops[s]["phys"] == "N" else o["hold"])
+                       for s in succ[k]] + [o["cost"] + (LEAD if o["name"] == "YP0" else 0.0)])
+    INFO.update(tail=list(tail), succ=succ, ops=ops)
     for k in range(n):
         tail[k] += ops[k]["bonus"]
-    left = [len(o["deps"]) for o in ops]
-    fin, free, order = [0.0] * n, {}, []
-    ready = {}
-    for k in range(n):
-        if left[k] == 0:
-            ready.setdefault(ops[k]["phys"], {})[k] = 0.0
-    while ready:
-        best = None
-        for e, lst in ready.items():
-            f = free.get(e, 0.0)
-            t0 = max(f, min(lst.values()))
-            if best is None or t0 < best[0]:
-                best = (t0, e)
-        t0, e = best
-        lst = ready[e]
-        k = max((tail[k] - IDLE * max(0.0, r - t0), -k) for k, r in lst.items() if r <= t0 + LOOK)[1] * -1
-        st = max(free.get(e, 0.0), lst.pop(k))
-        if not lst:
-            del ready[e]
-        o = ops[k]
-        fin[k] = st + o["cost"]
-        if e != "N":
-            free[e] = st + (o["cost"] if o["comp"] else (0.1 if o["eng"] != "G" else 1.0))
-        order.append(k)
-        for s in succ[k]:
-            left[s] -= 1
-            if left[s] == 0:
-                ready.setdefault(ops[s]["phys"], {})[s] = max([fin[d] + (WAKE if ops[s]["deps"][d] == "wait" else 0.0) for d in ops[s]["deps"]])
-    ops[0]["makespan"] = max(fin)
-    ops[0]["fin"] = dict(enumerate(fin))
+    hold = [0.0 if o["phys"] == "N" else o["hold"] for o in ops]
+    lag = [{d: ops[d]["cost"] + WAKE if w == "wait" else ops[d]["cost"] if o["phys"] == "N" else hold[d] for d, w in o["deps"].items()} for o in ops]
+    back = [{s: hold[s] + lag[s][k] - hold[k] for s in succ[k]} for k in range(n)]
+
+    def place(pri, pre, post, first):
+        left, at, busy = [len(p) for p in pre], [0.0] * n, {}
+        ready = set(k for k in range(n) if left[k] == 0)
+        while ready:
+            k = max(ready, key=lambda x: (pri[x], -x))
+            ready.remove(k)
+            t0 = max([first[k]] + [at[d] + x for d, x in pre[k].items()])
+            if hold[k]:
+                lst = busy.setdefault(ops[k]["phys"], [])
+                i = len(lst)
+                while i and lst[i - 1][1] > t0:
+                    i -= 1
+                while i < len(lst) and lst[i][0] < t0 + hold[k] - 1e-9:
+                    t0 = max(t0, lst[i][1])
+                    i += 1
+                lst.insert(i, (t0, t0 + hold[k]))
+            at[k] = t0
+            for s in post[k]:
+                left[s] -= 1
+                if left[s] == 0:
+                    ready.add(s)
+        return at
+
+    def greedy(pri):
+        left, at, free, ready = [len(p) for p in lag], [0.0] * n, {}, {}
+        for k in range(n):
+            if left[k] == 0:
+                ready.setdefault(ops[k]["phys"], {})[k] = 0.0
+        while ready:
+            t0, e = min((max(free.get(e, 0.0), min(lst.values())), e) for e, lst in ready.items())
+            lst = ready[e]
+            k = max((pri[k], -k) for k, r in lst.items() if r <= t0 + LOOK)[1] * -1
+            soon = [u for u, r in lst.items() if r < t0 + hold[k] - GAP and pri[u] > pri[k] + MARGIN]
+            if soon:
+                u = min(soon, key=lambda x: (lst[x], x))
+                fit = [c for c, r in lst.items() if max(r, t0) + hold[c] <= lst[u] + GAP]
+                k = max(fit, key=lambda x: (pri[x], -x)) if fit else u
+            at[k] = max(free.get(e, 0.0), lst.pop(k))
+            if not lst:
+                del ready[e]
+            if e != "N":
+                free[e] = at[k] + hold[k]
+            for s in succ[k]:
+                left[s] -= 1
+                if left[s] == 0:
+                    ready.setdefault(ops[s]["phys"], {})[s] = max(at[d] + x for d, x in lag[s].items())
+        return at
+
+    at = greedy(tail)
+    best, pri = (max(at[k] + ops[k]["cost"] for k in range(n)), at), tail
+    for it in range(PASSES):
+        at = greedy(pri)
+        span = max(at[k] + ops[k]["cost"] for k in range(n))
+        if best is None or span < best[0]:
+            best = (span, at)
+        rv = place([at[k] + hold[k] for k in range(n)], back, lag, [ops[k]["cost"] - hold[k] for k in range(n)])
+        pri = [rv[k] + hold[k] for k in range(n)]
+    INFO.update(span=best[0], at=best[1], lag=lag, hold=hold)
+    order, done = [], [False] * n
+    for k in sorted(range(n), key=lambda x: (best[1][x], x)):
+        todo = [k]
+        while todo:
+            x = todo[-1]
+            rest = [d for d in lag[x] if not done[d]]
+            if rest:
+                todo.append(rest[0])
+            else:
+                todo.pop()
+                if not done[x]:
+                    done[x] = True
+                    order.append(x)
     return order
 
 

from concourse.mybir import dt, AluOpType, AxisListType, ActivationFunctionType

A = AluOpType
AF = ActivationFunctionType
N, D, NV, CH = 4, 3456, 4, 128
PAD = 3472
XW = PAD + 32
MAGIC = 12582912.0
BIG = 131072.0
KK = 4194304.0
NP = 4
PW = D // NP
X1 = (("S", 0, 76), ("V", 76, 128))
X1F = (("S", 0, 64), ("V", 64, 128))
XC = (("S", 0, 76), ("V", 76, 128))
X2 = (("S", 0, 64), ("V", 64, 128))
ONS = "CX5"
UR = "G"
ZR = "SVVV"
AR = "SVSV"
BONUS = [0] * 10

POOLS = {"float32": ("pf", 4), "bfloat16": ("pb", 2), "int32": ("pi", 4), "uint16": ("pu", 2)}
TILES, SIZE = {}, {"float32": 0, "bfloat16": 0, "int32": 0, "uint16": 0}


def tile(name, dtype, cols):
    per = 32 // POOLS[dtype][1]
    TILES[name] = (POOLS[dtype][0], SIZE[dtype], cols)
    SIZE[dtype] += -(-cols // per) * per


for _n in ("ONES", "IDENT", "BO", "CONSTL", "KS", "KC2", "K155", "LT", "P15", "M64", "BO8K", "N8K", "N4K", "IBIG", "NBIG", "D2M", "DPB",
           "NID", "I16", "I256", "NHUGE"):
    tile(_n, "bfloat16", 128)
for _n, _c in (("DG", 128), ("FULL0", 8), ("FULL1", 8), ("E1", 8), ("E16", 8), ("E16N", 8), ("E32", 8), ("E32N", 8), ("EBN", 8), ("E164", 32), ("SEL", 2048), ("ZERO", 16), ("XS", 256), ("XB", 256), ("K775", 256), ("NDQ", 128),
               ("AB", 400), ("MASK5", 400), ("SCN", 400), ("JUNK", 16)):
    tile(_n, "bfloat16", _c)
for _n, _c in (("BOF", 128), ("MASK", 128), ("MASKF", 144), ("IDF", 128), ("DQF", 128), ("ONESF", 128), ("SELC", 8), ("THE", 8), ("DUM", 16),
               ("MCOL", 1), ("M64C", 1), ("DGC", 1), ("OHB", 1), ("B15", 1), ("PC15", 1), ("PC2", 1), ("LIMF", 1), ("TH", 1), ("CNT", 1),
               ("RJ", 2048), ("QROW", 128), ("MB1", 1), ("PB1", 1), ("JB", 16), ("LL", 16), ("TT", 16), ("OFF", 16), ("POW", 16), ("TWO", 16),
               ("SGN", 50), ("FN", 256), ("VI", 256), ("VV", 256), ("T1", 256), ("XM", 256)):
    tile(_n, "float32", _c)
for _n, _c in (("MI", 1), ("MI2", 1), ("LIMI", 1), ("CI", 1), ("CI2", 1), ("DI", 256), ("WI", 256), ("XN", 256)):
    tile(_n, "int32", _c)
tile("SL", "uint16", 16)
for _h in range(2):
    for _n in ("F1", "OHS", "KEEP", "OHE", "OHK", "OHD", "VB", "SG"):
        tile(_n + str(_h), "bfloat16", CH)
    for _n in ("SC", "SCA", "RR", "D2", "U32", "Y", "W2", "MBK", "VM", "VMS", "MBA", "CF", "MB2", "D3", "WR", "YM", "YP", "YQ", "YR"):
        tile(_n + str(_h), "float32", CH)
    tile("CU" + str(_h), "uint16", CH)
    tile("L2" + str(_h), "uint16", CH)
    tile("TI" + str(_h), "int32", CH)
    tile("GI" + str(_h), "int32", CH)
    tile("LC" + str(_h), "uint16", 16)
    for _t in range(NV):
        tile("LU%d%d" % (_h, _t), "uint16", CH)
        tile("DW%d%d" % (_h, _t), "float32", 2 * CH)
    for _t in range(1, NV + 1):
        tile("SLU%d%d" % (_h, _t), "uint16", CH)
        tile("SW%d%d" % (_h, _t), "float32", CH)

SCRATCH = {"R": ("sbuf", [128, D], "int32"), "NB50": ("sbuf", [128, 4, 50], "float32"),
           "TRI50": ("sbuf", [128, 4, 50], "bfloat16")}
for _t in range(NV + 1):
    SCRATCH["X%d" % _t] = ("sbuf", [128, XW], "bfloat16")
for _d in POOLS:
    SCRATCH[POOLS[_d][0]] = ("sbuf", [128, SIZE[_d]], _d)
for _h in range(2):
    for _n in ("x1", "x2", "z", "xc", "ax"):
        SCRATCH[_n + str(_h)] = ("sbuf", [128, 16 * CH], "bfloat16")
    SCRATCH["MBS" + str(_h)] = ("sbuf", [128, 4, 32], "float32")
for _n in ("K0", "K1", "M0", "M1", "B0", "B1", "TB"):
    SCRATCH[_n] = ("psum", [128, 512], "float32")
SCRATCH["S5"] = ("psum", [128, 8, 64], "float32")

SEMAPHORES = ["cV", "cS", "cT", "cG"] + ["d%d" % k for k in range(40)] + \
    ["r%d" % k for k in range(12)] + ["l%d" % k for k in range(12)]


def rank_program(g, core, T, topo):
    rank = T.rank_of(core)
    if rank is None:
        return
    nxt, prv = T.cores[(rank + 1) % N], T.cores[(rank - 1) % N]
    QUEUE = {"V": g.vector, "S": g.scalar, "T": g.tensor, "G": g, "Y": g.sync, "SD": g.scalar}

    def t(name, a=0, b=None, s=None):
        pool, off, cols = TILES[name]
        b = cols if b is None else b
        return T[pool][:, off + a:off + b:s] if s else T[pool][:, off + a:off + b]

    def rev(name):
        pool, off, cols = TILES[name]
        return T[pool][:, off + cols - 1:(off - 1 if off else None):-1]

    def slot(bank, j):
        return T.S5[:, 2 * j:2 * j + 2, :] if bank == "S5" else T[bank][:, 128 * j:128 * j + 128]

    ops = []
    last_w, readers, banks, last_pe = {}, {}, {}, {}
    dcount, now = [0], [0.0]

    def add(eng, fn, rd, wr, cost, hold=None, sem=None, need=1, extra=(), comp=True, acc=False):
        k = len(ops)
        deps = {}
        phys = {"SD": "S"}.get(eng, eng)

        def dep(o, kind):
            if o == k:
                return
            if (kind == "war" or kind == "waw" and acc) and comp and ops[o]["phys"] == phys and ops[o]["comp"]:
                deps.setdefault(o, "order")
            else:
                deps[o] = "wait"
        for x in rd:
            if x in last_w:
                dep(last_w[x], "raw")
        for x in wr:
            if x in last_w:
                dep(last_w[x], "waw")
            for o in readers.get(x, ()):
                dep(o, "war")
        for b in sorted(set(x[1:3] for x in list(rd) + list(wr) if x[0] == "@")):
            ep = banks.setdefault(b, [phys, [], []])
            if ep[0] != phys:
                ep[0], ep[1], ep[2] = phys, [], ep[1]
            for o in ep[2]:
                dep(o, "bank")
            ep[1].append(k)
            if phys == "T":
                if b in last_pe:
                    deps.setdefault(last_pe[b], "order")
                last_pe[b] = k
        for o in extra:
            deps.setdefault(o, "order")
        ops.append(dict(eng=eng, phys=phys, comp=comp, fn=fn, deps=deps, cost=cost, hold=cost if hold is None else hold, sem=sem, need=need,
                        name=(wr or rd)[0], bonus=now[0]))
        for x in rd:
            readers.setdefault(x, []).append(k)
        for x in wr:
            last_w[x] = k
            readers[x] = []
        return k

    def V(fn, rd, wr, n):
        return add("V", lambda: fn(g.vector), rd, wr, COST[0] + max(n, 64) * 0.83e-3)

    def S(fn, rd, wr, n):
        return add("S", lambda: fn(g.scalar), rd, wr, COST[1] + max(n, 64) * 0.83e-3)

    def P(lst, rd, wr, n, start=True, stop=True, after=()):
        def f():
            for k, (o, l, x) in enumerate(lst):
                r = g.tensor.matmul(o, l, x, start[k] if isinstance(start, list) else start and k == 0,
                                    stop[k] if isinstance(stop, list) else stop and k == len(lst) - 1)
            return r
        return add("T", f, rd, wr, 0.06 + n * COST[2], hold=n * COST[2], acc=start is False, extra=after)

    def G(fn, rd, wr, n):
        return add("G", lambda: fn(g), rd, wr, 0.17 + n * 1.66e-3)

    def dma(eng, out, in_, rd, wr, lat):
        s = "d%d" % dcount[0]
        dcount[0] += 1
        k = add(eng, lambda: QUEUE[eng].dma_start(out, in_), rd, wr, lat, hold=0.05, sem=s, need=16, extra=loads.get(eng, []) if not rd else [], comp=False)
        loads[eng] = [k]

    loads = {}

    def ts(out, i0, s1, op0, s2=None, op1=None):
        if s2 is None:
            return lambda v: v.tensor_scalar(out, i0, s1, None, op0)
        return lambda v: v.tensor_scalar(out, i0, s1, s2, op0, op1)

    def tt(out, a, b, op):
        return lambda v: v.tensor_tensor(out, a, b, op)

    def cp(out, a):
        return lambda v: v.tensor_copy(out, a)

    def ms(out, c):
        return lambda v: v.memset(out, c)

    def scan(out, a, b, op0, op1, first=0.0):
        return lambda v: v.tensor_tensor_scan(out, a, b, first, op0, op1)

    def act(out, a, func=AF.Identity, bias=0.0, scale=1.0):
        return lambda s: s.activation(out, a, func, bias=bias, scale=scale)

    def sel(out, a, pattern, op, fill, base, mult):
        return lambda q: q.affine_select(out, a, pattern, op, fill, base, mult)

    def iota(out, pattern, base, mult):
        return lambda q: q.iota(out, pattern, base, mult, allow_small_or_imprecise_dtypes=True)

    now[0] = 100.0
    dma("Y", t("WI"), T.why[:], [], ["WI"], 1.5 + DM * 1.3)
    dma("SD", t("DI"), T.drugs[:], [], ["DI"], 1.5 + DM * 2.6)
    dma("Y", t("LIMI"), T.lim[:], [], ["LIMI"], 1.6 + DM * 2.6)
    for k in range(NP):
        dma("Y" if k % 2 == 0 else "SD", T.X0[:, k * PW:(k + 1) * PW], T.eff[:, k * PW:(k + 1) * PW], [], ["Xr%d" % k], 1.6 + DM * (2.6 + 2.2 * (k + 1)))
    dma("Y", T.R[:, :D // 2], T.rem[:, :D // 2], [], ["Ra"], 1.6 + DM * 20.3)
    dma("Y", T.R[:, D // 2:], T.rem[:, D // 2:], [], ["Rb"], 1.6 + DM * 29.1)
    XK = [["Xr%d" % k for k in range(NP)] + ["Xz"]] + [["X%d" % k] for k in range(1, NV + 1)]

    now[0] = 5.0
    V(ms(t("ONES"), 1.0), [], ["ONES"], 64)
    G(lambda q: q.iota(t("MI"), [[0, 1]], 0, 1), [], ["MI"], 1)
    G(sel(t("IDF"), t("ONES"), [[-1, 128]], A.is_equal, 0.0, 0, 1), ["ONES"], ["IDF"], 128)
    V(ts(t("MI2"), t("MI"), 15, A.bitwise_and), ["MI"], ["MI2"], 64)
    V(cp(t("MCOL"), t("MI2")), ["MI2"], ["MCOL"], 64)
    S(act(t("IDENT"), t("IDF"), AF.Copy), ["IDF"], ["IDENT"], 128)
    G(iota(t("QROW"), [[0, 8], [1, 16]], 0, 0), [], ["QROW"], 128)
    V(ts(t("DQF"), t("QROW"), t("MCOL"), A.is_equal), ["QROW", "MCOL"], ["DQF"], 128)
    V(ms(t("TWO"), 2.0), [], ["TWO"], 64)
    V(ms(t("ZERO"), 0.0), [], ["ZERO"], 128)
    V(scan(t("POW"), t("TWO"), t("ZERO", 0, 16), A.mult, A.add, 0.5), ["TWO", "ZERO"], ["POW"], 64)
    V(tt(t("TT"), t("POW"), t("DQF", 0, 16), A.mult), ["POW", "DQF"], ["TT"], 64)
    V(lambda v: v.tensor_reduce(t("PC2"), t("TT"), AxisListType.X, A.add), ["TT"], ["PC2"], 64)
    V(ts(t("MB1"), t("MCOL"), -BIG, A.mult, -BIG, A.add), ["MCOL"], ["MB1"], 64)
    V(ts(t("JB"), t("QROW", 0, 16), t("MCOL"), A.subtract, BIG, A.mult), ["QROW", "MCOL"], ["JB"], 64)
    V(ts(t("JB"), t("JB"), -0.5, A.add, KK, A.mult), ["JB"], ["JB"], 64)

    V(ts(t("FN"), t("WI"), t("MCOL"), A.not_equal), ["WI", "MCOL"], ["FN"], 256)
    V(ts(t("VI"), t("WI"), 1.0, A.add, BIG, A.mult), ["WI"], ["VI"], 256)
    V(tt(t("VI"), t("VI"), t("FN"), A.mult), ["VI", "FN"], ["VI"], 512)
    V(ts(t("VV"), t("VI"), t("MB1"), A.add, t("PC2"), A.add), ["VI", "MB1", "PC2"], ["VV0", "VV1"], 256)
    for j in range(15, -1, -1):
        RJ = "RJ%d" % j
        rj = t("RJ", j * 128, j * 128 + 128)
        now[0] = 5.0
        G(sel(rj, t("IDF"), [[-16, 8], [0, 16]], A.not_equal, 1.0, -j, 1), ["IDF"], [RJ], 128)
        for h in range(2):
            H = str(h)
            now[0] = BONUS[9] * (1 - h)
            bank = ("S5", "TB")[h]
            o, key, vv = slot(bank, 0), "@%s:c" % bank, t("VV", h * CH, h * CH + CH)
            S(act(t("SG" + H), vv, AF.Relu, t("JB", j, j + 1), -KK), ["VV" + H, "JB"], ["SG" + H], 128)
            P([(o, rj, vv)], [RJ, "VV" + H], [key], 512, True, False)
            P([(o, t("IDENT"), t("SG" + H))], ["IDENT", "SG" + H], [key], 128, False, True)
            V(tt(vv, vv, o, A.min), ["VV" + H, key], ["VV" + H], 128)
    now[0] = 0.0
    V(ts(t("PB1"), t("MCOL"), BIG, A.mult), ["MCOL"], ["PB1"], 64)
    S(act(t("DPB"), t("IDENT"), AF.Copy, 0.0, t("PB1")), ["IDENT", "PB1"], ["DPB"], 128)
    S(act(t("IBIG"), t("IDENT"), AF.Copy, 0.0, BIG), ["IDENT"], ["IBIG"], 128)
    V(ts(t("T1"), t("WI"), 1 / 64, A.mult, 1 / 64, A.add), ["WI"], ["T1"], 256)
    for h in range(2):
        H, c = str(h), (h * CH, h * CH + CH)
        V(cp(t("LU%d0" % h), t("DI", *c)), ["DI"], ["LU%d0" % h], 128)
        V(ts(t("F1" + H), t("LU%d0" % h), D - 0.5, A.is_lt), ["LU%d0" % h], ["F1" + H], 64)
        bank = ("S5", "TB")[h]
        o, key = slot(bank, 1), "@%s:w" % bank
        P([(o, t("IDF"), t("VV", *c)), (o, t("DPB"), t("ONES")), (o, t("IBIG"), t("F1" + H)), (o, t("IDF"), t("T1", *c))],
          ["IDF", "VV" + H, "DPB", "ONES", "IBIG", "F1" + H, "T1"], [key], 1280)
        S(act(t("DW%d0" % h, CH), o, AF.Relu), [key], ["W%d0" % h], 128)

    V(ms(T.X0[:, D:], 0.0), [], ["Xz"], 64)
    G(sel(t("BO"), t("ONES"), [[-16, 8], [0, 16]], A.is_ge, 0.0, 0, 1), ["ONES"], ["BO"], 128)
    G(sel(t("BO"), t("BO"), [[16, 8], [0, 16]], A.is_ge, 0.0, 15, -1), ["BO"], ["BO"], 128)
    G(sel(t("CONSTL"), t("ONES"), [[0, 128]], A.is_ge, 0.0, 1, -1), ["ONES"], ["CONSTL"], 128)
    E = t("BO", 0, 128, 16)
    for nm, sc in (("E1", 1.0), ("E16", 16.0), ("E16N", -16.0), ("E32", 32.0), ("E32N", -32.0), ("EBN", -BIG), ("SELC", 1.0)):
        V(ts(t(nm), E, sc, A.mult), ["BO"], [nm], 64)
    V(ts(t("E164"), t("BO", 0, 128, 4), 16.0, A.mult), ["BO"], ["E164"], 64)
    G(iota(t("KS"), [[0, 8], [-1, 16]], 15, 0), [], ["KS"], 128)
    G(sel(t("KS"), t("KS"), [[0, 128]], A.is_ge, BIG, 0, -1), ["KS"], ["KS"], 128)
    V(ts(t("KC2"), t("QROW"), 0.5, A.mult, -8.0, A.add), ["QROW"], ["KC2"], 128)
    V(ms(t("K155"), -3.75), [], ["K155"], 64)
    V(ms(t("K775"), -7.75), [], ["K775"], 128)
    V(ts(t("NDQ"), t("DQF"), BIG, A.mult, -BIG, A.add), ["DQF"], ["NDQ"], 128)
    G(sel(t("LT"), t("BO"), [[1, 128]], A.is_gt, 0.0, 0, -1), ["BO"], ["LT"], 128)
    G(sel(t("LT"), t("LT"), [[1, 128]], A.not_equal, -32.0, 0, -1), ["LT"], ["LT"], 128)
    V(ts(t("OHB"), t("MCOL"), -1.0 if UR == "G" else -2.0, A.mult, 1.0 if UR == "G" else 33.0, A.add), ["MCOL"], ["OHB"], 64)
    V(ts(t("M64C"), t("MCOL"), 1 / 64, A.mult, 1 / 64, A.add), ["MCOL"], ["M64C"], 64)
    V(ts(t("DGC"), t("MCOL"), -1.0, A.mult, 16.0, A.add), ["MCOL"], ["DGC"], 64)
    V(ts(t("B15"), t("MCOL"), -1.0, A.mult, 135.0, A.add), ["MCOL"], ["B15"], 64)
    V(ms(t("TWO"), 0.5), [], ["TWO"], 64)
    V(scan(t("POW"), t("TWO"), t("ZERO", 0, 16), A.mult, A.add, 65536.0 if UR == "G" else 1.0), ["TWO", "ZERO"], ["POW"], 64)
    V(tt(t("TT"), t("POW"), t("DQF", 0, 16), A.mult), ["POW", "DQF"], ["TT"], 64)
    V(lambda v: v.tensor_reduce(t("PC15"), t("TT"), AxisListType.X, A.add), ["TT"], ["PC15"], 64)
    for nm, src, sc in (("DG", "IDENT", "DGC"), ("P15", "BO", "PC15"), ("BOF", "BO", 1.0), ("M64", "BO", "M64C"), ("BO8K", "BO", 8192.0),
                        ("NBIG", "BO", -BIG - MAGIC), ("N8K", "IDENT", -8192.0), ("N4K", "IDENT", -4096.0),
                        ("D2M", "IDENT", "PC2"), ("NID", "IDENT", -1.0), ("I16", "IDENT", 16.0), ("I256", "IDENT", 1 / 256),
                        ("NHUGE", "IDENT", -BIG * 65536)):
        if nm != "I256" or "S" in UR + ZR:
            S(act(t(nm, 0, 128), t(src), AF.Copy, 0.0, t(sc) if sc in TILES else sc), [src] + ([sc] if sc in TILES else []), [nm], 128)
    V(ms(t("ONESF"), 1.0), [], ["ONESF"], 128)
    V(ms(t("MASK"), 1.0), [], ["MASK"], 128)
    V(ms(t("MASK", 0, 128, 16), 0.0), [], ["MASK"], 64)
    for q in range(4 * (UR != "G")):
        G(lambda e, q=q: e.iota(t("SEL", 512 * q, 512 * q + 512), [[4, 4], [16, 8], [0, 16]], q, -1, allow_small_or_imprecise_dtypes=True),
          [], ["SEL%d" % q], 512)
        V(ts(t("SEL", 512 * q, 512 * q + 512), t("SEL", 512 * q, 512 * q + 512), 0.0, A.is_equal), ["SEL%d" % q], ["SEL%d" % q], 256)
    V(ms(t("SGN"), -1.0), [], ["SGN"], 64)
    V(ms(t("SGN", 16, 50, 33), 1.0), [], ["SGN"], 64)
    for r in range(4):
        V(ts(T.NB50[:, r, 0:17], t("SGN", 0, 17), t("SELC", 2 * r, 2 * r + 1), A.mult), ["SGN", "SELC"], ["NB%da" % r], 64)
        V(ts(T.NB50[:, r, 17:50], t("SGN", 17, 50), t("SELC", 2 * r + 1, 2 * r + 2), A.mult), ["SGN", "SELC"], ["NB%db" % r], 64)
    NB = ["NB%d%s" % (r, c) for r in range(4) for c in "ab"]
    V(ms(T.TRI50[:], 0.0), [], ["TRI50"], 100)
    for a in (0, 17):
        V(ts(T.TRI50[:, :, a:a + 16], t("QROW", 0, 64), t("MCOL"), A.is_ge, 8192.0, A.mult), ["QROW", "MCOL", "TRI50"], ["TRI50"], 64)
    V(ms(t("MASK5"), 0.0), [], ["MASK5"], 200)
    for b in range(2):
        V(ms(t("MASK5", 17 * b, 400, 50), 16384.0), [], ["MASK5"], 64)
        V(ts(t("DUM", b, b + 1), t("MCOL"), PAD + 1.0 + 16 * b, A.add), ["MCOL"], ["DUM%d" % b], 64)
    V(cp(t("LIMF"), t("LIMI")), ["LIMI"], ["LIMF"], 64)
    V(ts(t("TH"), t("LIMF"), BIG / 16, A.mult), ["LIMF"], ["TH"], 64)
    V(ts(t("THE"), t("SELC"), t("TH"), A.mult), ["SELC", "TH"], ["THE"], 64)

    def gather(dst, lst, h, vt, plan):
        w = []
        for (e, a, b) in plan:
            key = "%s%d:%d" % (dst, h, a)
            o, s = T[dst + str(h)][:, 16 * a:16 * b], T["X%d" % vt][:].indirect(t(lst, a, b))
            (S if e == "S" else V)(act(o, s, AF.Copy) if e == "S" else cp(o, s), XK[vt] + [lst], [key, dst + str(h) + "w%d" % a], 16 * (b - a) * 1.56)
            w.append(key)
        return w

    def argmax(h, kill=None, kl=None):
        H = str(h)
        src, k16 = "@K%s:k" % H, slot("K" + H, 0)
        V(scan(t("SCA" + H), t("MASK"), k16, A.mult, A.max), [src, "MASK"], ["SCA" + H], 128)
        if kill is not None:
            V(tt(t("SCA" + H, 15, 128, 16), t("SCA" + H, 15, 128, 16), kill, A.max), [kl, "SCA" + H], ["SCA" + H], 64)
        V(scan(rev("SC" + H), t("MASK"), rev("SCA" + H), A.mult, A.max), ["SCA" + H, "MASK"], ["SC" + H], 128)
        V(tt(t("OHD" + H), k16, t("SC" + H), A.is_equal), [src, "SC" + H], ["OHD" + H], 128)

    def row(x, m):
        k = 4 * (m % 4) + m // 4
        return x[:, 128 * k:128 * k + 128]

    def four(out, x, b, y, op):
        def f(v):
            for m in range(b, 16, 4):
                r = v.tensor_tensor(row(out, m), x[:, m::16], y, op)
            return r
        return f

    kx1, kx2 = {}, {}

    def phase1(vt, h):
        H = str(h)
        LU, DW = "LU%d%d" % (h, vt), "DW%d%d" % (h, vt)
        DF, W = "DF%d%d" % (h, vt), "W%d%d" % (h, vt)
        K, M, B, x = T["K" + H], "M" + H, "B" + H, T["x1" + H]
        kx = kx1[h] = gather("x1", LU, h, vt, X1 if vt else X1F)
        V(ts(t(DW, 0, CH), t(LU), 1.0, A.add), [LU], [DF], 128)
        S(act(t("WR" + H), t(DW, CH), AF.Identity, MAGIC), [W], ["WR" + H], 128)
        if vt:
            V(ts(t("F1" + H), t(LU), D - 0.5, A.is_lt), [LU], ["F1" + H], 64)
        P([(T[M][:, 0:8], t("F1" + H), t("E1"))], ["F1" + H, "E1"], ["@%s:e" % M], 64)
        S(act(t("FULL" + H), T[M][:, 0:8], AF.Relu, -15.0), ["@%s:e" % M], ["FULL" + H], 8)
        kk, kill, kl = "@K%s:k" % H, T[M][:, 8:16], "@%s:kill" % M
        P([(K[:, 0:128], t("F1" + H), t("DG"))], ["F1" + H, "DG"], [kk], 128, True, False)
        P([(kill, t("ONESF"), t("THE")), (kill, t("NHUGE"), t("FULL" + H))], ["ONESF", "THE", "NHUGE", "FULL" + H], [kl], 320, True, False)
        first = P([(K[:, m:128:16], x[:, m::16], t("E32")) for m in range(16)], ["E32"] + kx, [kk], 1024, False, True)
        P([(kill, x[:, m::16], t("EBN")) for m in range(16)], ["EBN"] + kx, [kl], 1024, False, True, [first])
        argmax(h, kill, kl)
        if UR == "G":
            P([(slot(M, 3), t("IDF"), t(DW, CH))], ["IDF", W], ["@%s:1" % M], 512, True, False)
        else:
            P([(T[M][:, 256:512], t("IDF"), t(DW)), (slot(M, 1), t("LT"), t("F1" + H))], ["IDF", DF, W, "LT", "F1" + H], ["@%s:1" % M], 1152, True, False)
        P([(slot(B, 0), t("OHD" + H), t("IDENT"))], ["OHD" + H, "IDENT"], ["@%s:0" % B], 128)
        S(act(t("OHS" + H), slot(B, 0), AF.Copy), ["@%s:0" % B], ["OHS" + H], 128)
        V(tt(T["MBS" + H][:], slot(B, 0), t(DW, 0, CH), A.mult), ["@%s:0" % B, DF], ["MBS" + H], 128)
        B = "K" + H
        P([(slot(B, 0), t("P15"), t("OHS" + H))], ["P15", "OHS" + H], ["@%s:0" % B], 128)
        if UR == "G":
            V(tt(t("TI" + H), t(DW, CH), slot(B, 0), A.mult), [W, "@%s:0" % B], ["TI" + H], 128)
            V(ts(t("GI" + H), t("TI" + H), 3, A.logical_shift_right, 4096, A.bitwise_and), ["TI" + H], ["GI" + H], 128)
            V(tt(t("D2" + H), t(DW, 0, CH), t("GI" + H), A.max), [DF, "GI" + H], ["D2" + H], 256)
            V(ts(t("L2" + H), t("D2" + H), 1.0, A.subtract, float(D), A.min), ["D2" + H], ["L2" + H], 128)
            V(ts(t("KEEP" + H), t("L2" + H), D - 0.5, A.is_lt), ["L2" + H], ["KEEP" + H], 64)
            return
        V(tt(slot(B, 1), t(DW, CH), slot(B, 0), A.mult), [W, "@%s:0" % B], ["@%s:1" % B], 128)
        V(ts(t("RR" + H), slot(B, 1), MAGIC, A.add, MAGIC, A.subtract), ["@%s:1" % B], ["RR" + H], 128)
        V(tt(t("KEEP" + H), t("RR" + H), slot(B, 1), A.is_le), ["RR" + H, "@%s:1" % B], ["KEEP" + H], 128)

    def phase2(vt, h):
        H = str(h)
        K, M, x, x2, keep = T["K" + H], "M" + H, T["x1" + H], T["x2" + H], t("KEEP" + H)

        def mask(b):
            bank = "BK"[b % 2] + H
            key = "@%s:w" % bank
            rows = [(T[bank][:, u::4], t("SEL", 128 * (4 * b + u), 128 * (4 * b + u + 1)), keep) for u in range(4)]
            if UR[b] == "V":
                P(rows, ["SEL%d" % b, "KEEP" + H], [key], 512, [True] * 4, [True] * 4)
                V(tt(x2[:, b::4], x[:, b::4], T[bank][:], A.mult), kx1[h] + [key], ["x2%s:%d" % (H, b)], 512)
            else:
                P([(T[bank][:], t("I256"), x[:, b::4])] + rows, ["SEL%d" % b, "KEEP" + H, "I256"] + kx1[h], [key], 1024)
                S(act(x2[:, b::4], T[bank][:], AF.Relu, -256.0, 256.0), [key], ["x2%s:%d" % (H, b)], 512)
        if UR == "G":
            kx2[h] = gather("x2", "L2" + H, h, vt, X2)
            P([(slot(M, 3), t("IBIG"), keep)], ["IBIG", "KEEP" + H], ["@%s:1" % M], 128, False, True)
            P([(slot(M, 1), t("LT"), keep)], ["LT", "KEEP" + H], ["@%s:2" % M], 128)
            S(act(t("OHE" + H), slot(M, 1), AF.Relu, t("OHB")), ["@%s:2" % M, "OHB"], ["OHE" + H], 128)
            S(act(t("W2" + H), slot(M, 3), AF.Relu, -BIG), ["@%s:1" % M], ["W2" + H], 128)
            u, ku = slot("B" + H, 0), "@B%s:u" % H
            P([(u, t("CONSTL"), t("K155"))], ["CONSTL", "K155"], [ku], 128, True, False)
            pieces = sorted(zip(X2, kx2[h]), key=lambda x: x[0][2] - x[0][1])
            for (e, a, b), key in pieces:
                P([(T["B" + H][:, a:b], t("IDENT"), x2[:, 16 * a + m:16 * b:16]) for m in range(16)], ["IDENT", key], [ku], 16 * max(64, b - a),
                  False, key == pieces[-1][1])
        else:
            kx2[h] = []
            mask(0)
            mask(1)
            P([(slot(M, 1), t("LT"), keep), (slot(M, 2), t("N4K"), keep), (slot(M, 3), t("IBIG"), keep)],
              ["LT", "N4K", "IBIG", "KEEP" + H], ["@%s:1" % M], 384, False, True)
            S(act(t("OHE" + H), slot(M, 1), AF.Relu, t("OHB")), ["@%s:1" % M, "OHB"], ["OHE" + H], 128)
            S(act(t("D2" + H), slot(M, 2), AF.Identity, 4096.0), ["@%s:1" % M], ["D2" + H], 128)
            S(act(t("W2" + H), slot(M, 3), AF.Relu, -BIG), ["@%s:1" % M], ["W2" + H], 128)
            mask(2)
            mask(3)
            u, ku = slot(M, 0), "@%s:0" % M
            for b in range(4):
                P([(u, t("CONSTL"), t("K155"))] * (b == 0) + [(u, t("IDENT"), x2[:, m::16]) for m in range(b, 16, 4)],
                  ["CONSTL", "K155", "IDENT", "x2%s:%d" % (H, b)], [ku], 512 + 128 * (b == 0), b == 0, b == 3)
        S(act(t("U32" + H), u, AF.Identity, t("B15"), 16.0), [ku, "B15"], ["U32" + H], 128)
        S(act(t("Y" + H), u, AF.Identity, MAGIC, 1 / 16), [ku], ["Y" + H], 128)
        P([(K[:, 0:128], t("U32" + H), t("IDF"))], ["U32" + H, "IDF"], ["@K%s:k" % H], 512)
        S(act(t("VB" + H), t("Y" + H), AF.Identity, MAGIC + 255, -1.0), ["Y" + H], ["VB" + H], 128)
        argmax(h)

    def phase3(vt, h):
        H = str(h)
        DW = "DW%d%d" % (h, vt)
        DF = "DF%d%d" % (h, vt)
        K, M, B, x2, z = T["K" + H], "M" + H, "B" + H, T["x2" + H], T["z" + H]
        kk = "@K%s:k" % H
        P([(slot(B, 0), t("OHD" + H), t("IDENT"))], ["OHD" + H, "IDENT"], ["@%s:w" % B], 128)
        if UR == "G":
            P([(K[:, 0:128], t("KEEP" + H), t("DG"))], ["KEEP" + H, "DG"], [kk], 128, True, False)
        else:
            P([(K[:, 0:128], t("F1" + H), t("DG")), (K[:, 0:128], t("KEEP" + H), t("DG")), (K[:, 0:128], t("CONSTL"), t("KC2"))],
              ["F1" + H, "KEEP" + H, "DG", "CONSTL", "KC2"], [kk], 384, True, False)
        for b in range(4):
            if ZR[b] == "V":
                V(four(z, x2, b, slot(B, 0), A.mult), kx2[h] + ["@%s:w" % B], ["z%s:%d" % (H, b)], 512 + 3 * COST[0] / 0.83e-3)
            else:
                P([(slot(M, u), t("I256"), x2[:, 4 * u + b::16]) for u in range(4)], kx2[h] + ["I256"], ["@%s:w" % M], 512, True, False)
                P([(slot(M, u), t("OHD" + H), t("IDENT")) for u in range(4)], ["OHD" + H, "IDENT"], ["@%s:w" % M], 512, False, True)
                S(act(z[:, 512 * b:512 * b + 512], T[M][:], AF.Relu, -256.0, 256.0), ["@%s:w" % M], ["z%s:%d" % (H, b)], 512)
        for b in range(4):
            P([(K[:, m:128:16], row(z, m), t("E32")) for m in range(b, 16, 4)], ["E32", "z%s:%d" % (H, b)], [kk], 256, False, b == 3)
        argmax(h)
        P([(slot(M, 0), t("OHD" + H), t("IDENT"))], ["OHD" + H, "IDENT"], ["@%s:0" % M], 128)
        V(tt(t("MBK" + H), slot(M, 0), t(DW, 0, CH), A.mult), ["@%s:0" % M, DF], ["MBK" + H], 128)
        V(tt(t("MBA" + H), slot(M, 0), t("WR" + H), A.mult), ["@%s:0" % M, "WR" + H], ["MBA" + H], 128)
        S(act(t("OHK" + H), slot(M, 0), AF.Copy), ["@%s:0" % M], ["OHK" + H], 128)
        if "K" in ONS:
            P([(slot(B, 0), t("IDENT"), t("NDQ"))], ["IDENT", "NDQ"], ["@%s:0" % B], 128, True, False)
            P([(slot(B, 0), t("MBK" + H), t("BOF"))], ["MBK" + H, "BOF"], ["@%s:0" % B], 512, False, True)
            S(act(t("VM" + H), slot(B, 0), AF.Relu), ["@%s:0" % B], ["VM" + H], 128)
        else:
            P([(slot(B, 0), t("MBK" + H), t("BOF"))], ["MBK" + H, "BOF"], ["@%s:0" % B], 512)
            V(tt(t("VM" + H), slot(B, 0), t("DQF"), A.mult), ["@%s:0" % B, "DQF"], ["VM" + H], 128)
        P([(T[B][:, 128:136], t("VM" + H), t("SELC"))], ["VM" + H, "SELC"], ["@%s:1" % B], 256)
        V(ts(t("LC" + H, 0, 8), T[B][:, 128:136], 1.0, A.subtract, D - 1.0, A.min), ["@%s:1" % B], ["LC" + H], 64)
        V(cp(t("CU" + H), T.R[:].indirect(t("LC" + H, 0, 8))), ["Ra", "Rb", "LC" + H], ["CU" + H], 200)

    def phase4(vt, h):
        H = str(h)
        K, M, B, xc, ax = T["K" + H], "M" + H, "B" + H, T["xc" + H], T["ax" + H]
        kk, SW, vb = "@K%s:k" % H, "SW%d%d" % (h, vt + 1), t("VB" + H)
        last = vt == NV - 1
        kx = gather("xc", "CU" + H, h, vt, XC)
        if "C" in ONS:
            S(act(t("CF" + H), T.R[:].indirect(t("LC" + H, 0, 8)), AF.Identity, 1.0), ["Ra", "Rb", "LC" + H], ["CF" + H], 200)
        else:
            V(ts(t("CF" + H), t("CU" + H), 1.0, A.add), ["CU" + H], ["CF" + H], 128)
        o = slot(M, 3)
        P([(o, t("BOF"), t("MBA" + H)), (o, t("NBIG"), t("OHK" + H)), (o, t("IBIG"), t("OHE" + H)), (o, t("D2M"), t("OHE" + H)), (o, t("M64"), t("OHK" + H))],
          ["BOF", "MBA" + H, "D2M", "OHE" + H, "IBIG", "NBIG", "OHK" + H, "M64"], ["@%s:3" % M], 1024)
        V(tt(t(SW), t("W2" + H), o, A.max), ["W2" + H, "@%s:3" % M], [SW], 128)
        if not last:
            send(t(SW), t("DW%d%d" % (h, vt + 1), CH), SW, "W%d%d" % (h, vt + 1), 6 * h + 2 * vt + 1, COST[4])
        else:
            V(ts(t("YM" + H), t(SW), MAGIC, A.add, MAGIC, A.subtract), [SW], ["YM" + H], 128)
            V(tt(t("YQ" + H), t(SW), t("YM" + H), A.subtract), ["YM" + H, SW], ["YQ" + H], 256)
            S(act(t("YR" + H), t("YQ" + H), AF.Relu, -1.0, 64.0), ["YQ" + H], ["YR" + H], 128)
            dma("Y", T.yq[:, h * CH:h * CH + CH], t("YR" + H), ["YR" + H], [], 2.5)
        P([(K[:, 0:128], t("CONSTL"), t("KS"))] + [(K[:, b:128:4], vb, t("E164")) for b in range(4) if AR[b] == "V"],
          ["CONSTL", "KS", "VB" + H, "E164"], [kk], 128 + 64 * AR.count("V"), True, False)
        if "V" in AR:
            P([(slot(B, 0), t("IDENT"), vb)], ["IDENT", "VB" + H], ["@%s:w" % B], 128)
        sbank = [M, M] if "V" in AR else [M, B]
        for b in range(4):
            ka = "ax%s:%d" % (H, b)
            if AR[b] == "V":
                V(four(ax, xc, b, slot(B, 0), A.max), kx + ["@%s:w" % B], [ka], 512 + 3 * COST[0] / 0.83e-3)
            else:
                bank = sbank[b % 2]
                P([(slot(bank, u), t("NID"), vb) for u in range(4)], ["NID", "VB" + H], ["@%s:w" % bank], 512, True, False)
                P([(slot(bank, u), t("IDENT"), xc[:, 4 * u + b::16]) for u in range(4)], ["IDENT"] + kx, ["@%s:w" % bank], 512, False, True)
                S(act(ax[:, 512 * b:512 * b + 512], T[bank][:], AF.Abs), ["@%s:w" % bank], [ka], 512)
        vs = [j for j in range(16) if AR[j % 4] == "V"]
        if vs:
            P([(K[:, j:128:16], xc[:, j::16], t("E16")) for j in vs], ["E16"] + kx, [kk], 64 * len(vs), False, False)
        for b in range(4):
            P([(K[:, j:128:16], row(ax, j), t("E32N" if AR[b] == "V" else "E16N")) for j in range(b, 16, 4)],
              ["E32N", "E16N", "ax%s:%d" % (H, b)], [kk], 256, False, b == 3)
        o = slot(B, 1)
        P([(o, t("BO8K"), t("OHK" + H)), (o, t("N8K"), t("OHE" + H))], ["BO8K", "N8K", "OHK" + H, "OHE" + H], ["@%s:1" % B], 256, True, False)
        argmax(h)
        P([(slot(M, 0), t("OHD" + H), t("IDENT"))], ["OHD" + H, "IDENT"], ["@%s:0" % M], 128)
        V(tt(t("MB2" + H), slot(M, 0), t("CF" + H), A.mult), ["@%s:0" % M, "CF" + H], ["MB2" + H], 128)
        P([(o, t("BOF"), t("MB2" + H))], ["BOF", "MB2" + H], ["@%s:1" % B], 512, False, True)
        V(tt(t("D3" + H), t("D2" + H), o, A.min), ["D2" + H, "@%s:1" % B], ["D3" + H], 128)
        if not last:
            LN, LU = "SLU%d%d" % (h, vt + 1), "LU%d%d" % (h, vt + 1)
            V(ts(t(LN), t("D3" + H), 1.0, A.subtract, float(D), A.min), ["D3" + H], [LN], 128)
            send(t(LN), t(LU), LN, LU, 6 * h + 2 * vt, COST[3])
        else:
            V(ts(t("YP" + H), t("D3" + H), 1.0, A.subtract, float(D), A.min), ["D3" + H], ["YP" + H], 128)
            dma("Y", T.yp[:, h * CH:h * CH + CH], t("YP" + H), ["YP" + H], [], 2.5)

    def send(src, dst, rd, wr, k, lat):
        mask, n = topo.mask(core, nxt), len(topo.engines(core, nxt))
        rid, pid = topo.addr(nxt)[:2]
        o = add("G", lambda: g.remote_dma(dst, src, T.sem["r%d" % k], T.sem["l%d" % k], pid, rid, mask), [rd], ["sent:" + rd], 1.0, hold=0.6,
                sem="l%d" % k, need=n, comp=False)
        add("N", None, [], [wr], lat, sem="r%d" % k, need=len(topo.engines(prv, core)), extra=[o], comp=False)

    def pairs(vt, h):
        H = str(h)
        x, mbs, dd = T["x1" + H], T["MBS" + H], T.S5
        if h == 0:
            P([(T.TB[:, 0:256], t("CONSTL"), t("K775"))], ["CONSTL", "K775"], ["@TB:t"], 256, True, False)
        for b in range(4):
            P([(slot("TB", h), t("IDENT"), x[:, m::16]) for m in range(b, 16, 4)], ["IDENT"] + kx1[h], ["@TB:t"], 512, False, False)
        P([(slot("S5", 2 * h), t("IDENT"), t("NDQ"))] * ("5" in ONS) + [(slot("S5", 2 * h), mbs[:], t("BOF"))], ["MBS" + H, "BOF", "IDENT", "NDQ"],
          ["@S5:c" + H], 512 + 128 * ("5" in ONS))
        if "5" in ONS:
            S(act(t("VMS" + H), slot("S5", 2 * h), AF.Relu), ["@S5:c" + H], ["VMS" + H], 128)
        else:
            V(tt(t("VMS" + H), slot("S5", 2 * h), t("DQF"), A.mult), ["@S5:c" + H, "DQF"], ["VMS" + H], 128)
        r = slice(4 * h, 4 * h + 4)
        P([(dd[:, r, 0:50], t("VMS" + H), T.NB50[:]), (dd[:, r, 0:50], t("IDENT"), T.TRI50[:]), (dd[:, r, 0:16], t("BOF"), mbs[:, :, 0:16]),
           (dd[:, r, 17:33], t("BOF"), mbs[:, :, 16:32]), (dd[:, r, 33:49], t("BOF"), mbs[:, :, 0:16])],
          ["VMS" + H, "IDENT", "TRI50", "BOF", "MBS" + H] + NB, ["@S5:d" + H], 1768)

    def update(vt):
        dc, kd = T.S5[:, :, 16:50:33], ["@S5:d0", "@S5:d1"]
        S(act(t("AB"), T.S5[:, :, 0:50], AF.Abs), kd, ["AB"], 400)
        if vt < NV - 1:
            S(lambda s: s.activation(t("JUNK"), dc, AF.Sign, accum_out=t("CNT")), kd, ["JUNK", "CNT"], 40)
        V(scan(t("SCN"), t("MASK5"), t("AB"), A.add, A.min), ["MASK5", "AB"], ["SCN"], 200)
        for b in range(2):
            V(ts(t("LL", b, 16, 2), t("SCN", 16 + 33 * b, 400, 50), 0.5, A.is_lt, t("DUM", b, b + 1), A.mult), ["SCN", "DUM%d" % b], ["LL%d" % b], 64)
        V(tt(t("OFF"), t("LL"), dc, A.max), ["LL0", "LL1"] + kd, ["OFF"], 64)
        V(ts(t("SL"), t("OFF"), 1.0, A.subtract), ["OFF"], ["SL"], 64)
        S(act(t("XS"), T["X%d" % vt][:].indirect(t("SL")), AF.Copy), XK[vt] + ["SL"], ["XS"], 400)
        P([(T.TB[:, 0:256], t("I16"), t("XS"))], ["I16", "XS"], ["@TB:t"], 256, False, True)
        if "X" in ONS:
            S(act(t("XM"), T.TB[:, 0:256], AF.Identity, MAGIC, 1 / 32), ["@TB:t"], ["XM"], 256)
            S(act(t("XB"), t("XM"), AF.Identity, -MAGIC), ["XM"], ["XN"], 256)
        else:
            V(ts(t("XN"), T.TB[:, 0:256], 1 / 32, A.mult), ["@TB:t"], ["XN"], 256)
        if vt < NV - 1:
            P([(T.S5[:, 0, 56:57], t("ONESF"), t("CNT"))], ["ONESF", "CNT"], ["@S5:n"], 256)
            V(cp(t("CI"), T.S5[:, 0, 56:57]), ["@S5:n"], ["CI"], 64)
            V(ts(t("CI2"), t("CI"), 255, A.bitwise_and), ["CI"], ["CI2"], 64)
            V(ts(t("TH"), t("CI2"), t("LIMF"), A.add, BIG / 16, A.mult), ["CI2", "LIMF"], ["TH"], 64)
            V(ts(t("THE"), t("SELC"), t("TH"), A.mult), ["SELC", "TH"], ["THE"], 64)
        for r in range(7, -1, -1):
            V(cp(T["X%d" % (vt + 1)][:].indirect(t("SL", 2 * r, 2 * r + 2)), t("XB" if "X" in ONS else "XN", 32 * r, 32 * r + 32)),
              ["SL", "XN"], XK[vt + 1], 32 * 3.8)

    for vt in range(NV):
        now[0] = 0.0
        dma("Y", T["X%d" % (vt + 1)][:], T["X%d" % vt][:], XK[vt] + ["sent:SLU%d%d" % (h, vt) for h in range(2)], XK[vt + 1], 2.0 + 9 * DM)
        for h in range(2):
            now[0] = BONUS[h]
            phase1(vt, h)
        now[0] = BONUS[8]
        for h in range(2):
            pairs(vt, h)
        update(vt)
        if vt == NV - 1:
            for k in range(NP):
                dma("Y", T.yx[:, k * PW:(k + 1) * PW], T["X%d" % NV][:, k * PW:(k + 1) * PW], XK[NV], [], 2.0 + DM * 2.2 * (k + 1))
        for ph in (phase2, phase3, phase4):
            for h in range(2):
                now[0] = BONUS[2 * (phase1, phase2, phase3, phase4).index(ph) + h]
                ph(vt, h)

    if rank == 0 or "order" not in INFO:
        INFO["order"] = schedule(ops)
    emit(g, T, ops, INFO["order"], QUEUE)


WAKE, PASSES, LOOK, GAP, MARGIN = 0.14, 3, 0.06, 0.2, 1.5
COST = [0.005, 0.01, 0.45e-3, 2.4, 3.3]
LEAD = 3.0
DM = 0.6
INFO = {}


def schedule(ops):
    n = len(ops)
    succ = [[] for _ in range(n)]
    for k, o in enumerate(ops):
        for d in o["deps"]:
            succ[d].append(k)
    tail = [0.0] * n
    for k in range(n - 1, -1, -1):
        o = ops[k]
        tail[k] = max([tail[s] + (o["cost"] + WAKE if ops[s]["deps"][k] == "wait" else o["cost"] if ops[s]["phys"] == "N" else o["hold"])
                       for s in succ[k]] + [o["cost"] + (LEAD if o["name"] == "YP0" else 0.0)])
    INFO.update(tail=list(tail), succ=succ, ops=ops)
    for k in range(n):
        tail[k] += ops[k]["bonus"]
    hold = [0.0 if o["phys"] == "N" else o["hold"] for o in ops]
    lag = [{d: ops[d]["cost"] + WAKE if w == "wait" else ops[d]["cost"] if o["phys"] == "N" else hold[d] for d, w in o["deps"].items()} for o in ops]
    back = [{s: hold[s] + lag[s][k] - hold[k] for s in succ[k]} for k in range(n)]

    def place(pri, pre, post, first):
        left, at, busy = [len(p) for p in pre], [0.0] * n, {}
        ready = set(k for k in range(n) if left[k] == 0)
        while ready:
            k = max(ready, key=lambda x: (pri[x], -x))
            ready.remove(k)
            t0 = max([first[k]] + [at[d] + x for d, x in pre[k].items()])
            if hold[k]:
                lst = busy.setdefault(ops[k]["phys"], [])
                i = len(lst)
                while i and lst[i - 1][1] > t0:
                    i -= 1
                while i < len(lst) and lst[i][0] < t0 + hold[k] - 1e-9:
                    t0 = max(t0, lst[i][1])
                    i += 1
                lst.insert(i, (t0, t0 + hold[k]))
            at[k] = t0
            for s in post[k]:
                left[s] -= 1
                if left[s] == 0:
                    ready.add(s)
        return at

    def greedy(pri):
        left, at, free, ready = [len(p) for p in lag], [0.0] * n, {}, {}
        for k in range(n):
            if left[k] == 0:
                ready.setdefault(ops[k]["phys"], {})[k] = 0.0
        while ready:
            t0, e = min((max(free.get(e, 0.0), min(lst.values())), e) for e, lst in ready.items())
            lst = ready[e]
            k = max((pri[k], -k) for k, r in lst.items() if r <= t0 + LOOK)[1] * -1
            soon = [u for u, r in lst.items() if r < t0 + hold[k] - GAP and pri[u] > pri[k] + MARGIN]
            if soon:
                u = min(soon, key=lambda x: (lst[x], x))
                fit = [c for c, r in lst.items() if max(r, t0) + hold[c] <= lst[u] + GAP]
                k = max(fit, key=lambda x: (pri[x], -x)) if fit else u
            at[k] = max(free.get(e, 0.0), lst.pop(k))
            if not lst:
                del ready[e]
            if e != "N":
                free[e] = at[k] + hold[k]
            for s in succ[k]:
                left[s] -= 1
                if left[s] == 0:
                    ready.setdefault(ops[s]["phys"], {})[s] = max(at[d] + x for d, x in lag[s].items())
        return at

    at = greedy(tail)
    best, pri = (max(at[k] + ops[k]["cost"] for k in range(n)), at), tail
    for it in range(PASSES):
        at = greedy(pri)
        span = max(at[k] + ops[k]["cost"] for k in range(n))
        if best is None or span < best[0]:
            best = (span, at)
        rv = place([at[k] + hold[k] for k in range(n)], back, lag, [ops[k]["cost"] - hold[k] for k in range(n)])
        pri = [rv[k] + hold[k] for k in range(n)]
    INFO.update(span=best[0], at=best[1], lag=lag, hold=hold)
    order, done = [], [False] * n
    for k in sorted(range(n), key=lambda x: (best[1][x], x)):
        todo = [k]
        while todo:
            x = todo[-1]
            rest = [d for d in lag[x] if not done[d]]
            if rest:
                todo.append(rest[0])
            else:
                todo.pop()
                if not done[x]:
                    done[x] = True
                    order.append(x)
    return order


def emit(g, T, ops, order, QUEUE):
    know = {e: {} for e in ("V", "S", "T", "G", "Y")}
    cnt = {}
    for k in order:
        o = ops[k]
        e = o["phys"]
        if e == "N":
            o["sig"], o["kn"] = (o["sem"], o["need"]), {}
            continue
        q, kn = QUEUE[o["eng"]], know[e]
        waits, src = {}, {}
        for d in o["deps"]:
            if o["deps"][d] == "wait":
                s, v = ops[d]["sig"]
                if kn.get(s, 0) < v and waits.get(s, 0) < v:
                    waits[s], src[s] = v, d
        for s in list(waits):
            if any(s2 != s and ops[src[s2]]["kn"].get(s, 0) >= waits[s] for s2 in waits):
                del waits[s]
        for s in sorted(waits):
            q.wait_ge(T.sem[s], waits[s])
            for a, b in ops[src[s]]["kn"].items():
                kn[a] = max(kn.get(a, 0), b)
            kn[s] = max(kn.get(s, 0), waits[s])
        ins = o["fn"]()
        if o["comp"]:
            s = "c" + e
            cnt[s] = cnt.get(s, 0) + 1
            ins.then_inc(T.sem[s], 1)
            o["sig"] = (s, cnt[s])
        else:
            o["sig"] = (o["sem"], o["need"])
            if o["eng"] != "G":
                ins.then_inc(T.sem[o["sem"]], 16)
        o["kn"] = dict(kn)
    for s in sorted(cnt):
        g.wait_ge(T.sem[s], cnt[s])
    for o in ops:
        if not o["comp"] and o["phys"] != "N":
            g.wait_ge(T.sem[o["sig"][0]], o["sig"][1])
